import numpy as np
import ml_dtypes


def mxq(x, axis, fmt="e4m3"):
    dtype, down = {"e4m3": (ml_dtypes.float8_e4m3fn, 7), "e5m2": (ml_dtypes.float8_e5m2, 14)}[fmt]
    v = np.moveaxis(np.asarray(x, np.float32).astype(ml_dtypes.bfloat16).astype(np.float64), axis, -1)
    blocks = v.reshape(v.shape[:-1] + (-1, 32))
    amax = np.abs(blocks).max(-1, keepdims=True)
    byte = np.maximum(np.where(amax > 0, np.frexp(amax)[1] - 1 + 127, 0) - down, 1)
    scale = np.exp2(byte - 127.0)
    codes = (blocks / scale).astype(np.float32).astype(dtype).astype(np.float64)
    return np.moveaxis((codes * scale).reshape(v.shape), -1, axis)


WIDE = False


def mx_kscale(k):
    if not WIDE:
        return np.ones(k)
    levels = np.array([10, -10, 5, -5, 0])
    if k % 512:
        return np.exp2(np.random.permutation(np.resize(levels, k // 32))).repeat(32)
    a = np.empty((k // 512, 16))
    for p in range(k // 512):
        a[p, :8] = np.random.permutation(np.resize(levels, 8))
        for g in range(8):
            far = levels[np.abs(levels - a[p, g]) >= 10]
            a[p, g + 8] = far[np.random.randint(len(far))]
    return np.exp2(a.ravel()).repeat(32)


def f64(x):
    return np.asarray(x).astype(np.float64)


def striped(idx):
    return np.tile(idx.reshape(-1, 16).T, (8, 1)).astype(np.uint16)


def unstriped(offs):
    return offs[:16].T.reshape(-1).astype(np.int64)


def pack_weight(w):
    k, n = w.shape
    w = f64(np.asarray(w, np.float32).astype(ml_dtypes.bfloat16)).reshape(k // 32, 32, n)
    amax = np.abs(w).max(1)
    byte = np.clip(np.where(amax > 0, np.frexp(amax)[1] - 1 + 127 - 7, 1), 1, 254)
    scaled = (w * np.exp2(127.0 - byte)[:, None, :]).reshape(k, n).astype(np.float32)
    words = np.ascontiguousarray(scaled.reshape(k // 512, 128, 4, n).transpose(0, 1, 3, 2)).astype(ml_dtypes.float8_e4m3fn).view(np.uint8)
    return words, np.ascontiguousarray(byte.astype(np.uint8).reshape(k // 512, 16, n))


def unpack_weight(words, scales):
    g, p, n, _ = words.shape
    vals = np.ascontiguousarray(words).view(ml_dtypes.float8_e4m3fn).astype(np.float64) * np.repeat(np.exp2(scales.astype(np.float64) - 127.0), 8, axis=1)[..., None]
    return vals.transpose(0, 1, 3, 2).reshape(g * 512, n)


def silu(v):
    return v / (1.0 + np.exp(-np.maximum(v, -700.0)))


K, T, E, C, N = 1024, 768, 12, 128, 256


def by_expert(wq, xq):
    return np.concatenate([wq[e].T @ xq[:, e * C:(e + 1) * C] for e in range(E)], axis=1)


def setup_inputs():
    n = np.random.standard_normal
    s = mx_kscale(K)[:, None]
    first = np.random.permutation(np.repeat(np.arange(E), T // E))
    second = (first + 1 + np.random.permutation(np.repeat(np.arange(E - 1), -(-T // (E - 1)))[:T])) % E
    while np.bincount(second, minlength=E).max() != T // E:
        load = np.bincount(second, minlength=E); hi, lo = int(load.argmax()), int(load.argmin())
        t = np.flatnonzero((second == hi) & (first != lo))[0]; second[t] = lo
    slot_token = np.empty(E * C, np.int64); pos = np.empty((2, T), np.int64); fill = np.zeros(E, np.int64)
    place = np.stack([np.random.permutation(C) for _ in range(E)])
    for r, deal in enumerate((first, second)):
        for t in np.random.permutation(T):
            e = deal[t]; j = e * C + place[e, fill[e]]; fill[e] += 1; slot_token[j] = t; pos[r, t] = j
    g = np.random.uniform(0.2, 0.8, T)
    packed = [pack_weight(m) for m in n((E, K, N)) / np.sqrt(K) / s[None]]
    w_slot = np.empty(E * C); w_slot[pos[0]] = g; w_slot[pos[1]] = 1.0 - g
    return {
        "xT": (n((K, T)) * s).astype(np.float32),
        "w_words": np.stack([m[0] for m in packed]),
        "w_scales": np.stack([m[1] for m in packed]),
        "b": (0.3 * n((N, E))).astype(np.float32),
        "gate": np.tile(w_slot, (K, 1)).astype(np.float32),
        "offs": striped(slot_token),
        "pos1": striped(pos[0]),
        "pos2": striped(pos[1]),
    }


def reference(xT, w_words, w_scales, b, gate, offs, pos1, pos2):
    idx = unstriped(offs)
    w = np.stack([unpack_weight(w_words[e], w_scales[e]) for e in range(E)])
    xq = mxq(f64(gate) * f64(xT)[:, idx], 0, "e4m3")
    y = by_expert(w, xq)
    y = silu(y + np.repeat(f64(b), C, axis=1))
    return y[:, unstriped(pos1)] + y[:, unstriped(pos2)]

@@ -1,0 +1,162 @@
+from contextlib import ExitStack
+
+import concourse.mybir as mybir
+
+K, T, E, C, N = 1024, 768, 12, 128, 256
+S = E * C
+FLOPS = 2 * K * N * S
+
+F32 = mybir.dt.float32
+BF16 = mybir.dt.bfloat16
+I32 = mybir.dt.int32
+U32 = mybir.dt.uint32
+U16 = mybir.dt.uint16
+U8 = mybir.dt.uint8
+FP8X4 = mybir.dt.float8_e4m3fn_x4
+MULT = mybir.AluOpType.mult
+ADD = mybir.AluOpType.add
+SILU = mybir.ActivationFunctionType.Silu
+
+P = 128
+PACK = 4
+PASSES = K // (P * PACK)
+HALVES = N // P
+LANES = 16
+
+STEPS = [(0, 512, 0), (0, 512, 1), (512, 512, 0), (512, 512, 1), (1024, 256, 0), (1024, 256, 1), (1280, 128, 0), (1280, 128, 1), (1408, 128, 0), (1408, 128, 1)]
+GATE_CUTS = [0, 512, 1024, 1536]
+BACK = [(0, 0, 768), (1, 0, 576), (1, 576, 192)]
+
+
+def tile_moe_pre_lin_silu_kernel(tc, xT, w_words, w_scales, b, gate, offs, pos1, pos2, out):
+    nc = tc.nc
+    with ExitStack() as ctx:
+        keep = ctx.enter_context(tc.tile_pool(name="keep", bufs=1))
+        stage = ctx.enter_context(tc.tile_pool(name="stage", bufs=3))
+        psum = ctx.enter_context(tc.psum_pool(name="psum", bufs=8))
+
+        offs_sb = keep.tile([P, S // LANES], U16, name="offs_sb")
+        pos1_sb = keep.tile([P, T // LANES], U16, name="pos1_sb")
+        pos2_sb = keep.tile([P, T // LANES], U16, name="pos2_sb")
+        gate_sb = keep.tile([P, S], F32, name="gate_sb")
+        planes = [[keep.tile([P, T], F32, name="x%d%d" % (a, j)) for j in range(PACK)] for a in range(PASSES)]
+        w_codes = keep.tile([P, E * PASSES, N], U32, name="w_codes", align_bytes=64)
+        w_plane = keep.tile([P, E * PASSES, N], U8, name="w_plane", align_bytes=64)
+        bias_sb = keep.tile([P, HALVES, 16], F32, name="bias_sb")
+        x_codes = keep.tile([P, PASSES, S], U32, name="x_codes", align_bytes=64)
+        x_plane = keep.tile([P, PASSES, S], U8, name="x_plane", align_bytes=64)
+        y = [keep.tile([P, S], F32, name="y%d" % h) for h in range(HALVES)]
+        first = [keep.tile([P, T], F32, name="first%d" % h) for h in range(HALVES)]
+        second = [keep.tile([P, T], F32, name="second%d" % h) for h in range(HALVES)]
+        total = [keep.tile([P, T], F32, name="total%d" % h) for h in range(HALVES)]
+
+        nc.vector.memset(w_plane[:].rearrange("p g n -> p (g n)").bitcast(I32), 0)
+
+        x_rows = xT.rearrange("(a p j) t -> a j p t", a=PASSES, j=PACK)
+        words = w_words.rearrange("e a p n r -> p (e a) (n r)")
+        scale_rows = w_scales.rearrange("e a q n -> q (e a) n")
+
+        def load_gate(i):
+            cols = slice(GATE_CUTS[i], GATE_CUTS[i + 1])
+            nc.sync.dma_start(gate_sb[:, cols], gate[0:P, cols])
+
+        def load_words(e0, e1):
+            g = slice(e0 * PASSES, e1 * PASSES)
+            nc.sync.dma_start(w_codes[:, g, :].bitcast(I32), words[:, g, :].bitcast(I32))
+
+        nc.sync.dma_start(offs_sb[:], offs)
+        nc.sync.dma_start(planes[0][0][:], x_rows[0, 0])
+        load_gate(0)
+        for a in range(PASSES):
+            for j in range(PACK):
+                if a or j:
+                    nc.sync.dma_start(planes[a][j][:], x_rows[a, j])
+        load_gate(1)
+        for q in range(4):
+            nc.sync.dma_start(w_plane[32 * q : 32 * q + 4].bitcast(I32), scale_rows[4 * q : 4 * q + 4].bitcast(I32))
+        nc.sync.dma_start(bias_sb[:, :, 0:E], b.rearrange("(h p) e -> p h e", p=P))
+        load_words(0, 4)
+        load_gate(2)
+        load_words(4, 8)
+        load_words(8, 12)
+        nc.sync.dma_start(pos1_sb[:], pos1)
+        nc.sync.dma_start(pos2_sb[:], pos2)
+
+        gathered = {}
+        grouped = {}
+
+        def gather(i, j):
+            s0, w, a = STEPS[i]
+            if j == 0:
+                gathered[i] = stage.tile([P, PACK, w], F32, name="gathered")
+            nc.vector.tensor_tensor(
+                gathered[i][:, j, :],
+                planes[a][j][:].indirect(offs_sb[:, s0 // LANES : (s0 + w) // LANES]),
+                gate_sb[:, s0 : s0 + w],
+                MULT,
+            )
+
+        def interleave(i):
+            w = STEPS[i][1]
+            grouped[i] = stage.tile([P, w, PACK], BF16, name="grouped", align_bytes=64)
+            src = gathered[i][:].rearrange("p j s -> p s j")
+            if i == len(STEPS) - 1:
+                nc.vector.tensor_copy(grouped[i][:], src)
+            else:
+                nc.scalar.copy(grouped[i][:], src)
+
+        def quantise(i):
+            s0, w, a = STEPS[i]
+            nc.vector.quantize_mx(
+                out=x_codes[:, a, s0 : s0 + w].bitcast(FP8X4),
+                scales=x_plane[:, a, s0 : s0 + w],
+                in_=grouped[i][:].rearrange("p s j -> p (s j)"),
+            )
+            if a == PASSES - 1:
+                for h in range(HALVES):
+                    for e in range(s0 // C, (s0 + w) // C):
+                        expert(e, h)
+
+        def expert(e, h):
+            acc = psum.tile([P, C], F32, name="acc")
+            slots = slice(e * C, (e + 1) * C)
+            cols = slice(h * P, (h + 1) * P)
+            for a in range(PASSES):
+                nc.tensor.matmul_mx(
+                    out=acc[:],
+                    lhsT=w_codes[:, e * PASSES + a, cols].bitcast(FP8X4),
+                    lhsT_scale=w_plane[:, e * PASSES + a, cols],
+                    rhs=x_codes[:, a, slots].bitcast(FP8X4),
+                    rhs_scale=x_plane[:, a, slots],
+                    start=(a == 0),
+                    stop=(a == PASSES - 1),
+                )
+            nc.scalar.activation(y[h][:, slots], acc[:], SILU, bias=bias_sb[:, h, e : e + 1])
+
+        last = len(STEPS) - 1
+        for i in range(len(STEPS)):
+            for j in range(PACK):
+                gather(i, j)
+                if j == PACK - 2 and 0 < i < last:
+                    quantise(i - 1)
+            interleave(i)
+        quantise(last - 1)
+        quantise(last)
+
+        def fetch(i):
+            h, t0, w = BACK[i]
+            cols = slice(t0 // LANES, (t0 + w) // LANES)
+            nc.vector.tensor_copy(first[h][:, t0 : t0 + w], y[h][:].indirect(pos1_sb[:, cols]))
+            if i > 0:
+                combine(i - 1)
+            nc.vector.tensor_copy(second[h][:, t0 : t0 + w], y[h][:].indirect(pos2_sb[:, cols]))
+
+        def combine(i):
+            h, t0, w = BACK[i]
+            cols = slice(t0, t0 + w)
+            nc.vector.tensor_tensor(total[h][:, cols], first[h][:, cols], second[h][:, cols], ADD)
+            nc.sync.dma_start(out[h * P : (h + 1) * P, cols], total[h][:, cols])
+
+        for i in range(len(BACK)):
+            fetch(i)
+        combine(len(BACK) - 1)

@@ -22,29 +22,55 @@ PACK = 4
 PASSES = K // (P * PACK)
 HALVES = N // P
 LANES = 16
+QUADRANTS = 4
+LINE = 4
+BANKS = 8
 
-STEPS = [(0, 512, 0), (0, 512, 1), (512, 512, 0), (512, 512, 1), (1024, 256, 0), (1024, 256, 1), (1280, 128, 0), (1280, 128, 1), (1408, 128, 0), (1408, 128, 1)]
-GATE_CUTS = [0, 512, 1024, 1536]
-BACK = [(0, 0, 768), (1, 0, 576), (1, 576, 192)]
+WINDOW = T + LANES
+
+GROUPS = [(0, 768), (768, 1280), (1280, 1536)]
+STEPS = [(a, s0, s1) for s0, s1 in GROUPS for a in range(PASSES)]
+FIRST_SLOTS = 256
+QUANT_SLOTS = 512
+
+BACK = [(0, 0, 768), (1, 0, 384), (1, 384, 768)]
+
+GROUPED_BYTES = 2 * PACK
+BIAS_COLUMNS = 16
+BIAS_BYTES = HALVES * BIAS_COLUMNS * 4
+
+
+def grouped_offset(a, s):
+    s0, s1 = max(g for g in GROUPS if g[0] <= s)
+    return GROUPED_BYTES * (PASSES * s0 + a * (s1 - s0) + s - s0)
+
+
+BIAS_OFFSETS = [
+    grouped_offset(0, GROUPS[2][0]) - BIAS_BYTES // 2,
+    grouped_offset(1, GROUPS[2][0]),
+    GROUPED_BYTES * PASSES * S,
+]
 
 
 def tile_moe_pre_lin_silu_kernel(tc, xT, w_words, w_scales, b, gate, offs, pos1, pos2, out):
     nc = tc.nc
     with ExitStack() as ctx:
         keep = ctx.enter_context(tc.tile_pool(name="keep", bufs=1))
-        stage = ctx.enter_context(tc.tile_pool(name="stage", bufs=3))
-        psum = ctx.enter_context(tc.psum_pool(name="psum", bufs=8))
+        psum = ctx.enter_context(tc.psum_pool(name="psum", bufs=BANKS))
 
         offs_sb = keep.tile([P, S // LANES], U16, name="offs_sb")
         pos1_sb = keep.tile([P, T // LANES], U16, name="pos1_sb")
         pos2_sb = keep.tile([P, T // LANES], U16, name="pos2_sb")
         gate_sb = keep.tile([P, S], F32, name="gate_sb")
-        planes = [[keep.tile([P, T], F32, name="x%d%d" % (a, j)) for j in range(PACK)] for a in range(PASSES)]
+        row_tiles = [[keep.tile([P, WINDOW], F32, name="x%d%d" % (a, j)) for j in range(PACK)] for a in range(PASSES)]
         w_codes = keep.tile([P, E * PASSES, N], U32, name="w_codes", align_bytes=64)
         w_plane = keep.tile([P, E * PASSES, N], U8, name="w_plane", align_bytes=64)
-        bias_sb = keep.tile([P, HALVES, 16], F32, name="bias_sb")
-        x_codes = keep.tile([P, PASSES, S], U32, name="x_codes", align_bytes=64)
-        x_plane = keep.tile([P, PASSES, S], U8, name="x_plane", align_bytes=64)
+        shared = ctx.enter_context(tc.tile_pool(name="shared", bufs=1))
+        bias_sb = [
+            shared.tile([P, HALVES, BIAS_COLUMNS], F32, name="bias%d" % (s0 // C), offset=at, align_bytes=64)
+            for (s0, s1), at in zip(GROUPS, BIAS_OFFSETS)
+        ]
+        ring = ctx.enter_context(tc.tile_pool(name="ring", bufs=1))
         y = [keep.tile([P, S], F32, name="y%d" % h) for h in range(HALVES)]
         first = [keep.tile([P, T], F32, name="first%d" % h) for h in range(HALVES)]
         second = [keep.tile([P, T], F32, name="second%d" % h) for h in range(HALVES)]
@@ -56,107 +82,132 @@ def tile_moe_pre_lin_silu_kernel(tc, xT, w_words, w_scales, b, gate, offs, pos1,
         words = w_words.rearrange("e a p n r -> p (e a) (n r)")
         scale_rows = w_scales.rearrange("e a q n -> q (e a) n")
 
-        def load_gate(i):
-            cols = slice(GATE_CUTS[i], GATE_CUTS[i + 1])
-            nc.sync.dma_start(gate_sb[:, cols], gate[0:P, cols])
+        def load_rows(a, j):
+            nc.sync.dma_start(row_tiles[a][j][:, 0:T], x_rows[a, j])
 
-        def load_words(e0, e1):
-            g = slice(e0 * PASSES, e1 * PASSES)
-            nc.sync.dma_start(w_codes[:, g, :].bitcast(I32), words[:, g, :].bitcast(I32))
+        def load_gate(s0, s1):
+            nc.sync.dma_start(gate_sb[:, s0:s1], gate[0:P, s0:s1])
 
+        load_rows(0, 0)
         nc.sync.dma_start(offs_sb[:], offs)
-        nc.sync.dma_start(planes[0][0][:], x_rows[0, 0])
-        load_gate(0)
+        load_gate(0, FIRST_SLOTS)
+        load_gate(FIRST_SLOTS, GROUPS[0][1])
         for a in range(PASSES):
             for j in range(PACK):
-                if a or j:
-                    nc.sync.dma_start(planes[a][j][:], x_rows[a, j])
-        load_gate(1)
-        for q in range(4):
+                if (a, j) != (0, 0):
+                    load_rows(a, j)
+        load_gate(GROUPS[0][1], S)
+        for q in range(QUADRANTS):
             nc.sync.dma_start(w_plane[32 * q : 32 * q + 4].bitcast(I32), scale_rows[4 * q : 4 * q + 4].bitcast(I32))
-        nc.sync.dma_start(bias_sb[:, :, 0:E], b.rearrange("(h p) e -> p h e", p=P))
-        load_words(0, 4)
-        load_gate(2)
-        load_words(4, 8)
-        load_words(8, 12)
+        for bias in bias_sb:
+            nc.sync.dma_start(bias[:, :, 0:E], b.rearrange("(h p) e -> p h e", p=P))
+        for s0, s1 in GROUPS:
+            g = slice(s0 // C * PASSES, s1 // C * PASSES)
+            nc.sync.dma_start(w_codes[:, g, :].bitcast(I32), words[:, g, :].bitcast(I32))
         nc.sync.dma_start(pos1_sb[:], pos1)
         nc.sync.dma_start(pos2_sb[:], pos2)
 
         gathered = {}
         grouped = {}
+        x_codes = {}
+        x_plane = {}
 
-        def gather(i, j):
-            s0, w, a = STEPS[i]
-            if j == 0:
-                gathered[i] = stage.tile([P, PACK, w], F32, name="gathered")
-            nc.vector.tensor_tensor(
-                gathered[i][:, j, :],
-                planes[a][j][:].indirect(offs_sb[:, s0 // LANES : (s0 + w) // LANES]),
-                gate_sb[:, s0 : s0 + w],
-                MULT,
+        def gather(i):
+            a, s0, s1 = STEPS[i]
+            gathered[i] = ring.tile([P, PACK, s1 - s0], F32, name="gathered%d" % a)
+            for j in range(PACK):
+                cuts = [s0, FIRST_SLOTS, s1] if (i, j) == (0, 0) else [s0, s1]
+                for c0, c1 in zip(cuts, cuts[1:]):
+                    nc.vector.tensor_tensor(
+                        gathered[i][:, j, c0 - s0 : c1 - s0],
+                        row_tiles[a][j][:].indirect(offs_sb[:, c0 // LANES : c1 // LANES]),
+                        gate_sb[:, c0:c1],
+                        MULT,
+                    )
+
+        def interleave(copy, i, c0, c1):
+            a, s0, s1 = STEPS[i]
+            tile = shared.tile(
+                [P, c1 - c0, PACK], BF16, name="grouped%d_%d" % (a, c0), offset=grouped_offset(a, c0), align_bytes=64
+            )
+            grouped.setdefault(i, []).append((c0, tile))
+            copy(
+                tile[:].rearrange("p (c m) j -> p c j m", m=LINE),
+                gathered[i][:, :, c0 - s0 : c1 - s0].rearrange("p j (c m) -> p c j m", m=LINE),
             )
 
-        def interleave(i):
-            w = STEPS[i][1]
-            grouped[i] = stage.tile([P, w, PACK], BF16, name="grouped", align_bytes=64)
-            src = gathered[i][:].rearrange("p j s -> p s j")
-            if i == len(STEPS) - 1:
-                nc.vector.tensor_copy(grouped[i][:], src)
-            else:
-                nc.scalar.copy(grouped[i][:], src)
-
-        def quantise(i):
-            s0, w, a = STEPS[i]
+        def quantise(i, c0, c1):
+            a, s0, s1 = STEPS[i]
+            if i not in x_codes:
+                x_codes[i] = keep.tile([P, s1 - s0], U32, name="x_codes%d_%d" % (a, s0), align_bytes=64)
+                x_plane[i] = keep.tile([P, s1 - s0], U8, name="x_plane%d_%d" % (a, s0), align_bytes=64)
+            g0, tile = [piece for piece in grouped[i] if piece[0] <= c0][-1]
             nc.vector.quantize_mx(
-                out=x_codes[:, a, s0 : s0 + w].bitcast(FP8X4),
-                scales=x_plane[:, a, s0 : s0 + w],
-                in_=grouped[i][:].rearrange("p s j -> p (s j)"),
+                out=x_codes[i][:, c0 - s0 : c1 - s0].bitcast(FP8X4),
+                scales=x_plane[i][:, c0 - s0 : c1 - s0],
+                in_=tile[:, c0 - g0 : c1 - g0, :].rearrange("p s j -> p (s j)"),
             )
-            if a == PASSES - 1:
-                for h in range(HALVES):
-                    for e in range(s0 // C, (s0 + w) // C):
-                        expert(e, h)
 
-        def expert(e, h):
-            acc = psum.tile([P, C], F32, name="acc")
-            slots = slice(e * C, (e + 1) * C)
-            cols = slice(h * P, (h + 1) * P)
-            for a in range(PASSES):
-                nc.tensor.matmul_mx(
-                    out=acc[:],
-                    lhsT=w_codes[:, e * PASSES + a, cols].bitcast(FP8X4),
-                    lhsT_scale=w_plane[:, e * PASSES + a, cols],
-                    rhs=x_codes[:, a, slots].bitcast(FP8X4),
-                    rhs_scale=x_plane[:, a, slots],
-                    start=(a == 0),
-                    stop=(a == PASSES - 1),
-                )
-            nc.scalar.activation(y[h][:, slots], acc[:], SILU, bias=bias_sb[:, h, e : e + 1])
+        def experts(group):
+            s0, s1 = GROUPS[group]
+            for h in range(HALVES):
+                cols = slice(h * P, (h + 1) * P)
+                for e in range(s0 // C, s1 // C):
+                    acc = psum.tile([P, C], F32, name="acc")
+                    slots = slice(e * C - s0, (e + 1) * C - s0)
+                    for a in range(PASSES):
+                        nc.tensor.matmul_mx(
+                            out=acc[:],
+                            lhsT=w_codes[:, e * PASSES + a, cols].bitcast(FP8X4),
+                            lhsT_scale=w_plane[:, e * PASSES + a, cols],
+                            rhs=x_codes[group * PASSES + a][:, slots].bitcast(FP8X4),
+                            rhs_scale=x_plane[group * PASSES + a][:, slots],
+                            start=(a == 0),
+                            stop=(a == PASSES - 1),
+                        )
+                    nc.scalar.activation(
+                        y[h][:, e * C : (e + 1) * C], acc[:], SILU, bias=bias_sb[group][:, h, e : e + 1]
+                    )
+
+        def finish(i):
+            a, s0, s1 = STEPS[i]
+            for c0 in range(s0, s1, QUANT_SLOTS):
+                quantise(i, c0, min(c0 + QUANT_SLOTS, s1))
+            if a == PASSES - 1:
+                experts(i // PASSES)
 
         last = len(STEPS) - 1
-        for i in range(len(STEPS)):
-            for j in range(PACK):
-                gather(i, j)
-                if j == PACK - 2 and 0 < i < last:
-                    quantise(i - 1)
-            interleave(i)
-        quantise(last - 1)
-        quantise(last)
-
-        def fetch(i):
-            h, t0, w = BACK[i]
-            cols = slice(t0 // LANES, (t0 + w) // LANES)
-            nc.vector.tensor_copy(first[h][:, t0 : t0 + w], y[h][:].indirect(pos1_sb[:, cols]))
+        for i in range(last):
+            gather(i)
+            interleave(nc.scalar.copy, i, STEPS[i][1], STEPS[i][2])
             if i > 0:
-                combine(i - 1)
-            nc.vector.tensor_copy(second[h][:, t0 : t0 + w], y[h][:].indirect(pos2_sb[:, cols]))
+                finish(i - 1)
 
-        def combine(i):
-            h, t0, w = BACK[i]
-            cols = slice(t0, t0 + w)
-            nc.vector.tensor_tensor(total[h][:, cols], first[h][:, cols], second[h][:, cols], ADD)
-            nc.sync.dma_start(out[h * P : (h + 1) * P, cols], total[h][:, cols])
+        s0, s1 = GROUPS[-1]
+        middle = (s0 + s1) // 2
+        gather(last)
+        interleave(nc.scalar.copy, last, s0, middle)
+        quantise(last - 1, s0, middle)
+        interleave(nc.vector.tensor_copy, last, middle, s1)
+        quantise(last - 1, middle, s1)
+        quantise(last, s0, middle)
+        quantise(last, middle, s1)
+        experts(len(GROUPS) - 1)
 
-        for i in range(len(BACK)):
-            fetch(i)
-        combine(len(BACK) - 1)
+        def fetch(dst, positions, piece):
+            h, t0, t1 = piece
+            nc.vector.tensor_copy(dst[h][:, t0:t1], y[h][:].indirect(positions[:, t0 // LANES : t1 // LANES]))
+
+        def combine(engine, piece):
+            h, t0, t1 = piece
+            engine.tensor_tensor(total[h][:, t0:t1], first[h][:, t0:t1], second[h][:, t0:t1], ADD)
+            nc.sync.dma_start(out[h * P : (h + 1) * P, t0:t1], total[h][:, t0:t1])
+
+        for i, piece in enumerate(BACK):
+            fetch(first, pos1_sb, piece)
+            if i > 0:
+                combine(nc.gpsimd, BACK[i - 1])
+            fetch(second, pos2_sb, piece)
+        h, t0, t1 = BACK[-1]
+        combine(nc.vector, (h, t0, (t0 + t1) // 2))
+        combine(nc.vector, (h, (t0 + t1) // 2, t1))

@@ -24,39 +24,27 @@ HALVES = N // P
 LANES = 16
 QUADRANTS = 4
 LINE = 4
-BANKS = 8
 
 WINDOW = T + LANES
 
-GROUPS = [(0, 768), (768, 1280), (1280, 1536)]
-STEPS = [(a, s0, s1) for s0, s1 in GROUPS for a in range(PASSES)]
-FIRST_SLOTS = 256
-QUANT_SLOTS = 512
-
-BACK = [(0, 0, 768), (1, 0, 384), (1, 384, 768)]
-
-GROUPED_BYTES = 2 * PACK
+HEAD = [0, 256, 768]
+A, B, C_ = (0, 768), (768, 1280), (1280, S)
+BC = (768, S)
+B1, B2 = (768, 1024), (1024, 1280)
+C1, C2 = (1280, 1408), (1408, S)
+PLACE = {(0, BC): (0, 768), (1, A): (2288, 768), (1, B): (3072, 512), (1, C_): (2304, 512), (0, A): (5360, 768)}
+STAGE = {(0, A): 0, (0, BC): 768, (1, B): S, (1, A): S + 512, (1, C1): S + 1280, (1, C2): S + 1408}
+ARENA = 5360 + 4 * 768
+BACK = [(0, 0, 768), (1, 0, 576), (1, 576, 768)]
 BIAS_COLUMNS = 16
-BIAS_BYTES = HALVES * BIAS_COLUMNS * 4
-
-
-def grouped_offset(a, s):
-    s0, s1 = max(g for g in GROUPS if g[0] <= s)
-    return GROUPED_BYTES * (PASSES * s0 + a * (s1 - s0) + s - s0)
-
-
-BIAS_OFFSETS = [
-    grouped_offset(0, GROUPS[2][0]) - BIAS_BYTES // 2,
-    grouped_offset(1, GROUPS[2][0]),
-    GROUPED_BYTES * PASSES * S,
-]
 
 
 def tile_moe_pre_lin_silu_kernel(tc, xT, w_words, w_scales, b, gate, offs, pos1, pos2, out):
     nc = tc.nc
     with ExitStack() as ctx:
         keep = ctx.enter_context(tc.tile_pool(name="keep", bufs=1))
-        psum = ctx.enter_context(tc.psum_pool(name="psum", bufs=BANKS))
+        psum = ctx.enter_context(tc.psum_pool(name="psum", bufs=6))
+        late = ctx.enter_context(tc.psum_pool(name="late", bufs=1))
 
         offs_sb = keep.tile([P, S // LANES], U16, name="offs_sb")
         pos1_sb = keep.tile([P, T // LANES], U16, name="pos1_sb")
@@ -65,16 +53,17 @@ def tile_moe_pre_lin_silu_kernel(tc, xT, w_words, w_scales, b, gate, offs, pos1,
         row_tiles = [[keep.tile([P, WINDOW], F32, name="x%d%d" % (a, j)) for j in range(PACK)] for a in range(PASSES)]
         w_codes = keep.tile([P, E * PASSES, N], U32, name="w_codes", align_bytes=64)
         w_plane = keep.tile([P, E * PASSES, N], U8, name="w_plane", align_bytes=64)
-        shared = ctx.enter_context(tc.tile_pool(name="shared", bufs=1))
-        bias_sb = [
-            shared.tile([P, HALVES, BIAS_COLUMNS], F32, name="bias%d" % (s0 // C), offset=at, align_bytes=64)
-            for (s0, s1), at in zip(GROUPS, BIAS_OFFSETS)
-        ]
-        ring = ctx.enter_context(tc.tile_pool(name="ring", bufs=1))
+        arena = keep.tile([P, ARENA], F32, name="arena", align_bytes=64)
+        x_codes = [keep.tile([P, S], U32, name="x_codes%d" % a, align_bytes=64) for a in range(PASSES)]
+        x_plane = [keep.tile([P, S], U8, name="x_plane%d" % a, align_bytes=64) for a in range(PASSES)]
         y = [keep.tile([P, S], F32, name="y%d" % h) for h in range(HALVES)]
         first = [keep.tile([P, T], F32, name="first%d" % h) for h in range(HALVES)]
-        second = [keep.tile([P, T], F32, name="second%d" % h) for h in range(HALVES)]
-        total = [keep.tile([P, T], F32, name="total%d" % h) for h in range(HALVES)]
+        shared = ctx.enter_context(tc.tile_pool(name="shared", bufs=1))
+        bias_sb = shared.tile([P, HALVES, BIAS_COLUMNS], F32, name="bias_sb", offset=0)
+        staged = ctx.enter_context(tc.tile_pool(name="staged", bufs=1))
+        bias_a = staged.tile([P, HALVES, BIAS_COLUMNS], F32, name="bias_a", offset=8 * S - 64, align_bytes=64)
+        bias_b = staged.tile([P, HALVES, BIAS_COLUMNS], F32, name="bias_b", offset=8 * STAGE[(1, C1)], align_bytes=64)
+        grouped = {}
 
         nc.vector.memset(w_plane[:].rearrange("p g n -> p (g n)").bitcast(I32), 0)
 
@@ -85,129 +74,138 @@ def tile_moe_pre_lin_silu_kernel(tc, xT, w_words, w_scales, b, gate, offs, pos1,
         def load_rows(a, j):
             nc.sync.dma_start(row_tiles[a][j][:, 0:T], x_rows[a, j])
 
-        def load_gate(s0, s1):
-            nc.sync.dma_start(gate_sb[:, s0:s1], gate[0:P, s0:s1])
-
         load_rows(0, 0)
         nc.sync.dma_start(offs_sb[:], offs)
-        load_gate(0, FIRST_SLOTS)
-        load_gate(FIRST_SLOTS, GROUPS[0][1])
+        for c0, c1 in zip(HEAD, HEAD[1:]):
+            nc.sync.dma_start(gate_sb[:, c0:c1], gate[0:P, c0:c1])
         for a in range(PASSES):
             for j in range(PACK):
                 if (a, j) != (0, 0):
                     load_rows(a, j)
-        load_gate(GROUPS[0][1], S)
+        nc.sync.dma_start(gate_sb[:, BC[0] : S], gate[0:P, BC[0] : S])
         for q in range(QUADRANTS):
             nc.sync.dma_start(w_plane[32 * q : 32 * q + 4].bitcast(I32), scale_rows[4 * q : 4 * q + 4].bitcast(I32))
-        for bias in bias_sb:
+        for bias in (bias_a, bias_b, bias_sb):
             nc.sync.dma_start(bias[:, :, 0:E], b.rearrange("(h p) e -> p h e", p=P))
-        for s0, s1 in GROUPS:
+        for s0, s1 in (A, B, C_):
             g = slice(s0 // C * PASSES, s1 // C * PASSES)
             nc.sync.dma_start(w_codes[:, g, :].bitcast(I32), words[:, g, :].bitcast(I32))
         nc.sync.dma_start(pos1_sb[:], pos1)
         nc.sync.dma_start(pos2_sb[:], pos2)
 
-        gathered = {}
-        grouped = {}
-        x_codes = {}
-        x_plane = {}
+        def rows(a, group):
+            base, stride = PLACE[(a, group)]
+            view = arena[:, base : base + PACK * stride].rearrange("p (j s) -> p j s", j=PACK)
+            return view[:, :, 0 : group[1] - group[0]]
 
-        def gather(i):
-            a, s0, s1 = STEPS[i]
-            gathered[i] = ring.tile([P, PACK, s1 - s0], F32, name="gathered%d" % a)
-            for j in range(PACK):
-                cuts = [s0, FIRST_SLOTS, s1] if (i, j) == (0, 0) else [s0, s1]
+        def gather(a, group, js, cuts=None):
+            cuts = cuts or group
+            for j in js:
                 for c0, c1 in zip(cuts, cuts[1:]):
                     nc.vector.tensor_tensor(
-                        gathered[i][:, j, c0 - s0 : c1 - s0],
+                        rows(a, group)[:, j, c0 - group[0] : c1 - group[0]],
                         row_tiles[a][j][:].indirect(offs_sb[:, c0 // LANES : c1 // LANES]),
                         gate_sb[:, c0:c1],
                         MULT,
                     )
 
-        def interleave(copy, i, c0, c1):
-            a, s0, s1 = STEPS[i]
-            tile = shared.tile(
-                [P, c1 - c0, PACK], BF16, name="grouped%d_%d" % (a, c0), offset=grouped_offset(a, c0), align_bytes=64
-            )
-            grouped.setdefault(i, []).append((c0, tile))
+        def rounded(a, c0, c1):
+            home = [g for pa, g in STAGE if pa == a and g[0] <= c0 < g[1]][0]
+            if (a, home) not in grouped:
+                grouped[(a, home)] = staged.tile(
+                    [P, PACK * (home[1] - home[0])],
+                    BF16,
+                    name="grouped%d_%d" % (a, home[0]),
+                    offset=8 * STAGE[(a, home)],
+                    align_bytes=64,
+                )
+            return grouped[(a, home)][:, PACK * (c0 - home[0]) : PACK * (c1 - home[0])]
+
+        def interleave(copy, a, group, piece):
+            c0, c1 = piece
             copy(
-                tile[:].rearrange("p (c m) j -> p c j m", m=LINE),
-                gathered[i][:, :, c0 - s0 : c1 - s0].rearrange("p j (c m) -> p c j m", m=LINE),
+                rounded(a, c0, c1).rearrange("p (c m j) -> p c j m", m=LINE, j=PACK),
+                rows(a, group)[:, :, c0 - group[0] : c1 - group[0]].rearrange("p j (c m) -> p c j m", m=LINE),
             )
 
-        def quantise(i, c0, c1):
-            a, s0, s1 = STEPS[i]
-            if i not in x_codes:
-                x_codes[i] = keep.tile([P, s1 - s0], U32, name="x_codes%d_%d" % (a, s0), align_bytes=64)
-                x_plane[i] = keep.tile([P, s1 - s0], U8, name="x_plane%d_%d" % (a, s0), align_bytes=64)
-            g0, tile = [piece for piece in grouped[i] if piece[0] <= c0][-1]
-            nc.vector.quantize_mx(
-                out=x_codes[i][:, c0 - s0 : c1 - s0].bitcast(FP8X4),
-                scales=x_plane[i][:, c0 - s0 : c1 - s0],
-                in_=tile[:, c0 - g0 : c1 - g0, :].rearrange("p s j -> p (s j)"),
-            )
+        def quantise(a, piece):
+            for c0 in range(piece[0], piece[1], 512):
+                c1 = min(c0 + 512, piece[1])
+                nc.vector.quantize_mx(
+                    out=x_codes[a][:, c0:c1].bitcast(FP8X4), scales=x_plane[a][:, c0:c1], in_=rounded(a, c0, c1)
+                )
 
-        def experts(group):
-            s0, s1 = GROUPS[group]
-            for h in range(HALVES):
-                cols = slice(h * P, (h + 1) * P)
-                for e in range(s0 // C, s1 // C):
+        def product(acc, e, h):
+            cols = slice(h * P, (h + 1) * P)
+            slots = slice(e * C, (e + 1) * C)
+            for a in range(PASSES):
+                nc.tensor.matmul_mx(
+                    out=acc,
+                    lhsT=w_codes[:, e * PASSES + a, cols].bitcast(FP8X4),
+                    lhsT_scale=w_plane[:, e * PASSES + a, cols],
+                    rhs=x_codes[a][:, slots].bitcast(FP8X4),
+                    rhs_scale=x_plane[a][:, slots],
+                    start=(a == 0),
+                    stop=(a == PASSES - 1),
+                )
+
+        def silu(acc, e, h):
+            nc.scalar.activation(y[h][:, e * C : (e + 1) * C], acc, SILU, bias=(bias_a if e * C < A[1] else bias_b if e * C < B1[1] else bias_sb)[:, h, e : e + 1])
+
+        def experts(piece, halves):
+            for h in halves:
+                for e in range(piece[0] // C, piece[1] // C):
                     acc = psum.tile([P, C], F32, name="acc")
-                    slots = slice(e * C - s0, (e + 1) * C - s0)
-                    for a in range(PASSES):
-                        nc.tensor.matmul_mx(
-                            out=acc[:],
-                            lhsT=w_codes[:, e * PASSES + a, cols].bitcast(FP8X4),
-                            lhsT_scale=w_plane[:, e * PASSES + a, cols],
-                            rhs=x_codes[group * PASSES + a][:, slots].bitcast(FP8X4),
-                            rhs_scale=x_plane[group * PASSES + a][:, slots],
-                            start=(a == 0),
-                            stop=(a == PASSES - 1),
-                        )
-                    nc.scalar.activation(
-                        y[h][:, e * C : (e + 1) * C], acc[:], SILU, bias=bias_sb[group][:, h, e : e + 1]
-                    )
+                    product(acc[:], e, h)
+                    silu(acc[:], e, h)
 
-        def finish(i):
-            a, s0, s1 = STEPS[i]
-            for c0 in range(s0, s1, QUANT_SLOTS):
-                quantise(i, c0, min(c0 + QUANT_SLOTS, s1))
-            if a == PASSES - 1:
-                experts(i // PASSES)
+        def late_bank(tag, es, h):
+            bank = late.tile([P, 4 * C], F32, name=tag)
+            for i, e in enumerate(es):
+                product(bank[:, i * C : (i + 1) * C], e, h)
+            for i, e in enumerate(es):
+                silu(bank[:, i * C : (i + 1) * C], e, h)
 
-        last = len(STEPS) - 1
-        for i in range(last):
-            gather(i)
-            interleave(nc.scalar.copy, i, STEPS[i][1], STEPS[i][2])
-            if i > 0:
-                finish(i - 1)
+        gather(0, A, (0,), HEAD)
+        gather(0, A, (1, 2, 3))
+        interleave(nc.scalar.copy, 0, A, A)
+        gather(1, A, range(PACK))
+        interleave(nc.scalar.copy, 1, A, A)
+        quantise(0, A)
+        gather(0, BC, (0, 1))
+        quantise(1, A)
+        experts(A, range(HALVES))
+        gather(0, BC, (2, 3))
+        interleave(nc.scalar.copy, 0, BC, BC)
+        gather(1, B, range(PACK))
+        interleave(nc.scalar.copy, 1, B, B1)
+        interleave(nc.scalar.copy, 1, B, B2)
+        quantise(0, BC)
+        gather(1, C_, (0, 1))
+        quantise(1, B1)
+        experts(B1, (0, 1))
+        gather(1, C_, (2, 3))
+        interleave(nc.scalar.copy, 1, C_, C1)
+        quantise(1, B2)
+        experts(B2, (0,))
+        interleave(nc.vector.tensor_copy, 1, C_, C2)
+        quantise(1, C1)
+        late_bank("bank_x", [10], 0)
+        quantise(1, C2)
+        late_bank("bank_y", [11], 0)
+        late_bank("bank_x", [8, 10], 1)
+        late_bank("bank_y", [9, 11], 1)
 
-        s0, s1 = GROUPS[-1]
-        middle = (s0 + s1) // 2
-        gather(last)
-        interleave(nc.scalar.copy, last, s0, middle)
-        quantise(last - 1, s0, middle)
-        interleave(nc.vector.tensor_copy, last, middle, s1)
-        quantise(last - 1, middle, s1)
-        quantise(last, s0, middle)
-        quantise(last, middle, s1)
-        experts(len(GROUPS) - 1)
+        total = [
+            shared.tile([P, T], F32, name="total0", offset=0),
+            shared.tile([P, T], F32, name="total1", offset=4 * T),
+        ]
 
-        def fetch(dst, positions, piece):
-            h, t0, t1 = piece
-            nc.vector.tensor_copy(dst[h][:, t0:t1], y[h][:].indirect(positions[:, t0 // LANES : t1 // LANES]))
+        def window(h, positions, t0, t1):
+            return y[h][:].indirect(positions[:, t0 // LANES : t1 // LANES])
 
-        def combine(engine, piece):
-            h, t0, t1 = piece
-            engine.tensor_tensor(total[h][:, t0:t1], first[h][:, t0:t1], second[h][:, t0:t1], ADD)
+        for h in range(HALVES):
+            nc.vector.tensor_copy(first[h][:], window(h, pos1_sb, 0, T))
+        for h, t0, t1 in BACK:
+            nc.vector.tensor_tensor(total[h][:, t0:t1], window(h, pos2_sb, t0, t1), first[h][:, t0:t1], ADD)
             nc.sync.dma_start(out[h * P : (h + 1) * P, t0:t1], total[h][:, t0:t1])
-
-        for i, piece in enumerate(BACK):
-            fetch(first, pos1_sb, piece)
-            if i > 0:
-                combine(nc.gpsimd, BACK[i - 1])
-            fetch(second, pos2_sb, piece)
-        h, t0, t1 = BACK[-1]
-        combine(nc.vector, (h, t0, (t0 + t1) // 2))
-        combine(nc.vector, (h, (t0 + t1) // 2, t1))

@@ -32,10 +32,10 @@ A, B, C_ = (0, 768), (768, 1280), (1280, S)
 BC = (768, S)
 B1, B2 = (768, 1024), (1024, 1280)
 C1, C2 = (1280, 1408), (1408, S)
-PLACE = {(0, BC): (0, 768), (1, A): (2288, 768), (1, B): (3072, 512), (1, C_): (2304, 512), (0, A): (5360, 768)}
+PLACE = {(0, BC): (0, 768), (1, A): (2288, 768), (1, B): (3072, 512), (1, C_): (2048, 256), (0, A): (5360, 768)}
 STAGE = {(0, A): 0, (0, BC): 768, (1, B): S, (1, A): S + 512, (1, C1): S + 1280, (1, C2): S + 1408}
 ARENA = 5360 + 4 * 768
-BACK = [(0, 0, 768), (1, 0, 576), (1, 576, 768)]
+BACK = [(0, 0, 768), (1, 0, 416), (1, 416, 640), (1, 640, 768)]
 BIAS_COLUMNS = 16
 
 
@@ -43,7 +43,7 @@ def tile_moe_pre_lin_silu_kernel(tc, xT, w_words, w_scales, b, gate, offs, pos1,
     nc = tc.nc
     with ExitStack() as ctx:
         keep = ctx.enter_context(tc.tile_pool(name="keep", bufs=1))
-        psum = ctx.enter_context(tc.psum_pool(name="psum", bufs=6))
+        psum = ctx.enter_context(tc.psum_pool(name="psum", bufs=4))
         late = ctx.enter_context(tc.psum_pool(name="late", bufs=1))
 
         offs_sb = keep.tile([P, S // LANES], U16, name="offs_sb")
@@ -62,7 +62,6 @@ def tile_moe_pre_lin_silu_kernel(tc, xT, w_words, w_scales, b, gate, offs, pos1,
         bias_sb = shared.tile([P, HALVES, BIAS_COLUMNS], F32, name="bias_sb", offset=0)
         staged = ctx.enter_context(tc.tile_pool(name="staged", bufs=1))
         bias_a = staged.tile([P, HALVES, BIAS_COLUMNS], F32, name="bias_a", offset=8 * S - 64, align_bytes=64)
-        bias_b = staged.tile([P, HALVES, BIAS_COLUMNS], F32, name="bias_b", offset=8 * STAGE[(1, C1)], align_bytes=64)
         grouped = {}
 
         nc.vector.memset(w_plane[:].rearrange("p g n -> p (g n)").bitcast(I32), 0)
@@ -85,7 +84,7 @@ def tile_moe_pre_lin_silu_kernel(tc, xT, w_words, w_scales, b, gate, offs, pos1,
         nc.sync.dma_start(gate_sb[:, BC[0] : S], gate[0:P, BC[0] : S])
         for q in range(QUADRANTS):
             nc.sync.dma_start(w_plane[32 * q : 32 * q + 4].bitcast(I32), scale_rows[4 * q : 4 * q + 4].bitcast(I32))
-        for bias in (bias_a, bias_b, bias_sb):
+        for bias in (bias_a, bias_sb):
             nc.sync.dma_start(bias[:, :, 0:E], b.rearrange("(h p) e -> p h e", p=P))
         for s0, s1 in (A, B, C_):
             g = slice(s0 // C * PASSES, s1 // C * PASSES)
@@ -150,7 +149,7 @@ def tile_moe_pre_lin_silu_kernel(tc, xT, w_words, w_scales, b, gate, offs, pos1,
                 )
 
         def silu(acc, e, h):
-            nc.scalar.activation(y[h][:, e * C : (e + 1) * C], acc, SILU, bias=(bias_a if e * C < A[1] else bias_b if e * C < B1[1] else bias_sb)[:, h, e : e + 1])
+            nc.scalar.activation(y[h][:, e * C : (e + 1) * C], acc, SILU, bias=(bias_a if e * C < A[1] else bias_sb)[:, h, e : e + 1])
 
         def experts(piece, halves):
             for h in halves:
@@ -178,23 +177,19 @@ def tile_moe_pre_lin_silu_kernel(tc, xT, w_words, w_scales, b, gate, offs, pos1,
         gather(0, BC, (2, 3))
         interleave(nc.scalar.copy, 0, BC, BC)
         gather(1, B, range(PACK))
-        interleave(nc.scalar.copy, 1, B, B1)
-        interleave(nc.scalar.copy, 1, B, B2)
+        interleave(nc.scalar.copy, 1, B, B)
         quantise(0, BC)
-        gather(1, C_, (0, 1))
-        quantise(1, B1)
-        experts(B1, (0, 1))
-        gather(1, C_, (2, 3))
+        gather(1, C_, (0, 1, 2))
+        gather(1, C_, (3,), [C1[0], C2[0], S])
         interleave(nc.scalar.copy, 1, C_, C1)
-        quantise(1, B2)
-        experts(B2, (0,))
-        interleave(nc.vector.tensor_copy, 1, C_, C2)
+        interleave(nc.scalar.copy, 1, C_, C2)
+        quantise(1, B)
+        experts(B, (0,))
         quantise(1, C1)
         late_bank("bank_x", [10], 0)
         quantise(1, C2)
         late_bank("bank_y", [11], 0)
-        late_bank("bank_x", [8, 10], 1)
-        late_bank("bank_y", [9, 11], 1)
+        experts(BC, (1,))
 
         total = [
             shared.tile([P, T], F32, name="total0", offset=0),

@@ -1,6 +1,7 @@
 from contextlib import ExitStack
 
 import concourse.mybir as mybir
+from concourse.masks import make_identity
 
 K, T, E, C, N = 1024, 768, 12, 128, 256
 S = E * C
@@ -15,6 +16,7 @@ U8 = mybir.dt.uint8
 FP8X4 = mybir.dt.float8_e4m3fn_x4
 MULT = mybir.AluOpType.mult
 ADD = mybir.AluOpType.add
+COPY = mybir.ActivationFunctionType.Copy
 SILU = mybir.ActivationFunctionType.Silu
 
 P = 128
@@ -24,183 +26,223 @@ HALVES = N // P
 LANES = 16
 QUADRANTS = 4
 LINE = 4
+TURNS = 4
+ALIGN = 64
 
-WINDOW = T + LANES
+ALL, EARLY, LATE = (0, S), (0, S // 2), (S // 2, S)
+GROUP = S // 2
 
-HEAD = [0, 256, 768]
-A, B, C_ = (0, 768), (768, 1280), (1280, S)
-BC = (768, S)
-B1, B2 = (768, 1024), (1024, 1280)
-C1, C2 = (1280, 1408), (1408, S)
-PLACE = {(0, BC): (0, 768), (1, A): (2288, 768), (1, B): (3072, 512), (1, C_): (2048, 256), (0, A): (5360, 768)}
-STAGE = {(0, A): 0, (0, BC): 768, (1, B): S, (1, A): S + 512, (1, C1): S + 1280, (1, C2): S + 1408}
-ARENA = 5360 + 4 * 768
+WINDOWS = [S + LANES, GROUP + LANES]
+FIRST_WINDOW = S * 4 // 3
+
+EARLY_PAIRS = [(0, 256), (256, 512), (512, 768)]
+EARLY_COPIES = [(0, 256), (256, 768)]
+LAST_ROW_CUTS = [768, 896, 1152, S]
+LATE_COPIES = [(768, 896), (896, 1152), (1152, 1408), (1408, S)]
+QUANT_SLOTS = 512
+
 BACK = [(0, 0, 768), (1, 0, 416), (1, 416, 640), (1, 640, 768)]
+
+PASS1_AT = {LATE: 0, EARLY: 2 * GROUP - EARLY_COPIES[0][1]}
+PASS1_COLUMNS = PASS1_AT[EARLY] + PACK * GROUP
+
+SLOT_BYTES = 2 * PACK
+ROUNDED0_AT = 0
+GATHERED0_AT = ROUNDED0_AT + SLOT_BYTES * S
+ROUNDED1_EARLY_AT = GATHERED0_AT + 4 * PACK * S - ALIGN
+LATE_CODES0_AT = ROUNDED1_EARLY_AT + SLOT_BYTES * GROUP
+ROUNDED1_LATE_AT = LATE_CODES0_AT + 4 * GROUP
+EARLY_BIAS_AT = ROUNDED1_LATE_AT - ALIGN
 BIAS_COLUMNS = 16
+
+RING_BANKS = 4
+NAMED_BANKS = ("bank_w", "bank_x", "bank_y", "bank_z")
 
 
 def tile_moe_pre_lin_silu_kernel(tc, xT, w_words, w_scales, b, gate, offs, pos1, pos2, out):
     nc = tc.nc
     with ExitStack() as ctx:
         keep = ctx.enter_context(tc.tile_pool(name="keep", bufs=1))
-        psum = ctx.enter_context(tc.psum_pool(name="psum", bufs=4))
-        late = ctx.enter_context(tc.psum_pool(name="late", bufs=1))
+        staged = ctx.enter_context(tc.tile_pool(name="staged", bufs=1))
+        ending = ctx.enter_context(tc.tile_pool(name="ending", bufs=1))
+        ring = ctx.enter_context(tc.psum_pool(name="ring", bufs=RING_BANKS))
+        named = ctx.enter_context(tc.psum_pool(name="named", bufs=1))
 
         offs_sb = keep.tile([P, S // LANES], U16, name="offs_sb")
         pos1_sb = keep.tile([P, T // LANES], U16, name="pos1_sb")
         pos2_sb = keep.tile([P, T // LANES], U16, name="pos2_sb")
         gate_sb = keep.tile([P, S], F32, name="gate_sb")
-        row_tiles = [[keep.tile([P, WINDOW], F32, name="x%d%d" % (a, j)) for j in range(PACK)] for a in range(PASSES)]
-        w_codes = keep.tile([P, E * PASSES, N], U32, name="w_codes", align_bytes=64)
-        w_plane = keep.tile([P, E * PASSES, N], U8, name="w_plane", align_bytes=64)
-        arena = keep.tile([P, ARENA], F32, name="arena", align_bytes=64)
-        x_codes = [keep.tile([P, S], U32, name="x_codes%d" % a, align_bytes=64) for a in range(PASSES)]
-        x_plane = [keep.tile([P, S], U8, name="x_plane%d" % a, align_bytes=64) for a in range(PASSES)]
+        x_sb = {
+            (a, j): keep.tile([P, FIRST_WINDOW if (a, j) == (0, 0) else WINDOWS[a]], F32, name="x%d%d" % (a, j))
+            for a in range(PASSES)
+            for j in range(PACK)
+        }
+        w_codes = keep.tile([P, E * PASSES, N], U32, name="w_codes", align_bytes=ALIGN)
+        w_plane = keep.tile([P, E * PASSES, N], U8, name="w_plane", align_bytes=ALIGN)
+        gathered1 = keep.tile([P, PASS1_COLUMNS], F32, name="gathered1", align_bytes=ALIGN)
+        x_plane = [keep.tile([P, S], U8, name="x_plane%d" % a, align_bytes=ALIGN) for a in range(PASSES)]
         y = [keep.tile([P, S], F32, name="y%d" % h) for h in range(HALVES)]
         first = [keep.tile([P, T], F32, name="first%d" % h) for h in range(HALVES)]
-        shared = ctx.enter_context(tc.tile_pool(name="shared", bufs=1))
-        bias_sb = shared.tile([P, HALVES, BIAS_COLUMNS], F32, name="bias_sb", offset=0)
-        staged = ctx.enter_context(tc.tile_pool(name="staged", bufs=1))
-        bias_a = staged.tile([P, HALVES, BIAS_COLUMNS], F32, name="bias_a", offset=8 * S - 64, align_bytes=64)
-        grouped = {}
+        ungated = keep.tile([P, S], F32, name="ungated")
+        gate_by_slot = keep.tile([P, E], F32, name="gate_by_slot")
+        gated_by_slot = keep.tile([P, S], F32, name="gated_by_slot")
+        identity = keep.tile([P, P], F32, name="identity")
+        gathered0 = staged.tile([P, PACK * S], F32, name="gathered0", offset=GATHERED0_AT, align_bytes=ALIGN)
+        early_bias = staged.tile([P, HALVES, BIAS_COLUMNS], F32, name="early_bias", offset=EARLY_BIAS_AT, align_bytes=ALIGN)
+        late_bias = ending.tile([P, HALVES, BIAS_COLUMNS], F32, name="late_bias", offset=0)
+        x_codes = {
+            key: keep.tile([P, GROUP], U32, name="x_codes%d_%d" % (key[0], key[1][0]), align_bytes=ALIGN)
+            for key in ((0, EARLY), (1, EARLY), (1, LATE))
+        }
+        rounded = {}
 
+        make_identity(nc, identity[:])
         nc.vector.memset(w_plane[:].rearrange("p g n -> p (g n)").bitcast(I32), 0)
 
         x_rows = xT.rearrange("(a p j) t -> a j p t", a=PASSES, j=PACK)
         words = w_words.rearrange("e a p n r -> p (e a) (n r)")
         scale_rows = w_scales.rearrange("e a q n -> q (e a) n")
-
-        def load_rows(a, j):
-            nc.sync.dma_start(row_tiles[a][j][:, 0:T], x_rows[a, j])
-
-        load_rows(0, 0)
-        nc.sync.dma_start(offs_sb[:], offs)
-        for c0, c1 in zip(HEAD, HEAD[1:]):
-            nc.sync.dma_start(gate_sb[:, c0:c1], gate[0:P, c0:c1])
-        for a in range(PASSES):
-            for j in range(PACK):
-                if (a, j) != (0, 0):
-                    load_rows(a, j)
-        nc.sync.dma_start(gate_sb[:, BC[0] : S], gate[0:P, BC[0] : S])
+        for (a, j), tile in x_sb.items():
+            nc.sync.dma_start(tile[:, 0:T], x_rows[a, j])
+            if (a, j) == (0, 0):
+                nc.sync.dma_start(offs_sb[:], offs)
+                nc.sync.dma_start(gate_sb[:], gate[0:P, :])
         for q in range(QUADRANTS):
             nc.sync.dma_start(w_plane[32 * q : 32 * q + 4].bitcast(I32), scale_rows[4 * q : 4 * q + 4].bitcast(I32))
-        for bias in (bias_a, bias_sb):
+        for bias in (early_bias, late_bias):
             nc.sync.dma_start(bias[:, :, 0:E], b.rearrange("(h p) e -> p h e", p=P))
-        for s0, s1 in (A, B, C_):
+        for s0, s1 in (EARLY, LATE):
             g = slice(s0 // C * PASSES, s1 // C * PASSES)
             nc.sync.dma_start(w_codes[:, g, :].bitcast(I32), words[:, g, :].bitcast(I32))
         nc.sync.dma_start(pos1_sb[:], pos1)
         nc.sync.dma_start(pos2_sb[:], pos2)
 
-        def rows(a, group):
-            base, stride = PLACE[(a, group)]
-            view = arena[:, base : base + PACK * stride].rearrange("p (j s) -> p j s", j=PACK)
-            return view[:, :, 0 : group[1] - group[0]]
+        def group_of(s):
+            return EARLY if s < EARLY[1] else LATE
 
-        def gather(a, group, js, cuts=None):
-            cuts = cuts or group
-            for j in js:
-                for c0, c1 in zip(cuts, cuts[1:]):
-                    nc.vector.tensor_tensor(
-                        rows(a, group)[:, j, c0 - group[0] : c1 - group[0]],
-                        row_tiles[a][j][:].indirect(offs_sb[:, c0 // LANES : c1 // LANES]),
-                        gate_sb[:, c0:c1],
-                        MULT,
-                    )
+        def gathered(a, c0, c1):
+            if a == 0:
+                return gathered0[:].rearrange("p (j s) -> p j s", j=PACK)[:, :, c0:c1]
+            group = group_of(c0)
+            rows = gathered1[:, PASS1_AT[group] : PASS1_AT[group] + PACK * GROUP].rearrange("p (j s) -> p j s", j=PACK)
+            return rows[:, :, c0 - group[0] : c1 - group[0]]
 
-        def rounded(a, c0, c1):
-            home = [g for pa, g in STAGE if pa == a and g[0] <= c0 < g[1]][0]
-            if (a, home) not in grouped:
-                grouped[(a, home)] = staged.tile(
-                    [P, PACK * (home[1] - home[0])],
-                    BF16,
-                    name="grouped%d_%d" % (a, home[0]),
-                    offset=8 * STAGE[(a, home)],
-                    align_bytes=64,
-                )
-            return grouped[(a, home)][:, PACK * (c0 - home[0]) : PACK * (c1 - home[0])]
-
-        def interleave(copy, a, group, piece):
-            c0, c1 = piece
-            copy(
-                rounded(a, c0, c1).rearrange("p (c m j) -> p c j m", m=LINE, j=PACK),
-                rows(a, group)[:, :, c0 - group[0] : c1 - group[0]].rearrange("p j (c m) -> p c j m", m=LINE),
+        def gather(a, j, c0, c1):
+            nc.vector.tensor_tensor(
+                gathered(a, c0, c1)[:, j, :],
+                x_sb[(a, j)][:].indirect(offs_sb[:, c0 // LANES : c1 // LANES]),
+                gate_sb[:, c0:c1],
+                MULT,
             )
 
-        def quantise(a, piece):
-            for c0 in range(piece[0], piece[1], 512):
-                c1 = min(c0 + 512, piece[1])
-                nc.vector.quantize_mx(
-                    out=x_codes[a][:, c0:c1].bitcast(FP8X4), scales=x_plane[a][:, c0:c1], in_=rounded(a, c0, c1)
-                )
+        def turn(bank, source, e0):
+            for i in range(TURNS):
+                nc.tensor.transpose(bank[:, i, :], source[:, (e0 + i) * C : (e0 + i + 1) * C], identity[:])
 
-        def product(acc, e, h):
+        def rounded_slots(a, c0, c1):
+            group = ALL if a == 0 else group_of(c0)
+            return rounded[(a, group)][:, PACK * (c0 - group[0]) : PACK * (c1 - group[0])]
+
+        def interleave(a, c0, c1):
+            nc.scalar.copy(
+                rounded_slots(a, c0, c1).rearrange("p (c m j) -> p c j m", m=LINE, j=PACK),
+                gathered(a, c0, c1).rearrange("p j (c m) -> p c j m", m=LINE),
+            )
+
+        def codes(a, c0, c1):
+            group = group_of(c0)
+            return x_codes[(a, group)][:, c0 - group[0] : c1 - group[0]].bitcast(FP8X4)
+
+        def quantise(a, s0, s1):
+            for c0 in range(s0, s1, QUANT_SLOTS):
+                c1 = min(c0 + QUANT_SLOTS, s1)
+                nc.vector.quantize_mx(out=codes(a, c0, c1), scales=x_plane[a][:, c0:c1], in_=rounded_slots(a, c0, c1))
+
+        def expert(e, h, pool, tag):
+            acc = pool.tile([P, C], F32, name=tag)
             cols = slice(h * P, (h + 1) * P)
-            slots = slice(e * C, (e + 1) * C)
             for a in range(PASSES):
                 nc.tensor.matmul_mx(
-                    out=acc,
+                    out=acc[:],
                     lhsT=w_codes[:, e * PASSES + a, cols].bitcast(FP8X4),
                     lhsT_scale=w_plane[:, e * PASSES + a, cols],
-                    rhs=x_codes[a][:, slots].bitcast(FP8X4),
-                    rhs_scale=x_plane[a][:, slots],
+                    rhs=codes(a, e * C, (e + 1) * C),
+                    rhs_scale=x_plane[a][:, e * C : (e + 1) * C],
                     start=(a == 0),
                     stop=(a == PASSES - 1),
                 )
+            bias = early_bias if group_of(e * C) == EARLY else late_bias
+            nc.scalar.activation(y[h][:, e * C : (e + 1) * C], acc[:], SILU, bias=bias[:, h, e : e + 1])
 
-        def silu(acc, e, h):
-            nc.scalar.activation(y[h][:, e * C : (e + 1) * C], acc, SILU, bias=(bias_a if e * C < A[1] else bias_sb)[:, h, e : e + 1])
+        nc.vector.tensor_copy(ungated[:], x_sb[(0, 0)][:].indirect(offs_sb[:]))
+        for e0, tag in zip(range(0, E, TURNS), NAMED_BANKS):
+            bank = named.tile([P, TURNS, P], F32, name=tag)
+            turn(bank, gate_sb, e0)
+            nc.scalar.copy(gate_by_slot[:, e0 : e0 + TURNS], bank[:, :, 0])
+        for e0 in range(0, E, TURNS):
+            bank = ring.tile([P, TURNS, P], F32, name="ring_bank")
+            turn(bank, ungated, e0)
+            for e in range(e0, e0 + TURNS):
+                nc.scalar.activation(
+                    gated_by_slot[:, e * C : (e + 1) * C], bank[:, e - e0, :], COPY, scale=gate_by_slot[:, e : e + 1]
+                )
+        for e0, tag in zip(range(0, E, TURNS), NAMED_BANKS):
+            bank = named.tile([P, TURNS, P], F32, name=tag)
+            turn(bank, gated_by_slot, e0)
+            nc.scalar.copy(gathered(0, e0 * C, (e0 + TURNS) * C)[:, 0, :], bank[:].rearrange("p i s -> p (i s)"))
 
-        def experts(piece, halves):
-            for h in halves:
-                for e in range(piece[0] // C, piece[1] // C):
-                    acc = psum.tile([P, C], F32, name="acc")
-                    product(acc[:], e, h)
-                    silu(acc[:], e, h)
+        for j in range(1, PACK):
+            gather(0, j, *ALL)
+        rounded[(0, ALL)] = staged.tile([P, PACK * S], BF16, name="rounded0", offset=ROUNDED0_AT, align_bytes=ALIGN)
+        for group in (EARLY, LATE):
+            interleave(0, *group)
 
-        def late_bank(tag, es, h):
-            bank = late.tile([P, 4 * C], F32, name=tag)
-            for i, e in enumerate(es):
-                product(bank[:, i * C : (i + 1) * C], e, h)
-            for i, e in enumerate(es):
-                silu(bank[:, i * C : (i + 1) * C], e, h)
+        for j in range(PACK):
+            gather(1, j, *EARLY)
+        rounded[(1, EARLY)] = staged.tile(
+            [P, PACK * GROUP], BF16, name="rounded1_early", offset=ROUNDED1_EARLY_AT, align_bytes=ALIGN
+        )
+        for piece in EARLY_COPIES:
+            interleave(1, *piece)
+        gather(1, 0, *LATE)
+        quantise(0, *EARLY)
+        for i, (s0, s1) in enumerate(EARLY_PAIRS):
+            quantise(1, s0, s1)
+            products = [(e, h) for h in range(HALVES) for e in range(s0 // C, s1 // C)]
+            for (e, h), tag in zip(products, NAMED_BANKS):
+                if i == 1:
+                    expert(e, h, named, tag)
+                else:
+                    expert(e, h, ring, "ring_bank")
+            if i == 0:
+                gather(1, 1, *LATE)
 
-        gather(0, A, (0,), HEAD)
-        gather(0, A, (1, 2, 3))
-        interleave(nc.scalar.copy, 0, A, A)
-        gather(1, A, range(PACK))
-        interleave(nc.scalar.copy, 1, A, A)
-        quantise(0, A)
-        gather(0, BC, (0, 1))
-        quantise(1, A)
-        experts(A, range(HALVES))
-        gather(0, BC, (2, 3))
-        interleave(nc.scalar.copy, 0, BC, BC)
-        gather(1, B, range(PACK))
-        interleave(nc.scalar.copy, 1, B, B)
-        quantise(0, BC)
-        gather(1, C_, (0, 1, 2))
-        gather(1, C_, (3,), [C1[0], C2[0], S])
-        interleave(nc.scalar.copy, 1, C_, C1)
-        interleave(nc.scalar.copy, 1, C_, C2)
-        quantise(1, B)
-        experts(B, (0,))
-        quantise(1, C1)
-        late_bank("bank_x", [10], 0)
-        quantise(1, C2)
-        late_bank("bank_y", [11], 0)
-        experts(BC, (1,))
+        gather(1, 2, *LATE)
+        for c0, c1 in zip(LAST_ROW_CUTS, LAST_ROW_CUTS[1:]):
+            gather(1, PACK - 1, c0, c1)
+        rounded[(1, LATE)] = staged.tile(
+            [P, PACK * GROUP], BF16, name="rounded1_late", offset=ROUNDED1_LATE_AT, align_bytes=ALIGN
+        )
+        for piece in LATE_COPIES:
+            interleave(1, *piece)
+        x_codes[(0, LATE)] = staged.tile([P, GROUP], U32, name="late_codes0", offset=LATE_CODES0_AT, align_bytes=ALIGN)
+        quantise(0, *LATE)
+        last_two = dict(zip((E - 2, E - 1), NAMED_BANKS))
+        for s0, s1 in LATE_COPIES:
+            quantise(1, s0, s1)
+            for e in range(s0 // C, s1 // C):
+                if e in last_two:
+                    expert(e, 0, named, last_two[e])
+                else:
+                    expert(e, 0, ring, "ring_bank")
+        for e in range(LATE[0] // C, E):
+            expert(e, 1, ring, "ring_bank")
 
-        total = [
-            shared.tile([P, T], F32, name="total0", offset=0),
-            shared.tile([P, T], F32, name="total1", offset=4 * T),
-        ]
-
-        def window(h, positions, t0, t1):
-            return y[h][:].indirect(positions[:, t0 // LANES : t1 // LANES])
-
+        total = [ending.tile([P, T], F32, name="total%d" % h, offset=4 * T * h) for h in range(HALVES)]
         for h in range(HALVES):
-            nc.vector.tensor_copy(first[h][:], window(h, pos1_sb, 0, T))
+            nc.vector.tensor_copy(first[h][:], y[h][:].indirect(pos1_sb[:]))
         for h, t0, t1 in BACK:
-            nc.vector.tensor_tensor(total[h][:, t0:t1], window(h, pos2_sb, t0, t1), first[h][:, t0:t1], ADD)
+            nc.vector.tensor_tensor(
+                total[h][:, t0:t1], y[h][:].indirect(pos2_sb[:, t0 // LANES : t1 // LANES]), first[h][:, t0:t1], ADD
+            )
             nc.sync.dma_start(out[h * P : (h + 1) * P, t0:t1], total[h][:, t0:t1])

@@ -97,6 +97,8 @@ def tile_moe_pre_lin_silu_kernel(tc, xT, w_words, w_scales, b, gate, offs, pos1,
         rounded = {}
 
         make_identity(nc, identity[:])
+        warm = keep.tile([P, 1], F32, name="warm")
+        nc.scalar.activation(warm[:], identity[:, 0:1], SILU)
         nc.vector.memset(w_plane[:].rearrange("p g n -> p (g n)").bitcast(I32), 0)
 
         x_rows = xT.rearrange("(a p j) t -> a j p t", a=PASSES, j=PACK)

@@ -35,7 +35,8 @@ GROUP = S // 2
 WINDOWS = [S + LANES, GROUP + LANES]
 FIRST_WINDOW = S * 4 // 3
 
-EARLY_PAIRS = [(0, 256), (256, 512), (512, 768)]
+EARLY_PAIRS = [(0, 256), (256, 512)]
+HELD = (512, 768)
 EARLY_COPIES = [(0, 256), (256, 768)]
 LAST_ROW_CUTS = [768, 896, 1152, S]
 LATE_COPIES = [(768, 896), (896, 1152), (1152, 1408), (1408, S)]
@@ -51,7 +52,8 @@ ROUNDED0_AT = 0
 GATHERED0_AT = ROUNDED0_AT + SLOT_BYTES * S
 ROUNDED1_EARLY_AT = GATHERED0_AT + 4 * PACK * S - ALIGN
 LATE_CODES0_AT = ROUNDED1_EARLY_AT + SLOT_BYTES * GROUP
-ROUNDED1_LATE_AT = LATE_CODES0_AT + 4 * GROUP
+HELD_WORDS = (S - HELD[0]) + (HELD[1] - HELD[0])
+ROUNDED1_LATE_AT = LATE_CODES0_AT + 4 * HELD_WORDS
 EARLY_BIAS_AT = ROUNDED1_LATE_AT - ALIGN
 BIAS_COLUMNS = 16
 
@@ -90,10 +92,9 @@ def tile_moe_pre_lin_silu_kernel(tc, xT, w_words, w_scales, b, gate, offs, pos1,
         gathered0 = staged.tile([P, PACK * S], F32, name="gathered0", offset=GATHERED0_AT, align_bytes=ALIGN)
         early_bias = staged.tile([P, HALVES, BIAS_COLUMNS], F32, name="early_bias", offset=EARLY_BIAS_AT, align_bytes=ALIGN)
         late_bias = ending.tile([P, HALVES, BIAS_COLUMNS], F32, name="late_bias", offset=0)
-        x_codes = {
-            key: keep.tile([P, GROUP], U32, name="x_codes%d_%d" % (key[0], key[1][0]), align_bytes=ALIGN)
-            for key in ((0, EARLY), (1, EARLY), (1, LATE))
-        }
+        early_codes = [keep.tile([P, HELD[0]], U32, name="early_codes%d" % a, align_bytes=ALIGN) for a in range(PASSES)]
+        late_codes1 = keep.tile([P, GROUP], U32, name="late_codes1", align_bytes=ALIGN)
+        held_codes = []
         rounded = {}
 
         make_identity(nc, identity[:])
@@ -152,29 +153,41 @@ def tile_moe_pre_lin_silu_kernel(tc, xT, w_words, w_scales, b, gate, offs, pos1,
             )
 
         def codes(a, c0, c1):
-            group = group_of(c0)
-            return x_codes[(a, group)][:, c0 - group[0] : c1 - group[0]].bitcast(FP8X4)
+            if c0 < HELD[0]:
+                return early_codes[a][:, c0:c1].bitcast(FP8X4)
+            if a == 0:
+                return held_codes[0][:, c0 - HELD[0] : c1 - HELD[0]].bitcast(FP8X4)
+            if c0 < HELD[1]:
+                at = S - 2 * HELD[0]
+                return held_codes[0][:, at + c0 : at + c1].bitcast(FP8X4)
+            return late_codes1[:, c0 - LATE[0] : c1 - LATE[0]].bitcast(FP8X4)
 
         def quantise(a, s0, s1):
             for c0 in range(s0, s1, QUANT_SLOTS):
                 c1 = min(c0 + QUANT_SLOTS, s1)
                 nc.vector.quantize_mx(out=codes(a, c0, c1), scales=x_plane[a][:, c0:c1], in_=rounded_slots(a, c0, c1))
 
+        def product(acc, e, h, a):
+            cols = slice(h * P, (h + 1) * P)
+            nc.tensor.matmul_mx(
+                out=acc[:],
+                lhsT=w_codes[:, e * PASSES + a, cols].bitcast(FP8X4),
+                lhsT_scale=w_plane[:, e * PASSES + a, cols],
+                rhs=codes(a, e * C, (e + 1) * C),
+                rhs_scale=x_plane[a][:, e * C : (e + 1) * C],
+                start=(a == 0),
+                stop=(a == PASSES - 1),
+            )
+
+        def activate(acc, e, h):
+            bias = early_bias if e * C < HELD[0] else late_bias
+            nc.scalar.activation(y[h][:, e * C : (e + 1) * C], acc[:], SILU, bias=bias[:, h, e : e + 1])
+
         def expert(e, h, pool, tag):
             acc = pool.tile([P, C], F32, name=tag)
-            cols = slice(h * P, (h + 1) * P)
             for a in range(PASSES):
-                nc.tensor.matmul_mx(
-                    out=acc[:],
-                    lhsT=w_codes[:, e * PASSES + a, cols].bitcast(FP8X4),
-                    lhsT_scale=w_plane[:, e * PASSES + a, cols],
-                    rhs=codes(a, e * C, (e + 1) * C),
-                    rhs_scale=x_plane[a][:, e * C : (e + 1) * C],
-                    start=(a == 0),
-                    stop=(a == PASSES - 1),
-                )
-            bias = early_bias if group_of(e * C) == EARLY else late_bias
-            nc.scalar.activation(y[h][:, e * C : (e + 1) * C], acc[:], SILU, bias=bias[:, h, e : e + 1])
+                product(acc, e, h, a)
+            activate(acc, e, h)
 
         nc.vector.tensor_copy(ungated[:], x_sb[(0, 0)][:].indirect(offs_sb[:]))
         for e0, tag in zip(range(0, E, TURNS), NAMED_BANKS):
@@ -207,7 +220,7 @@ def tile_moe_pre_lin_silu_kernel(tc, xT, w_words, w_scales, b, gate, offs, pos1,
         for piece in EARLY_COPIES:
             interleave(1, *piece)
         gather(1, 0, *LATE)
-        quantise(0, *EARLY)
+        quantise(0, 0, HELD[0])
         for i, (s0, s1) in enumerate(EARLY_PAIRS):
             quantise(1, s0, s1)
             products = [(e, h) for h in range(HALVES) for e in range(s0 // C, s1 // C)]
@@ -227,17 +240,22 @@ def tile_moe_pre_lin_silu_kernel(tc, xT, w_words, w_scales, b, gate, offs, pos1,
         )
         for piece in LATE_COPIES:
             interleave(1, *piece)
-        x_codes[(0, LATE)] = staged.tile([P, GROUP], U32, name="late_codes0", offset=LATE_CODES0_AT, align_bytes=ALIGN)
-        quantise(0, *LATE)
-        last_two = dict(zip((E - 2, E - 1), NAMED_BANKS))
-        for s0, s1 in LATE_COPIES:
-            quantise(1, s0, s1)
-            for e in range(s0 // C, s1 // C):
-                if e in last_two:
-                    expert(e, 0, named, last_two[e])
-                else:
-                    expert(e, 0, ring, "ring_bank")
-        for e in range(LATE[0] // C, E):
+        held_codes.append(staged.tile([P, HELD_WORDS], U32, name="held_codes", offset=LATE_CODES0_AT, align_bytes=ALIGN))
+        sums = {}
+        for s0, pool, tags, pieces in (
+            (HELD[0], ring, ["ring_bank"] * RING_BANKS, [HELD] + LATE_COPIES[:1]),
+            (HELD[0] + QUANT_SLOTS, named, NAMED_BANKS, LATE_COPIES[1:]),
+        ):
+            quantise(0, s0, s0 + QUANT_SLOTS)
+            for e, tag in zip(range(s0 // C, E), tags):
+                sums[e] = pool.tile([P, C], F32, name=tag)
+                product(sums[e], e, 0, 0)
+            for c0, c1 in pieces:
+                quantise(1, c0, c1)
+                for e in range(c0 // C, c1 // C):
+                    product(sums[e], e, 0, 1)
+                    activate(sums[e], e, 0)
+        for e in range(HELD[0] // C, E):
             expert(e, 1, ring, "ring_bank")
 
         total = [ending.tile([P, T], F32, name="total%d" % h, offset=4 * T * h) for h in range(HALVES)]

@@ -256,7 +256,10 @@ def tile_moe_pre_lin_silu_kernel(tc, xT, w_words, w_scales, b, gate, offs, pos1,
                     product(sums[e], e, 0, 1)
                     activate(sums[e], e, 0)
         for e in range(HELD[0] // C, E):
-            expert(e, 1, ring, "ring_bank")
+            if e < E - len(NAMED_BANKS):
+                expert(e, 1, ring, "ring_bank")
+            else:
+                expert(e, 1, named, NAMED_BANKS[e - E])
 
         total = [ending.tile([P, T], F32, name="total%d" % h, offset=4 * T * h) for h in range(HALVES)]
         for h in range(HALVES):

@@ -28,37 +28,32 @@ QUADRANTS = 4
 LINE = 4
 TURNS = 4
 ALIGN = 64
+BANKS = 8
 
-ALL, EARLY, LATE = (0, S), (0, S // 2), (S // 2, S)
 GROUP = S // 2
-
 WINDOWS = [S + LANES, GROUP + LANES]
 FIRST_WINDOW = S * 4 // 3
 
-EARLY_PAIRS = [(0, 256), (256, 512)]
-HELD = (512, 768)
-EARLY_COPIES = [(0, 256), (256, 768)]
-LAST_ROW_CUTS = [768, 896, 1152, S]
-LATE_COPIES = [(768, 896), (896, 1152), (1152, 1408), (1408, S)]
-QUANT_SLOTS = 512
+EARLY_CALLS = [[(1, 0), (1, 1), (0, 0), (0, 1)], [(0, 2), (0, 3), (1, 2), (1, 3)]]
+FIRST_LATE = E // 2
+LAST_CALLS = [
+    [(1, 6), (0, 4), (0, 5), (0, 6)],
+    [(0, 7), (1, 4), (1, 5), (1, 7)],
+    [(1, 8), (0, 8), (0, 9), (0, 10)],
+    [(0, 11), (1, 9)],
+    [(1, 10)],
+    [(1, 11)],
+]
+CALLS = EARLY_CALLS + LAST_CALLS
+PLACE = {unit: i for i, unit in enumerate(unit for call in CALLS for unit in call)}
 
 BACK = [(0, 0, 768), (1, 0, 416), (1, 416, 640), (1, 640, 768)]
 
-PASS1_AT = {LATE: 0, EARLY: 2 * GROUP - EARLY_COPIES[0][1]}
-PASS1_COLUMNS = PASS1_AT[EARLY] + PACK * GROUP
-
-SLOT_BYTES = 2 * PACK
-ROUNDED0_AT = 0
-GATHERED0_AT = ROUNDED0_AT + SLOT_BYTES * S
-ROUNDED1_EARLY_AT = GATHERED0_AT + 4 * PACK * S - ALIGN
-LATE_CODES0_AT = ROUNDED1_EARLY_AT + SLOT_BYTES * GROUP
-HELD_WORDS = (S - HELD[0]) + (HELD[1] - HELD[0])
-ROUNDED1_LATE_AT = LATE_CODES0_AT + 4 * HELD_WORDS
-EARLY_BIAS_AT = ROUNDED1_LATE_AT - ALIGN
+ROW_STEP = 2 * GROUP - 2 * C
+EARLY_AT = GROUP - 2 * C
+PIECE = GROUP // 2
 BIAS_COLUMNS = 16
-
-RING_BANKS = 4
-NAMED_BANKS = ("bank_w", "bank_x", "bank_y", "bank_z")
+WEIGHT_LOADS = 3
 
 
 def tile_moe_pre_lin_silu_kernel(tc, xT, w_words, w_scales, b, gate, offs, pos1, pos2, out):
@@ -67,8 +62,7 @@ def tile_moe_pre_lin_silu_kernel(tc, xT, w_words, w_scales, b, gate, offs, pos1,
         keep = ctx.enter_context(tc.tile_pool(name="keep", bufs=1))
         staged = ctx.enter_context(tc.tile_pool(name="staged", bufs=1))
         ending = ctx.enter_context(tc.tile_pool(name="ending", bufs=1))
-        ring = ctx.enter_context(tc.psum_pool(name="ring", bufs=RING_BANKS))
-        named = ctx.enter_context(tc.psum_pool(name="named", bufs=1))
+        psum = ctx.enter_context(tc.psum_pool(name="psum", bufs=1))
 
         offs_sb = keep.tile([P, S // LANES], U16, name="offs_sb")
         pos1_sb = keep.tile([P, T // LANES], U16, name="pos1_sb")
@@ -81,21 +75,18 @@ def tile_moe_pre_lin_silu_kernel(tc, xT, w_words, w_scales, b, gate, offs, pos1,
         }
         w_codes = keep.tile([P, E * PASSES, N], U32, name="w_codes", align_bytes=ALIGN)
         w_plane = keep.tile([P, E * PASSES, N], U8, name="w_plane", align_bytes=ALIGN)
-        gathered1 = keep.tile([P, PASS1_COLUMNS], F32, name="gathered1", align_bytes=ALIGN)
-        x_plane = [keep.tile([P, S], U8, name="x_plane%d" % a, align_bytes=ALIGN) for a in range(PASSES)]
+        gathered0 = keep.tile([P, PACK * S], F32, name="gathered0", align_bytes=ALIGN)
+        gathered1 = staged.tile([P, PACK + 1, ROW_STEP], F32, name="gathered1", offset=0)
+        rounded = keep.tile([P, PASSES * S * PACK], BF16, name="rounded", align_bytes=ALIGN)
+        x_codes = keep.tile([P, PASSES * S], U32, name="x_codes", align_bytes=ALIGN)
+        x_plane = keep.tile([P, PASSES * S], U8, name="x_plane", align_bytes=ALIGN)
         y = [keep.tile([P, S], F32, name="y%d" % h) for h in range(HALVES)]
         first = [keep.tile([P, T], F32, name="first%d" % h) for h in range(HALVES)]
         ungated = keep.tile([P, S], F32, name="ungated")
         gate_by_slot = keep.tile([P, E], F32, name="gate_by_slot")
-        gated_by_slot = keep.tile([P, S], F32, name="gated_by_slot")
+        gated_by_slot = staged.tile([P, S], F32, name="gated_by_slot", offset=0)
         identity = keep.tile([P, P], F32, name="identity")
-        gathered0 = staged.tile([P, PACK * S], F32, name="gathered0", offset=GATHERED0_AT, align_bytes=ALIGN)
-        early_bias = staged.tile([P, HALVES, BIAS_COLUMNS], F32, name="early_bias", offset=EARLY_BIAS_AT, align_bytes=ALIGN)
-        late_bias = ending.tile([P, HALVES, BIAS_COLUMNS], F32, name="late_bias", offset=0)
-        early_codes = [keep.tile([P, HELD[0]], U32, name="early_codes%d" % a, align_bytes=ALIGN) for a in range(PASSES)]
-        late_codes1 = keep.tile([P, GROUP], U32, name="late_codes1", align_bytes=ALIGN)
-        held_codes = []
-        rounded = {}
+        bias = ending.tile([P, HALVES, BIAS_COLUMNS], F32, name="bias", offset=0)
 
         make_identity(nc, identity[:])
         warm = keep.tile([P, 1], F32, name="warm")
@@ -110,25 +101,26 @@ def tile_moe_pre_lin_silu_kernel(tc, xT, w_words, w_scales, b, gate, offs, pos1,
             if (a, j) == (0, 0):
                 nc.sync.dma_start(offs_sb[:], offs)
                 nc.sync.dma_start(gate_sb[:], gate[0:P, :])
+            if (a, j) == (0, 1):
+                nc.sync.dma_start(bias[:, :, 0:E], b.rearrange("(h p) e -> p h e", p=P))
         for q in range(QUADRANTS):
             nc.sync.dma_start(w_plane[32 * q : 32 * q + 4].bitcast(I32), scale_rows[4 * q : 4 * q + 4].bitcast(I32))
-        for bias in (early_bias, late_bias):
-            nc.sync.dma_start(bias[:, :, 0:E], b.rearrange("(h p) e -> p h e", p=P))
-        for s0, s1 in (EARLY, LATE):
-            g = slice(s0 // C * PASSES, s1 // C * PASSES)
+        share = E * PASSES // WEIGHT_LOADS
+        for g0 in range(0, E * PASSES, share):
+            g = slice(g0, g0 + share)
             nc.sync.dma_start(w_codes[:, g, :].bitcast(I32), words[:, g, :].bitcast(I32))
         nc.sync.dma_start(pos1_sb[:], pos1)
         nc.sync.dma_start(pos2_sb[:], pos2)
 
-        def group_of(s):
-            return EARLY if s < EARLY[1] else LATE
+        def bank(i, shape):
+            return psum.tile(shape, F32, name="bank%d" % (i % BANKS))
 
         def gathered(a, c0, c1):
             if a == 0:
                 return gathered0[:].rearrange("p (j s) -> p j s", j=PACK)[:, :, c0:c1]
-            group = group_of(c0)
-            rows = gathered1[:, PASS1_AT[group] : PASS1_AT[group] + PACK * GROUP].rearrange("p (j s) -> p j s", j=PACK)
-            return rows[:, :, c0 - group[0] : c1 - group[0]]
+            if c0 < GROUP:
+                return gathered1[:, 1 : 1 + PACK, EARLY_AT + c0 : EARLY_AT + c1]
+            return gathered1[:, 0:PACK, c0 - GROUP : c1 - GROUP]
 
         def gather(a, j, c0, c1):
             nc.vector.tensor_tensor(
@@ -138,128 +130,100 @@ def tile_moe_pre_lin_silu_kernel(tc, xT, w_words, w_scales, b, gate, offs, pos1,
                 MULT,
             )
 
-        def turn(bank, source, e0):
+        def turn(into, source, e0):
             for i in range(TURNS):
-                nc.tensor.transpose(bank[:, i, :], source[:, (e0 + i) * C : (e0 + i + 1) * C], identity[:])
+                nc.tensor.transpose(into[:, i, :], source[:, (e0 + i) * C : (e0 + i + 1) * C], identity[:])
 
-        def rounded_slots(a, c0, c1):
-            group = ALL if a == 0 else group_of(c0)
-            return rounded[(a, group)][:, PACK * (c0 - group[0]) : PACK * (c1 - group[0])]
-
-        def interleave(a, c0, c1):
+        def interleave(a, e0, e1):
+            at = PLACE[(a, e0)] * C * PACK
             nc.scalar.copy(
-                rounded_slots(a, c0, c1).rearrange("p (c m j) -> p c j m", m=LINE, j=PACK),
-                gathered(a, c0, c1).rearrange("p j (c m) -> p c j m", m=LINE),
+                rounded[:, at : at + (e1 - e0) * C * PACK].rearrange("p (c m j) -> p c j m", m=LINE, j=PACK),
+                gathered(a, e0 * C, e1 * C).rearrange("p j (c m) -> p c j m", m=LINE),
             )
 
-        def codes(a, c0, c1):
-            if c0 < HELD[0]:
-                return early_codes[a][:, c0:c1].bitcast(FP8X4)
-            if a == 0:
-                return held_codes[0][:, c0 - HELD[0] : c1 - HELD[0]].bitcast(FP8X4)
-            if c0 < HELD[1]:
-                at = S - 2 * HELD[0]
-                return held_codes[0][:, at + c0 : at + c1].bitcast(FP8X4)
-            return late_codes1[:, c0 - LATE[0] : c1 - LATE[0]].bitcast(FP8X4)
-
-        def quantise(a, s0, s1):
-            for c0 in range(s0, s1, QUANT_SLOTS):
-                c1 = min(c0 + QUANT_SLOTS, s1)
-                nc.vector.quantize_mx(out=codes(a, c0, c1), scales=x_plane[a][:, c0:c1], in_=rounded_slots(a, c0, c1))
+        def quantise(call):
+            c0, c1 = PLACE[call[0]] * C, (PLACE[call[-1]] + 1) * C
+            nc.vector.quantize_mx(
+                out=x_codes[:, c0:c1].bitcast(FP8X4), scales=x_plane[:, c0:c1], in_=rounded[:, PACK * c0 : PACK * c1]
+            )
 
         def product(acc, e, h, a):
             cols = slice(h * P, (h + 1) * P)
+            slots = slice(PLACE[(a, e)] * C, (PLACE[(a, e)] + 1) * C)
             nc.tensor.matmul_mx(
                 out=acc[:],
                 lhsT=w_codes[:, e * PASSES + a, cols].bitcast(FP8X4),
                 lhsT_scale=w_plane[:, e * PASSES + a, cols],
-                rhs=codes(a, e * C, (e + 1) * C),
-                rhs_scale=x_plane[a][:, e * C : (e + 1) * C],
+                rhs=x_codes[:, slots].bitcast(FP8X4),
+                rhs_scale=x_plane[:, slots],
                 start=(a == 0),
                 stop=(a == PASSES - 1),
             )
 
-        def activate(acc, e, h):
-            bias = early_bias if e * C < HELD[0] else late_bias
-            nc.scalar.activation(y[h][:, e * C : (e + 1) * C], acc[:], SILU, bias=bias[:, h, e : e + 1])
+        def lodged(h, piece):
+            return gathered1[:, 2 + h, piece * PIECE : piece * PIECE + 1]
 
-        def expert(e, h, pool, tag):
-            acc = pool.tile([P, C], F32, name=tag)
+        def activate(acc, e, h):
+            column = lodged(h, e // 2) if e < 4 and e % 2 == h else bias[:, h, e : e + 1]
+            nc.scalar.activation(y[h][:, e * C : (e + 1) * C], acc[:], SILU, bias=column)
+
+        def expert(e, h, i):
+            acc = bank(i, [P, C])
             for a in range(PASSES):
                 product(acc, e, h, a)
             activate(acc, e, h)
 
         nc.vector.tensor_copy(ungated[:], x_sb[(0, 0)][:].indirect(offs_sb[:]))
-        for e0, tag in zip(range(0, E, TURNS), NAMED_BANKS):
-            bank = named.tile([P, TURNS, P], F32, name=tag)
-            turn(bank, gate_sb, e0)
-            nc.scalar.copy(gate_by_slot[:, e0 : e0 + TURNS], bank[:, :, 0])
-        for e0 in range(0, E, TURNS):
-            bank = ring.tile([P, TURNS, P], F32, name="ring_bank")
-            turn(bank, ungated, e0)
+        for i, e0 in enumerate(range(0, E, TURNS)):
+            turned = bank(i, [P, TURNS, P])
+            turn(turned, gate_sb, e0)
+            nc.scalar.copy(gate_by_slot[:, e0 : e0 + TURNS], turned[:, :, 0])
+        for i, e0 in enumerate(range(0, E, TURNS)):
+            turned = bank(3 + i, [P, TURNS, P])
+            turn(turned, ungated, e0)
             for e in range(e0, e0 + TURNS):
                 nc.scalar.activation(
-                    gated_by_slot[:, e * C : (e + 1) * C], bank[:, e - e0, :], COPY, scale=gate_by_slot[:, e : e + 1]
+                    gated_by_slot[:, e * C : (e + 1) * C], turned[:, e - e0, :], COPY, scale=gate_by_slot[:, e : e + 1]
                 )
-        for e0, tag in zip(range(0, E, TURNS), NAMED_BANKS):
-            bank = named.tile([P, TURNS, P], F32, name=tag)
-            turn(bank, gated_by_slot, e0)
-            nc.scalar.copy(gathered(0, e0 * C, (e0 + TURNS) * C)[:, 0, :], bank[:].rearrange("p i s -> p (i s)"))
+        for i, e0 in enumerate(range(0, E, TURNS)):
+            turned = bank(6 + i, [P, TURNS, P])
+            turn(turned, gated_by_slot, e0)
+            nc.scalar.copy(gathered(0, e0 * C, (e0 + TURNS) * C)[:, 0, :], turned[:].rearrange("p i s -> p (i s)"))
 
+        for h in range(HALVES):
+            for piece in range(2):
+                nc.scalar.copy(lodged(h, piece), bias[:, h, 2 * piece + h : 2 * piece + h + 1])
         for j in range(1, PACK):
-            gather(0, j, *ALL)
-        rounded[(0, ALL)] = staged.tile([P, PACK * S], BF16, name="rounded0", offset=ROUNDED0_AT, align_bytes=ALIGN)
-        for group in (EARLY, LATE):
-            interleave(0, *group)
-
+            gather(0, j, 0, S)
+        for e0, e1 in ((0, 4), (4, 8), (8, 11)):
+            interleave(0, e0, e1)
         for j in range(PACK):
-            gather(1, j, *EARLY)
-        rounded[(1, EARLY)] = staged.tile(
-            [P, PACK * GROUP], BF16, name="rounded1_early", offset=ROUNDED1_EARLY_AT, align_bytes=ALIGN
-        )
-        for piece in EARLY_COPIES:
-            interleave(1, *piece)
-        gather(1, 0, *LATE)
-        quantise(0, 0, HELD[0])
-        for i, (s0, s1) in enumerate(EARLY_PAIRS):
-            quantise(1, s0, s1)
-            products = [(e, h) for h in range(HALVES) for e in range(s0 // C, s1 // C)]
-            for (e, h), tag in zip(products, NAMED_BANKS):
-                if i == 1:
-                    expert(e, h, named, tag)
-                else:
-                    expert(e, h, ring, "ring_bank")
+            gather(1, j, 0, GROUP)
+        for e0 in range(0, FIRST_LATE, 2):
+            interleave(1, e0, e0 + 2)
+        for i, call in enumerate(EARLY_CALLS):
+            gather(1, i, GROUP, S)
+            quantise(call)
+            for n, (h, e) in enumerate((h, e) for h in range(HALVES) for e in (2 * i, 2 * i + 1)):
+                expert(e, h, 4 * i + n)
             if i == 0:
-                gather(1, 1, *LATE)
-
-        gather(1, 2, *LATE)
-        for c0, c1 in zip(LAST_ROW_CUTS, LAST_ROW_CUTS[1:]):
-            gather(1, PACK - 1, c0, c1)
-        rounded[(1, LATE)] = staged.tile(
-            [P, PACK * GROUP], BF16, name="rounded1_late", offset=ROUNDED1_LATE_AT, align_bytes=ALIGN
-        )
-        for piece in LATE_COPIES:
-            interleave(1, *piece)
-        held_codes.append(staged.tile([P, HELD_WORDS], U32, name="held_codes", offset=LATE_CODES0_AT, align_bytes=ALIGN))
+                interleave(0, E - 1, E)
+        for c0 in (GROUP, GROUP + GROUP // 2):
+            for j in (2, 3):
+                gather(1, j, c0, c0 + GROUP // 2)
+        for e in range(FIRST_LATE, E):
+            interleave(1, e, e + 1)
         sums = {}
-        for s0, pool, tags, pieces in (
-            (HELD[0], ring, ["ring_bank"] * RING_BANKS, [HELD] + LATE_COPIES[:1]),
-            (HELD[0] + QUANT_SLOTS, named, NAMED_BANKS, LATE_COPIES[1:]),
-        ):
-            quantise(0, s0, s0 + QUANT_SLOTS)
-            for e, tag in zip(range(s0 // C, E), tags):
-                sums[e] = pool.tile([P, C], F32, name=tag)
-                product(sums[e], e, 0, 0)
-            for c0, c1 in pieces:
-                quantise(1, c0, c1)
-                for e in range(c0 // C, c1 // C):
-                    product(sums[e], e, 0, 1)
+        for call in LAST_CALLS:
+            quantise(call)
+            for a, e in sorted(call, key=lambda unit: ((1, unit[1]) not in call, unit[1], unit[0])):
+                if a == 0:
+                    sums[e] = bank(e - 4, [P, C])
+                product(sums[e], e, 0, a)
+                if a == 1:
                     activate(sums[e], e, 0)
-        for e in range(HELD[0] // C, E):
-            if e < E - len(NAMED_BANKS):
-                expert(e, 1, ring, "ring_bank")
-            else:
-                expert(e, 1, named, NAMED_BANKS[e - E])
+        for e in range(4, E):
+            expert(e, 1, e - 4)
 
         total = [ending.tile([P, T], F32, name="total%d" % h, offset=4 * T * h) for h in range(HALVES)]
         for h in range(HALVES):

@@ -208,6 +208,17 @@ def tile_moe_pre_lin_silu_kernel(tc, xT, w_words, w_scales, b, gate, offs, pos1,
                 expert(e, h, 4 * i + n)
             if i == 0:
                 interleave(0, E - 1, E)
+        idle = bank(BANKS - 1, [P, 4 * C])
+        for i in range(3):
+            nc.tensor.matmul_mx(
+                out=idle[:],
+                lhsT=w_codes[:, 0, 0:P].bitcast(FP8X4),
+                lhsT_scale=w_plane[:, 0, 0:P],
+                rhs=x_codes[:, 0 : 4 * C].bitcast(FP8X4),
+                rhs_scale=x_plane[:, 0 : 4 * C],
+                start=True,
+                stop=True,
+            )
         for c0 in (GROUP, GROUP + GROUP // 2):
             for j in (2, 3):
                 gather(1, j, c0, c0 + GROUP // 2)

@@ -160,11 +160,16 @@ def tile_moe_pre_lin_silu_kernel(tc, xT, w_words, w_scales, b, gate, offs, pos1,
                 stop=(a == PASSES - 1),
             )
 
-        def lodged(h, piece):
-            return gathered1[:, 2 + h, piece * PIECE : piece * PIECE + 1]
+        lodgings = {
+            (1, 1): gathered1[:, 3, 0:1],
+            (0, 2): gathered1[:, 2, PIECE : PIECE + 1],
+            (1, 3): gathered1[:, 3, PIECE : PIECE + 1],
+            (1, 2): gathered1[:, PACK, EARLY_AT + 2 * C : EARLY_AT + 2 * C + 1],
+        }
+        halfway = gathered1[:, 2, 0:1]
 
         def activate(acc, e, h):
-            column = lodged(h, e // 2) if e < 4 and e % 2 == h else bias[:, h, e : e + 1]
+            column = lodgings.get((h, e), bias[:, h, e : e + 1])
             nc.scalar.activation(y[h][:, e * C : (e + 1) * C], acc[:], SILU, bias=column)
 
         def expert(e, h, i):
@@ -190,9 +195,9 @@ def tile_moe_pre_lin_silu_kernel(tc, xT, w_words, w_scales, b, gate, offs, pos1,
             turn(turned, gated_by_slot, e0)
             nc.scalar.copy(gathered(0, e0 * C, (e0 + TURNS) * C)[:, 0, :], turned[:].rearrange("p i s -> p (i s)"))
 
-        for h in range(HALVES):
-            for piece in range(2):
-                nc.scalar.copy(lodged(h, piece), bias[:, h, 2 * piece + h : 2 * piece + h + 1])
+        for h, e in ((1, 1), (0, 2), (1, 3)):
+            nc.scalar.copy(lodgings[(h, e)], bias[:, h, e : e + 1])
+        nc.scalar.copy(halfway, bias[:, 1, 2:3])
         for j in range(1, PACK):
             gather(0, j, 0, S)
         for e0, e1 in ((0, 4), (4, 8), (8, 11)):
@@ -201,6 +206,8 @@ def tile_moe_pre_lin_silu_kernel(tc, xT, w_words, w_scales, b, gate, offs, pos1,
             gather(1, j, 0, GROUP)
         for e0 in range(0, FIRST_LATE, 2):
             interleave(1, e0, e0 + 2)
+            if e0 == 2:
+                nc.scalar.copy(lodgings[(1, 2)], halfway)
         for i, call in enumerate(EARLY_CALLS):
             gather(1, i, GROUP, S)
             quantise(call)

@@ -1,7 +1,6 @@
 from contextlib import ExitStack
 
 import concourse.mybir as mybir
-from concourse.masks import make_identity
 
 K, T, E, C, N = 1024, 768, 12, 128, 256
 S = E * C
@@ -25,72 +24,55 @@ PASSES = K // (P * PACK)
 HALVES = N // P
 LANES = 16
 QUADRANTS = 4
-LINE = 4
-TURNS = 4
+PAIR = 2
 ALIGN = 64
 BANKS = 8
+WINDOW = T + LANES
 
-GROUP = S // 2
-WINDOWS = [S + LANES, GROUP + LANES]
-FIRST_WINDOW = S * 4 // 3
-
-EARLY_CALLS = [[(1, 0), (1, 1), (0, 0), (0, 1)], [(0, 2), (0, 3), (1, 2), (1, 3)]]
-FIRST_LATE = E // 2
-LAST_CALLS = [
-    [(1, 6), (0, 4), (0, 5), (0, 6)],
-    [(0, 7), (1, 4), (1, 5), (1, 7)],
-    [(1, 8), (0, 8), (0, 9), (0, 10)],
-    [(0, 11), (1, 9)],
-    [(1, 10)],
-    [(1, 11)],
-]
-CALLS = EARLY_CALLS + LAST_CALLS
-PLACE = {unit: i for i, unit in enumerate(unit for call in CALLS for unit in call)}
-
-BACK = [(0, 0, 768), (1, 0, 416), (1, 416, 640), (1, 640, 768)]
-
-ROW_STEP = 2 * GROUP - 2 * C
-EARLY_AT = GROUP - 2 * C
-PIECE = GROUP // 2
+OWN = (0, 3)
+MID = (3, 9)
+LAST = (9, 12)
+GROUPS = [OWN, MID, LAST]
 BIAS_COLUMNS = 16
 WEIGHT_LOADS = 3
+
+OWN_TOKENS = 192
+FETCHES = [(0, 192, 384), (0, 384, 768), (1, 0, 384), (1, 384, 768)]
+SUMS = [(0, 0, 192), (0, 192, 384), (0, 384, 768), (1, 0, 384), (1, 384, 640), (1, 640, 768)]
+STORES = [(0, 0, 768), (1, 0, 384), (1, 384, 640), (1, 640, 768)]
 
 
 def tile_moe_pre_lin_silu_kernel(tc, xT, w_words, w_scales, b, gate, offs, pos1, pos2, out):
     nc = tc.nc
     with ExitStack() as ctx:
         keep = ctx.enter_context(tc.tile_pool(name="keep", bufs=1))
-        staged = ctx.enter_context(tc.tile_pool(name="staged", bufs=1))
-        ending = ctx.enter_context(tc.tile_pool(name="ending", bufs=1))
         psum = ctx.enter_context(tc.psum_pool(name="psum", bufs=1))
 
         offs_sb = keep.tile([P, S // LANES], U16, name="offs_sb")
         pos1_sb = keep.tile([P, T // LANES], U16, name="pos1_sb")
         pos2_sb = keep.tile([P, T // LANES], U16, name="pos2_sb")
-        gate_sb = keep.tile([P, S], F32, name="gate_sb")
-        x_sb = {
-            (a, j): keep.tile([P, FIRST_WINDOW if (a, j) == (0, 0) else WINDOWS[a]], F32, name="x%d%d" % (a, j))
-            for a in range(PASSES)
-            for j in range(PACK)
-        }
+        gate_own = keep.tile([P, OWN[1] * C], F32, name="gate_own")
+        gate_rest = keep.tile([P, S - OWN[1] * C], F32, name="gate_rest")
+        x_sb = {(a, j): keep.tile([P, WINDOW], F32, name="x%d%d" % (a, j)) for a in range(PASSES) for j in range(PACK)}
         w_codes = keep.tile([P, E * PASSES, N], U32, name="w_codes", align_bytes=ALIGN)
         w_plane = keep.tile([P, E * PASSES, N], U8, name="w_plane", align_bytes=ALIGN)
-        gathered0 = keep.tile([P, PACK * S], F32, name="gathered0", align_bytes=ALIGN)
-        gathered1 = staged.tile([P, PACK + 1, ROW_STEP], F32, name="gathered1", offset=0)
-        rounded = keep.tile([P, PASSES * S * PACK], BF16, name="rounded", align_bytes=ALIGN)
-        x_codes = keep.tile([P, PASSES * S], U32, name="x_codes", align_bytes=ALIGN)
-        x_plane = keep.tile([P, PASSES * S], U8, name="x_plane", align_bytes=ALIGN)
+        gathered, rounded, x_codes, x_plane = {}, {}, {}, {}
+        for g, (e0, e1) in enumerate(GROUPS):
+            width = (e1 - e0) * C
+            for a in range(PASSES):
+                gathered[(g, a)] = keep.tile([P, PACK, width], F32, name="gathered%d%d" % (g, a), align_bytes=ALIGN)
+            rounded[g] = keep.tile([P, PASSES * width * PACK], BF16, name="rounded%d" % g, align_bytes=ALIGN)
+            x_codes[g] = keep.tile([P, PASSES * width], U32, name="x_codes%d" % g, align_bytes=ALIGN)
+            x_plane[g] = keep.tile([P, PASSES * width], U8, name="x_plane%d" % g, align_bytes=ALIGN)
         y = [keep.tile([P, S], F32, name="y%d" % h) for h in range(HALVES)]
         first = [keep.tile([P, T], F32, name="first%d" % h) for h in range(HALVES)]
-        ungated = keep.tile([P, S], F32, name="ungated")
-        gate_by_slot = keep.tile([P, E], F32, name="gate_by_slot")
-        gated_by_slot = staged.tile([P, S], F32, name="gated_by_slot", offset=0)
-        identity = keep.tile([P, P], F32, name="identity")
-        bias = ending.tile([P, HALVES, BIAS_COLUMNS], F32, name="bias", offset=0)
+        total = [keep.tile([P, T], F32, name="total%d" % h) for h in range(HALVES)]
+        bias = keep.tile([P, HALVES, BIAS_COLUMNS], F32, name="bias")
 
-        make_identity(nc, identity[:])
+        seed = keep.tile([P, 1], F32, name="seed")
         warm = keep.tile([P, 1], F32, name="warm")
-        nc.scalar.activation(warm[:], identity[:, 0:1], SILU)
+        nc.gpsimd.memset(seed[:], 0.0)
+        nc.scalar.activation(warm[:], seed[:], SILU)
         nc.vector.memset(w_plane[:].rearrange("p g n -> p (g n)").bitcast(I32), 0)
 
         x_rows = xT.rearrange("(a p j) t -> a j p t", a=PASSES, j=PACK)
@@ -100,9 +82,9 @@ def tile_moe_pre_lin_silu_kernel(tc, xT, w_words, w_scales, b, gate, offs, pos1,
             nc.sync.dma_start(tile[:, 0:T], x_rows[a, j])
             if (a, j) == (0, 0):
                 nc.sync.dma_start(offs_sb[:], offs)
-                nc.sync.dma_start(gate_sb[:], gate[0:P, :])
-            if (a, j) == (0, 1):
-                nc.sync.dma_start(bias[:, :, 0:E], b.rearrange("(h p) e -> p h e", p=P))
+                nc.sync.dma_start(gate_own[:], gate[0:P, 0 : OWN[1] * C])
+        nc.sync.dma_start(gate_rest[:], gate[0:P, OWN[1] * C : S])
+        nc.sync.dma_start(bias[:, :, 0:E], b.rearrange("(h p) e -> p h e", p=P))
         for q in range(QUADRANTS):
             nc.sync.dma_start(w_plane[32 * q : 32 * q + 4].bitcast(I32), scale_rows[4 * q : 4 * q + 4].bitcast(I32))
         share = E * PASSES // WEIGHT_LOADS
@@ -112,142 +94,100 @@ def tile_moe_pre_lin_silu_kernel(tc, xT, w_words, w_scales, b, gate, offs, pos1,
         nc.sync.dma_start(pos1_sb[:], pos1)
         nc.sync.dma_start(pos2_sb[:], pos2)
 
-        def bank(i, shape):
-            return psum.tile(shape, F32, name="bank%d" % (i % BANKS))
+        def window(g, a, j):
+            e0, e1 = GROUPS[g]
+            return x_sb[(a, j)][:].indirect(offs_sb[:, e0 * C // LANES : e1 * C // LANES])
 
-        def gathered(a, c0, c1):
-            if a == 0:
-                return gathered0[:].rearrange("p (j s) -> p j s", j=PACK)[:, :, c0:c1]
-            if c0 < GROUP:
-                return gathered1[:, 1 : 1 + PACK, EARLY_AT + c0 : EARLY_AT + c1]
-            return gathered1[:, 0:PACK, c0 - GROUP : c1 - GROUP]
+        def by_pairs(g, a, c0, c1):
+            at = (a * (GROUPS[g][1] - GROUPS[g][0]) * C + c0) * PACK
+            into = rounded[g][:, at : at + (c1 - c0) * PACK].rearrange("p (c m j) -> p c j m", m=PAIR, j=PACK)
+            return into, gathered[(g, a)][:, :, c0:c1].rearrange("p j (c m) -> p c j m", m=PAIR)
 
-        def gather(a, j, c0, c1):
-            nc.vector.tensor_tensor(
-                gathered(a, c0, c1)[:, j, :],
-                x_sb[(a, j)][:].indirect(offs_sb[:, c0 // LANES : c1 // LANES]),
-                gate_sb[:, c0:c1],
-                MULT,
-            )
+        def weigh(g, a, c0, c1):
+            into, source = by_pairs(g, a, c0, c1)
+            at = (GROUPS[g][0] - OWN[1]) * C
+            weight = gate_rest[:, at + c0 : at + c1].rearrange("p (c o m) -> p c o m", o=1, m=PAIR)
+            nc.vector.tensor_tensor(into, source, weight.to_broadcast([P, (c1 - c0) // PAIR, PACK, PAIR]), MULT)
 
-        def turn(into, source, e0):
-            for i in range(TURNS):
-                nc.tensor.transpose(into[:, i, :], source[:, (e0 + i) * C : (e0 + i + 1) * C], identity[:])
-
-        def interleave(a, e0, e1):
-            at = PLACE[(a, e0)] * C * PACK
-            nc.scalar.copy(
-                rounded[:, at : at + (e1 - e0) * C * PACK].rearrange("p (c m j) -> p c j m", m=LINE, j=PACK),
-                gathered(a, e0 * C, e1 * C).rearrange("p j (c m) -> p c j m", m=LINE),
-            )
-
-        def quantise(call):
-            c0, c1 = PLACE[call[0]] * C, (PLACE[call[-1]] + 1) * C
+        def quantise(g, c0, c1):
             nc.vector.quantize_mx(
-                out=x_codes[:, c0:c1].bitcast(FP8X4), scales=x_plane[:, c0:c1], in_=rounded[:, PACK * c0 : PACK * c1]
+                out=x_codes[g][:, c0:c1].bitcast(FP8X4),
+                scales=x_plane[g][:, c0:c1],
+                in_=rounded[g][:, PACK * c0 : PACK * c1],
             )
 
-        def product(acc, e, h, a):
+        def product(acc, g, e, h, a):
+            e0, e1 = GROUPS[g]
             cols = slice(h * P, (h + 1) * P)
-            slots = slice(PLACE[(a, e)] * C, (PLACE[(a, e)] + 1) * C)
+            at = (a * (e1 - e0) + e - e0) * C
             nc.tensor.matmul_mx(
-                out=acc[:],
+                out=acc,
                 lhsT=w_codes[:, e * PASSES + a, cols].bitcast(FP8X4),
                 lhsT_scale=w_plane[:, e * PASSES + a, cols],
-                rhs=x_codes[:, slots].bitcast(FP8X4),
-                rhs_scale=x_plane[:, slots],
+                rhs=x_codes[g][:, at : at + C].bitcast(FP8X4),
+                rhs_scale=x_plane[g][:, at : at + C],
                 start=(a == 0),
                 stop=(a == PASSES - 1),
             )
 
-        lodgings = {
-            (1, 1): gathered1[:, 3, 0:1],
-            (0, 2): gathered1[:, 2, PIECE : PIECE + 1],
-            (1, 3): gathered1[:, 3, PIECE : PIECE + 1],
-            (1, 2): gathered1[:, PACK, EARLY_AT + 2 * C : EARLY_AT + 2 * C + 1],
-        }
-        halfway = gathered1[:, 2, 0:1]
-
         def activate(acc, e, h):
-            column = lodgings.get((h, e), bias[:, h, e : e + 1])
-            nc.scalar.activation(y[h][:, e * C : (e + 1) * C], acc[:], SILU, bias=column)
+            nc.scalar.activation(y[h][:, e * C : (e + 1) * C], acc, SILU, bias=bias[:, h, e : e + 1])
 
-        def expert(e, h, i):
-            acc = bank(i, [P, C])
+        def triple(g, e0, h, i):
+            acc = psum.tile([P, 3, C], F32, name="bank%d" % i)
+            for e in range(e0, e0 + 3):
+                for a in range(PASSES):
+                    product(acc[:, e - e0, :], g, e, h, a)
+            for e in range(e0, e0 + 3):
+                activate(acc[:, e - e0, :], e, h)
+
+        for g in (1, 2):
             for a in range(PASSES):
-                product(acc, e, h, a)
-            activate(acc, e, h)
+                for j in range(PACK):
+                    nc.scalar.activation(gathered[(g, a)][:, j, :], window(g, a, j), COPY)
 
-        nc.vector.tensor_copy(ungated[:], x_sb[(0, 0)][:].indirect(offs_sb[:]))
-        for i, e0 in enumerate(range(0, E, TURNS)):
-            turned = bank(i, [P, TURNS, P])
-            turn(turned, gate_sb, e0)
-            nc.scalar.copy(gate_by_slot[:, e0 : e0 + TURNS], turned[:, :, 0])
-        for i, e0 in enumerate(range(0, E, TURNS)):
-            turned = bank(3 + i, [P, TURNS, P])
-            turn(turned, ungated, e0)
-            for e in range(e0, e0 + TURNS):
-                nc.scalar.activation(
-                    gated_by_slot[:, e * C : (e + 1) * C], turned[:, e - e0, :], COPY, scale=gate_by_slot[:, e : e + 1]
-                )
-        for i, e0 in enumerate(range(0, E, TURNS)):
-            turned = bank(6 + i, [P, TURNS, P])
-            turn(turned, gated_by_slot, e0)
-            nc.scalar.copy(gathered(0, e0 * C, (e0 + TURNS) * C)[:, 0, :], turned[:].rearrange("p i s -> p (i s)"))
+        own = OWN[1] * C
+        for a in range(PASSES):
+            for j in range(PACK):
+                nc.vector.tensor_tensor(gathered[(0, a)][:, j, :], window(0, a, j), gate_own[:], MULT)
+            into, source = by_pairs(0, a, 0, own)
+            nc.vector.tensor_copy(into, source)
+        weigh(1, 0, 0, 768)
+        quantise(0, 0, 512)
+        quantise(0, 512, 768)
+        quantise(1, 0, 512)
+        quantise(1, 512, 768)
+        weigh(1, 1, 0, 384)
+        weigh(1, 1, 384, 768)
+        quantise(1, 768, 1152)
+        weigh(2, 0, 0, 384)
+        quantise(1, 1152, 1536)
+        weigh(2, 1, 0, 128)
+        quantise(2, 0, 384)
+        weigh(2, 1, 128, 256)
+        quantise(2, 384, 512)
+        weigh(2, 1, 256, 384)
+        quantise(2, 512, 640)
+        quantise(2, 640, 768)
 
-        for h, e in ((1, 1), (0, 2), (1, 3)):
-            nc.scalar.copy(lodgings[(h, e)], bias[:, h, e : e + 1])
-        nc.scalar.copy(halfway, bias[:, 1, 2:3])
-        for j in range(1, PACK):
-            gather(0, j, 0, S)
-        for e0, e1 in ((0, 4), (4, 8), (8, 11)):
-            interleave(0, e0, e1)
-        for j in range(PACK):
-            gather(1, j, 0, GROUP)
-        for e0 in range(0, FIRST_LATE, 2):
-            interleave(1, e0, e0 + 2)
-            if e0 == 2:
-                nc.scalar.copy(lodgings[(1, 2)], halfway)
-        for i, call in enumerate(EARLY_CALLS):
-            gather(1, i, GROUP, S)
-            quantise(call)
-            for n, (h, e) in enumerate((h, e) for h in range(HALVES) for e in (2 * i, 2 * i + 1)):
-                expert(e, h, 4 * i + n)
-            if i == 0:
-                interleave(0, E - 1, E)
-        idle = bank(BANKS - 1, [P, 4 * C])
-        for i in range(3):
-            nc.tensor.matmul_mx(
-                out=idle[:],
-                lhsT=w_codes[:, 0, 0:P].bitcast(FP8X4),
-                lhsT_scale=w_plane[:, 0, 0:P],
-                rhs=x_codes[:, 0 : 4 * C].bitcast(FP8X4),
-                rhs_scale=x_plane[:, 0 : 4 * C],
-                start=True,
-                stop=True,
-            )
-        for c0 in (GROUP, GROUP + GROUP // 2):
-            for j in (2, 3):
-                gather(1, j, c0, c0 + GROUP // 2)
-        for e in range(FIRST_LATE, E):
-            interleave(1, e, e + 1)
-        sums = {}
-        for call in LAST_CALLS:
-            quantise(call)
-            for a, e in sorted(call, key=lambda unit: ((1, unit[1]) not in call, unit[1], unit[0])):
-                if a == 0:
-                    sums[e] = bank(e - 4, [P, C])
-                product(sums[e], e, 0, a)
-                if a == 1:
-                    activate(sums[e], e, 0)
-        for e in range(4, E):
-            expert(e, 1, e - 4)
-
-        total = [ending.tile([P, T], F32, name="total%d" % h, offset=4 * T * h) for h in range(HALVES)]
+        for i, (g, e0) in enumerate(((0, 0), (1, 3), (1, 6))):
+            for h in range(HALVES):
+                triple(g, e0, h, 2 * i + h)
+        last = {}
+        for n, (h, e) in enumerate((h, e) for h in range(HALVES) for e in range(*LAST)):
+            last[(h, e)] = psum.tile([P, C], F32, name="bank%d" % ((6 + n) % BANKS))
+            product(last[(h, e)][:], 2, e, h, 0)
         for h in range(HALVES):
-            nc.vector.tensor_copy(first[h][:], y[h][:].indirect(pos1_sb[:]))
-        for h, t0, t1 in BACK:
+            for e in range(*LAST):
+                product(last[(h, e)][:], 2, e, h, 1)
+                activate(last[(h, e)][:], e, h)
+
+        nc.vector.tensor_copy(first[0][:, 0:OWN_TOKENS], y[0][:].indirect(pos1_sb[:, 0 : OWN_TOKENS // LANES]))
+        for h, t0, t1 in FETCHES:
+            nc.scalar.activation(first[h][:, t0:t1], y[h][:].indirect(pos1_sb[:, t0 // LANES : t1 // LANES]), COPY)
+        for h, t0, t1 in SUMS:
             nc.vector.tensor_tensor(
                 total[h][:, t0:t1], y[h][:].indirect(pos2_sb[:, t0 // LANES : t1 // LANES]), first[h][:, t0:t1], ADD
             )
+        for h, t0, t1 in STORES:
             nc.sync.dma_start(out[h * P : (h + 1) * P, t0:t1], total[h][:, t0:t1])

@@ -27,18 +27,22 @@ QUADRANTS = 4
 PAIR = 2
 ALIGN = 64
 BANKS = 8
-WINDOW = T + LANES
 
-OWN = (0, 3)
-MID = (3, 9)
-LAST = (9, 12)
-GROUPS = [OWN, MID, LAST]
+OWN = 3 * C
+REST = S - OWN
+WIDTHS = [OWN, REST]
+CUT = 704
+FETCHED = [[(0, REST)], [(0, CUT), (CUT, REST)]]
+WINDOWS = [REST + LANES, T + LANES]
 BIAS_COLUMNS = 16
-WEIGHT_LOADS = 3
+WEIGHT_LOADS = 2
 
-OWN_TOKENS = 192
-FETCHES = [(0, 192, 384), (0, 384, 768), (1, 0, 384), (1, 384, 768)]
-SUMS = [(0, 0, 192), (0, 192, 384), (0, 384, 768), (1, 0, 384), (1, 384, 640), (1, 640, 768)]
+TRIPLES = [[(e, h) for e in range(e0, e0 + 3)] for e0 in (0, 3) for h in range(HALVES)]
+EARLY_BANKS = TRIPLES + [[(6, 0), (7, 0), (6, 1), (7, 1)]]
+
+OWN_FETCHES = [(0, 128), (128, 256)]
+FETCHES = [(0, 256, 512), (0, 512, 768), (1, 0, 384), (1, 384, 640), (1, 640, 768)]
+SUMS = [(0, 0, 128), (0, 128, 512), (0, 512, 768), (1, 0, 384), (1, 384, 640), (1, 640, 768)]
 STORES = [(0, 0, 768), (1, 0, 384), (1, 384, 640), (1, 640, 768)]
 
 
@@ -51,16 +55,16 @@ def tile_moe_pre_lin_silu_kernel(tc, xT, w_words, w_scales, b, gate, offs, pos1,
         offs_sb = keep.tile([P, S // LANES], U16, name="offs_sb")
         pos1_sb = keep.tile([P, T // LANES], U16, name="pos1_sb")
         pos2_sb = keep.tile([P, T // LANES], U16, name="pos2_sb")
-        gate_own = keep.tile([P, OWN[1] * C], F32, name="gate_own")
-        gate_rest = keep.tile([P, S - OWN[1] * C], F32, name="gate_rest")
-        x_sb = {(a, j): keep.tile([P, WINDOW], F32, name="x%d%d" % (a, j)) for a in range(PASSES) for j in range(PACK)}
+        gate_own = keep.tile([P, OWN], F32, name="gate_own")
+        gate_rest = keep.tile([P, REST], F32, name="gate_rest")
+        x_sb = {(a, j): keep.tile([P, WINDOWS[a]], F32, name="x%d%d" % (a, j)) for a in range(PASSES) for j in range(PACK)}
         w_codes = keep.tile([P, E * PASSES, N], U32, name="w_codes", align_bytes=ALIGN)
         w_plane = keep.tile([P, E * PASSES, N], U8, name="w_plane", align_bytes=ALIGN)
         gathered, rounded, x_codes, x_plane = {}, {}, {}, {}
-        for g, (e0, e1) in enumerate(GROUPS):
-            width = (e1 - e0) * C
+        for g, width in enumerate(WIDTHS):
             for a in range(PASSES):
-                gathered[(g, a)] = keep.tile([P, PACK, width], F32, name="gathered%d%d" % (g, a), align_bytes=ALIGN)
+                for c0, c1 in FETCHED[a] if g else [(0, OWN)]:
+                    gathered[(g, a, c0)] = keep.tile([P, PACK, c1 - c0], F32, name="gathered%d%d_%d" % (g, a, c0))
             rounded[g] = keep.tile([P, PASSES * width * PACK], BF16, name="rounded%d" % g, align_bytes=ALIGN)
             x_codes[g] = keep.tile([P, PASSES * width], U32, name="x_codes%d" % g, align_bytes=ALIGN)
             x_plane[g] = keep.tile([P, PASSES * width], U8, name="x_plane%d" % g, align_bytes=ALIGN)
@@ -82,8 +86,8 @@ def tile_moe_pre_lin_silu_kernel(tc, xT, w_words, w_scales, b, gate, offs, pos1,
             nc.sync.dma_start(tile[:, 0:T], x_rows[a, j])
             if (a, j) == (0, 0):
                 nc.sync.dma_start(offs_sb[:], offs)
-                nc.sync.dma_start(gate_own[:], gate[0:P, 0 : OWN[1] * C])
-        nc.sync.dma_start(gate_rest[:], gate[0:P, OWN[1] * C : S])
+                nc.sync.dma_start(gate_own[:], gate[0:P, 0:OWN])
+        nc.sync.dma_start(gate_rest[:], gate[0:P, OWN:S])
         nc.sync.dma_start(bias[:, :, 0:E], b.rearrange("(h p) e -> p h e", p=P))
         for q in range(QUADRANTS):
             nc.sync.dma_start(w_plane[32 * q : 32 * q + 4].bitcast(I32), scale_rows[4 * q : 4 * q + 4].bitcast(I32))
@@ -94,19 +98,22 @@ def tile_moe_pre_lin_silu_kernel(tc, xT, w_words, w_scales, b, gate, offs, pos1,
         nc.sync.dma_start(pos1_sb[:], pos1)
         nc.sync.dma_start(pos2_sb[:], pos2)
 
-        def window(g, a, j):
-            e0, e1 = GROUPS[g]
-            return x_sb[(a, j)][:].indirect(offs_sb[:, e0 * C // LANES : e1 * C // LANES])
+        def window(a, j, s0, s1):
+            return x_sb[(a, j)][:].indirect(offs_sb[:, s0 // LANES : s1 // LANES])
 
         def by_pairs(g, a, c0, c1):
-            at = (a * (GROUPS[g][1] - GROUPS[g][0]) * C + c0) * PACK
+            at = (a * WIDTHS[g] + c0) * PACK
             into = rounded[g][:, at : at + (c1 - c0) * PACK].rearrange("p (c m j) -> p c j m", m=PAIR, j=PACK)
-            return into, gathered[(g, a)][:, :, c0:c1].rearrange("p j (c m) -> p c j m", m=PAIR)
+            base = max(start for gg, aa, start in gathered if (gg, aa) == (g, a) and start <= c0)
+            return into, gathered[(g, a, base)][:, :, c0 - base : c1 - base].rearrange("p j (c m) -> p c j m", m=PAIR)
 
-        def weigh(g, a, c0, c1):
-            into, source = by_pairs(g, a, c0, c1)
-            at = (GROUPS[g][0] - OWN[1]) * C
-            weight = gate_rest[:, at + c0 : at + c1].rearrange("p (c o m) -> p c o m", o=1, m=PAIR)
+        def interleave(a, c0, c1):
+            into, source = by_pairs(0, a, c0, c1)
+            nc.vector.tensor_copy(into, source)
+
+        def weigh(a, c0, c1):
+            into, source = by_pairs(1, a, c0, c1)
+            weight = gate_rest[:, c0:c1].rearrange("p (c o m) -> p c o m", o=1, m=PAIR)
             nc.vector.tensor_tensor(into, source, weight.to_broadcast([P, (c1 - c0) // PAIR, PACK, PAIR]), MULT)
 
         def quantise(g, c0, c1):
@@ -116,75 +123,73 @@ def tile_moe_pre_lin_silu_kernel(tc, xT, w_words, w_scales, b, gate, offs, pos1,
                 in_=rounded[g][:, PACK * c0 : PACK * c1],
             )
 
-        def product(acc, g, e, h, a):
-            e0, e1 = GROUPS[g]
-            cols = slice(h * P, (h + 1) * P)
-            at = (a * (e1 - e0) + e - e0) * C
-            nc.tensor.matmul_mx(
-                out=acc,
-                lhsT=w_codes[:, e * PASSES + a, cols].bitcast(FP8X4),
-                lhsT_scale=w_plane[:, e * PASSES + a, cols],
-                rhs=x_codes[g][:, at : at + C].bitcast(FP8X4),
-                rhs_scale=x_plane[g][:, at : at + C],
-                start=(a == 0),
-                stop=(a == PASSES - 1),
-            )
-
-        def activate(acc, e, h):
-            nc.scalar.activation(y[h][:, e * C : (e + 1) * C], acc, SILU, bias=bias[:, h, e : e + 1])
-
-        def triple(g, e0, h, i):
-            acc = psum.tile([P, 3, C], F32, name="bank%d" % i)
-            for e in range(e0, e0 + 3):
+        def bank(i, sums):
+            tile = psum.tile([P, len(sums), C], F32, name="bank%d" % i)
+            accs = {unit: tile[:, n, :] for n, unit in enumerate(sums)}
+            for (e, h), acc in accs.items():
+                g = 0 if e * C < OWN else 1
+                cols = slice(h * P, (h + 1) * P)
                 for a in range(PASSES):
-                    product(acc[:, e - e0, :], g, e, h, a)
-            for e in range(e0, e0 + 3):
-                activate(acc[:, e - e0, :], e, h)
+                    at = a * WIDTHS[g] + e * C - g * OWN
+                    nc.tensor.matmul_mx(
+                        out=acc,
+                        lhsT=w_codes[:, e * PASSES + a, cols].bitcast(FP8X4),
+                        lhsT_scale=w_plane[:, e * PASSES + a, cols],
+                        rhs=x_codes[g][:, at : at + C].bitcast(FP8X4),
+                        rhs_scale=x_plane[g][:, at : at + C],
+                        start=(a == 0),
+                        stop=(a == PASSES - 1),
+                    )
+            return accs
 
-        for g in (1, 2):
-            for a in range(PASSES):
+        def activate(accs, e, h):
+            nc.scalar.activation(y[h][:, e * C : (e + 1) * C], accs[(e, h)], SILU, bias=bias[:, h, e : e + 1])
+
+        def fetch(h, t0, t1):
+            nc.scalar.activation(first[h][:, t0:t1], y[h][:].indirect(pos1_sb[:, t0 // LANES : t1 // LANES]), COPY)
+
+        for a in range(PASSES):
+            for c0, c1 in FETCHED[a]:
                 for j in range(PACK):
-                    nc.scalar.activation(gathered[(g, a)][:, j, :], window(g, a, j), COPY)
+                    nc.scalar.activation(gathered[(1, a, c0)][:, j, :], window(a, j, OWN + c0, OWN + c1), COPY)
 
-        own = OWN[1] * C
         for a in range(PASSES):
             for j in range(PACK):
-                nc.vector.tensor_tensor(gathered[(0, a)][:, j, :], window(0, a, j), gate_own[:], MULT)
-            into, source = by_pairs(0, a, 0, own)
-            nc.vector.tensor_copy(into, source)
-        weigh(1, 0, 0, 768)
+                nc.vector.tensor_tensor(gathered[(0, a, 0)][:, j, :], window(a, j, 0, OWN), gate_own[:], MULT)
+            if a == 0:
+                interleave(0, 0, OWN)
+        interleave(1, 0, C)
+        interleave(1, C, OWN)
         quantise(0, 0, 512)
         quantise(0, 512, 768)
-        quantise(1, 0, 512)
-        quantise(1, 512, 768)
-        weigh(1, 1, 0, 384)
-        weigh(1, 1, 384, 768)
-        quantise(1, 768, 1152)
-        weigh(2, 0, 0, 384)
-        quantise(1, 1152, 1536)
-        weigh(2, 1, 0, 128)
-        quantise(2, 0, 384)
-        weigh(2, 1, 128, 256)
-        quantise(2, 384, 512)
-        weigh(2, 1, 256, 384)
-        quantise(2, 512, 640)
-        quantise(2, 640, 768)
+        weigh(0, 0, REST)
+        quantise(1, 0, 1024)
+        weigh(1, 0, CUT)
+        quantise(1, 1024, REST + 384)
+        quantise(1, REST + 384, REST + 640)
+        weigh(1, CUT, 896)
+        weigh(1, 896, 1024)
+        quantise(1, REST + 640, REST + 896)
+        weigh(1, 1024, REST)
+        quantise(1, REST + 896, REST + 1024)
+        quantise(1, REST + 1024, 2 * REST)
 
-        for i, (g, e0) in enumerate(((0, 0), (1, 3), (1, 6))):
-            for h in range(HALVES):
-                triple(g, e0, h, 2 * i + h)
-        last = {}
-        for n, (h, e) in enumerate((h, e) for h in range(HALVES) for e in range(*LAST)):
-            last[(h, e)] = psum.tile([P, C], F32, name="bank%d" % ((6 + n) % BANKS))
-            product(last[(h, e)][:], 2, e, h, 0)
-        for h in range(HALVES):
-            for e in range(*LAST):
-                product(last[(h, e)][:], 2, e, h, 1)
-                activate(last[(h, e)][:], e, h)
-
-        nc.vector.tensor_copy(first[0][:, 0:OWN_TOKENS], y[0][:].indirect(pos1_sb[:, 0 : OWN_TOKENS // LANES]))
+        for i, sums in enumerate(EARLY_BANKS):
+            accs = bank(i, sums)
+            for e, h in sums:
+                activate(accs, e, h)
+        accs = bank(5, [(8, 0), (9, 0), (8, 1), (9, 1)])
+        for e, h in accs:
+            activate(accs, e, h)
+        accs = bank(6, [(10, 0)])
+        accs.update(bank(7, [(11, 0)]))
+        accs.update(bank(0, [(10, 1), (11, 1)]))
+        for e, h in accs:
+            activate(accs, e, h)
+        for t0, t1 in OWN_FETCHES:
+            nc.vector.tensor_copy(first[0][:, t0:t1], y[0][:].indirect(pos1_sb[:, t0 // LANES : t1 // LANES]))
         for h, t0, t1 in FETCHES:
-            nc.scalar.activation(first[h][:, t0:t1], y[h][:].indirect(pos1_sb[:, t0 // LANES : t1 // LANES]), COPY)
+            fetch(h, t0, t1)
         for h, t0, t1 in SUMS:
             nc.vector.tensor_tensor(
                 total[h][:, t0:t1], y[h][:].indirect(pos2_sb[:, t0 // LANES : t1 // LANES]), first[h][:, t0:t1], ADD

@@ -1,6 +1,7 @@
 from contextlib import ExitStack
 
 import concourse.mybir as mybir
+from concourse.masks import make_identity
 
 K, T, E, C, N = 1024, 768, 12, 128, 256
 S = E * C
@@ -31,14 +32,14 @@ BANKS = 8
 OWN = 3 * C
 REST = S - OWN
 WIDTHS = [OWN, REST]
-CUT = 704
-FETCHED = [[(0, REST)], [(0, CUT), (CUT, REST)]]
-WINDOWS = [REST + LANES, T + LANES]
+PIECE = 3 * C
+FETCHED = [[(0, 2 * PIECE), (2 * PIECE, REST)], [(0, PIECE), (PIECE, 2 * PIECE), (2 * PIECE, REST)]]
+WINDOW = T + LANES
+OWN_BYTES = 2 * PASSES * OWN * PACK
 BIAS_COLUMNS = 16
 WEIGHT_LOADS = 2
 
-TRIPLES = [[(e, h) for e in range(e0, e0 + 3)] for e0 in (0, 3) for h in range(HALVES)]
-EARLY_BANKS = TRIPLES + [[(6, 0), (7, 0), (6, 1), (7, 1)]]
+EARLY_BANKS = [[(e, h) for e in range(e0, e0 + 4)] for e0 in (0, 4) for h in range(HALVES)]
 
 OWN_FETCHES = [(0, 128), (128, 256)]
 FETCHES = [(0, 256, 512), (0, 512, 768), (1, 0, 384), (1, 384, 640), (1, 640, 768)]
@@ -50,14 +51,17 @@ def tile_moe_pre_lin_silu_kernel(tc, xT, w_words, w_scales, b, gate, offs, pos1,
     nc = tc.nc
     with ExitStack() as ctx:
         keep = ctx.enter_context(tc.tile_pool(name="keep", bufs=1))
+        shared = ctx.enter_context(tc.tile_pool(name="shared", bufs=1))
         psum = ctx.enter_context(tc.psum_pool(name="psum", bufs=1))
 
         offs_sb = keep.tile([P, S // LANES], U16, name="offs_sb")
         pos1_sb = keep.tile([P, T // LANES], U16, name="pos1_sb")
         pos2_sb = keep.tile([P, T // LANES], U16, name="pos2_sb")
-        gate_own = keep.tile([P, OWN], F32, name="gate_own")
-        gate_rest = keep.tile([P, REST], F32, name="gate_rest")
-        x_sb = {(a, j): keep.tile([P, WINDOWS[a]], F32, name="x%d%d" % (a, j)) for a in range(PASSES) for j in range(PACK)}
+        gate_own = shared.tile([P, OWN], F32, name="gate_own", offset=OWN_BYTES - 2 * OWN, align_bytes=ALIGN)
+        gate_blocks = keep.tile([P, C], F32, name="gate_blocks")
+        gate_by_slot = keep.tile([P, E], F32, name="gate_by_slot")
+        identity = keep.tile([P, P], F32, name="identity")
+        x_sb = {(a, j): keep.tile([P, WINDOW], F32, name="x%d%d" % (a, j)) for a in range(PASSES) for j in range(PACK)}
         w_codes = keep.tile([P, E * PASSES, N], U32, name="w_codes", align_bytes=ALIGN)
         w_plane = keep.tile([P, E * PASSES, N], U8, name="w_plane", align_bytes=ALIGN)
         gathered, rounded, x_codes, x_plane = {}, {}, {}, {}
@@ -65,9 +69,17 @@ def tile_moe_pre_lin_silu_kernel(tc, xT, w_words, w_scales, b, gate, offs, pos1,
             for a in range(PASSES):
                 for c0, c1 in FETCHED[a] if g else [(0, OWN)]:
                     gathered[(g, a, c0)] = keep.tile([P, PACK, c1 - c0], F32, name="gathered%d%d_%d" % (g, a, c0))
-            rounded[g] = keep.tile([P, PASSES * width * PACK], BF16, name="rounded%d" % g, align_bytes=ALIGN)
             x_codes[g] = keep.tile([P, PASSES * width], U32, name="x_codes%d" % g, align_bytes=ALIGN)
             x_plane[g] = keep.tile([P, PASSES * width], U8, name="x_plane%d" % g, align_bytes=ALIGN)
+        rounded[(0, 0)] = shared.tile([P, PASSES * OWN * PACK], BF16, name="rounded_own", offset=0, align_bytes=ALIGN)
+        rounded[(1, 0)] = shared.tile([P, REST * PACK], BF16, name="rounded0", offset=OWN_BYTES, align_bytes=ALIGN)
+        rounded[(1, REST)] = shared.tile([P, PIECE * PACK], BF16, name="rounded1", offset=0, align_bytes=ALIGN)
+        rounded[(1, REST + PIECE)] = keep.tile([P, (REST - PIECE) * PACK], BF16, name="rounded2", align_bytes=ALIGN)
+
+        def rounded_at(g, c0, c1):
+            base = max(start for gg, start in rounded if gg == g and start <= c0)
+            return rounded[(g, base)][:, (c0 - base) * PACK : (c1 - base) * PACK]
+
         y = [keep.tile([P, S], F32, name="y%d" % h) for h in range(HALVES)]
         first = [keep.tile([P, T], F32, name="first%d" % h) for h in range(HALVES)]
         total = [keep.tile([P, T], F32, name="total%d" % h) for h in range(HALVES)]
@@ -77,6 +89,7 @@ def tile_moe_pre_lin_silu_kernel(tc, xT, w_words, w_scales, b, gate, offs, pos1,
         warm = keep.tile([P, 1], F32, name="warm")
         nc.gpsimd.memset(seed[:], 0.0)
         nc.scalar.activation(warm[:], seed[:], SILU)
+        make_identity(nc, identity[:])
         nc.vector.memset(w_plane[:].rearrange("p g n -> p (g n)").bitcast(I32), 0)
 
         x_rows = xT.rearrange("(a p j) t -> a j p t", a=PASSES, j=PACK)
@@ -87,7 +100,7 @@ def tile_moe_pre_lin_silu_kernel(tc, xT, w_words, w_scales, b, gate, offs, pos1,
             if (a, j) == (0, 0):
                 nc.sync.dma_start(offs_sb[:], offs)
                 nc.sync.dma_start(gate_own[:], gate[0:P, 0:OWN])
-        nc.sync.dma_start(gate_rest[:], gate[0:P, OWN:S])
+                nc.sync.dma_start(gate_blocks[:], gate.rearrange("r (m s) -> (r m) s", s=C)[0:P, :])
         nc.sync.dma_start(bias[:, :, 0:E], b.rearrange("(h p) e -> p h e", p=P))
         for q in range(QUADRANTS):
             nc.sync.dma_start(w_plane[32 * q : 32 * q + 4].bitcast(I32), scale_rows[4 * q : 4 * q + 4].bitcast(I32))
@@ -102,25 +115,36 @@ def tile_moe_pre_lin_silu_kernel(tc, xT, w_words, w_scales, b, gate, offs, pos1,
             return x_sb[(a, j)][:].indirect(offs_sb[:, s0 // LANES : s1 // LANES])
 
         def by_pairs(g, a, c0, c1):
-            at = (a * WIDTHS[g] + c0) * PACK
-            into = rounded[g][:, at : at + (c1 - c0) * PACK].rearrange("p (c m j) -> p c j m", m=PAIR, j=PACK)
+            at = a * WIDTHS[g]
+            into = rounded_at(g, at + c0, at + c1).rearrange("p (c m j) -> p c j m", m=PAIR, j=PACK)
             base = max(start for gg, aa, start in gathered if (gg, aa) == (g, a) and start <= c0)
             return into, gathered[(g, a, base)][:, :, c0 - base : c1 - base].rearrange("p j (c m) -> p c j m", m=PAIR)
 
         def interleave(a, c0, c1):
             into, source = by_pairs(0, a, c0, c1)
-            nc.vector.tensor_copy(into, source)
+            nc.gpsimd.tensor_scalar(into, source, 1.0, 0.0, MULT, ADD)
+
+        turned = psum.tile([P, P], F32, name="bank4")
+        nc.tensor.transpose(turned[:], gate_blocks[:], identity[:])
+        nc.vector.tensor_copy(gate_by_slot[:], turned[:, 0:E])
+        gate_rest = [psum.tile([P, PIECE], F32, name="bank%d" % (5 + i)) for i in range(REST // PIECE)]
+        for c0 in range(0, REST, C):
+            column = gate_by_slot[:, (OWN + c0) // C : (OWN + c0) // C + 1]
+            nc.tensor.transpose(
+                gate_rest[c0 // PIECE][:, c0 % PIECE : c0 % PIECE + C], column.to_broadcast([P, P]), identity[:]
+            )
 
         def weigh(a, c0, c1):
             into, source = by_pairs(1, a, c0, c1)
-            weight = gate_rest[:, c0:c1].rearrange("p (c o m) -> p c o m", o=1, m=PAIR)
+            at = c0 % PIECE
+            weight = gate_rest[c0 // PIECE][:, at : at + c1 - c0].rearrange("p (c o m) -> p c o m", o=1, m=PAIR)
             nc.vector.tensor_tensor(into, source, weight.to_broadcast([P, (c1 - c0) // PAIR, PACK, PAIR]), MULT)
 
         def quantise(g, c0, c1):
             nc.vector.quantize_mx(
                 out=x_codes[g][:, c0:c1].bitcast(FP8X4),
                 scales=x_plane[g][:, c0:c1],
-                in_=rounded[g][:, PACK * c0 : PACK * c1],
+                in_=rounded_at(g, c0, c1),
             )
 
         def bank(i, sums):
@@ -148,28 +172,31 @@ def tile_moe_pre_lin_silu_kernel(tc, xT, w_words, w_scales, b, gate, offs, pos1,
         def fetch(h, t0, t1):
             nc.scalar.activation(first[h][:, t0:t1], y[h][:].indirect(pos1_sb[:, t0 // LANES : t1 // LANES]), COPY)
 
+        nc.vector.tensor_copy(gathered[(1, 0, 2 * PIECE)][:, 0, :], window(0, 0, OWN + 2 * PIECE, S))
         for a in range(PASSES):
             for c0, c1 in FETCHED[a]:
                 for j in range(PACK):
-                    nc.scalar.activation(gathered[(1, a, c0)][:, j, :], window(a, j, OWN + c0, OWN + c1), COPY)
+                    if (a, c0, j) != (0, 2 * PIECE, 0):
+                        nc.scalar.activation(gathered[(1, a, c0)][:, j, :], window(a, j, OWN + c0, OWN + c1), COPY)
 
         for a in range(PASSES):
             for j in range(PACK):
                 nc.vector.tensor_tensor(gathered[(0, a, 0)][:, j, :], window(a, j, 0, OWN), gate_own[:], MULT)
-            if a == 0:
-                interleave(0, 0, OWN)
-        interleave(1, 0, C)
-        interleave(1, C, OWN)
+        for a in range(PASSES):
+            interleave(a, 0, OWN)
+        for c0 in range(0, REST, PIECE):
+            weigh(0, c0, c0 + PIECE)
         quantise(0, 0, 512)
         quantise(0, 512, 768)
-        weigh(0, 0, REST)
+        weigh(1, 0, PIECE)
         quantise(1, 0, 1024)
-        weigh(1, 0, CUT)
-        quantise(1, 1024, REST + 384)
-        quantise(1, REST + 384, REST + 640)
-        weigh(1, CUT, 896)
+        weigh(1, PIECE, 2 * PIECE)
+        quantise(1, 1024, REST)
+        quantise(1, REST, REST + PIECE)
+        quantise(1, REST + PIECE, REST + 2 * PIECE)
+        weigh(1, 768, 896)
         weigh(1, 896, 1024)
-        quantise(1, REST + 640, REST + 896)
+        quantise(1, REST + 768, REST + 896)
         weigh(1, 1024, REST)
         quantise(1, REST + 896, REST + 1024)
         quantise(1, REST + 1024, 2 * REST)
@@ -178,12 +205,12 @@ def tile_moe_pre_lin_silu_kernel(tc, xT, w_words, w_scales, b, gate, offs, pos1,
             accs = bank(i, sums)
             for e, h in sums:
                 activate(accs, e, h)
-        accs = bank(5, [(8, 0), (9, 0), (8, 1), (9, 1)])
+        accs = bank(4, [(8, 0), (8, 1), (9, 0), (9, 1)])
         for e, h in accs:
             activate(accs, e, h)
-        accs = bank(6, [(10, 0)])
-        accs.update(bank(7, [(11, 0)]))
-        accs.update(bank(0, [(10, 1), (11, 1)]))
+        accs = bank(0, [(10, 0)])
+        accs.update(bank(1, [(11, 0)]))
+        accs.update(bank(2, [(10, 1), (11, 1)]))
         for e, h in accs:
             activate(accs, e, h)
         for t0, t1 in OWN_FETCHES:

@@ -29,17 +29,18 @@ PAIR = 2
 ALIGN = 64
 BANKS = 8
 
-OWN = 3 * C
-REST = S - OWN
-WIDTHS = [OWN, REST]
+OWN = 448
+HEAD = 288
 PIECE = 3 * C
-FETCHED = [[(0, 2 * PIECE), (2 * PIECE, REST)], [(0, PIECE), (PIECE, 2 * PIECE), (2 * PIECE, REST)]]
-WINDOW = T + LANES
-OWN_BYTES = 2 * PASSES * OWN * PACK
+CUTS = [OWN, 2 * PIECE, 3 * PIECE, S]
+PIECES = list(zip(CUTS[:-1], CUTS[1:]))
+WINDOWS = [S - OWN + LANES, T + LANES]
 BIAS_COLUMNS = 16
 WEIGHT_LOADS = 2
 
-EARLY_BANKS = [[(e, h) for e in range(e0, e0 + 4)] for e0 in (0, 4) for h in range(HALVES)]
+EARLY_BANKS = [[(e, h) for e in range(4)] for h in range(HALVES)] + [
+    [(e, h) for e in (e0, e0 + 1) for h in range(HALVES)] for e0 in (4, 6, 8)
+]
 
 OWN_FETCHES = [(0, 128), (128, 256)]
 FETCHES = [(0, 256, 512), (0, 512, 768), (1, 0, 384), (1, 384, 640), (1, 640, 768)]
@@ -52,33 +53,43 @@ def tile_moe_pre_lin_silu_kernel(tc, xT, w_words, w_scales, b, gate, offs, pos1,
     with ExitStack() as ctx:
         keep = ctx.enter_context(tc.tile_pool(name="keep", bufs=1))
         shared = ctx.enter_context(tc.tile_pool(name="shared", bufs=1))
+        staged = ctx.enter_context(tc.tile_pool(name="staged", bufs=1))
         psum = ctx.enter_context(tc.psum_pool(name="psum", bufs=1))
 
         offs_sb = keep.tile([P, S // LANES], U16, name="offs_sb")
         pos1_sb = keep.tile([P, T // LANES], U16, name="pos1_sb")
         pos2_sb = keep.tile([P, T // LANES], U16, name="pos2_sb")
-        gate_own = shared.tile([P, OWN], F32, name="gate_own", offset=OWN_BYTES - 2 * OWN, align_bytes=ALIGN)
+        early_bytes = 2 * PACK * (S + CUTS[1])
+        gate_own = shared.tile([P, OWN], F32, name="gate_own", offset=early_bytes - 2 * OWN, align_bytes=ALIGN)
         gate_blocks = keep.tile([P, C], F32, name="gate_blocks")
         gate_by_slot = keep.tile([P, E], F32, name="gate_by_slot")
         identity = keep.tile([P, P], F32, name="identity")
-        x_sb = {(a, j): keep.tile([P, WINDOW], F32, name="x%d%d" % (a, j)) for a in range(PASSES) for j in range(PACK)}
+        x_sb = {(a, j): keep.tile([P, WINDOWS[a]], F32, name="x%d%d" % (a, j)) for a in range(PASSES) for j in range(PACK)}
         w_codes = keep.tile([P, E * PASSES, N], U32, name="w_codes", align_bytes=ALIGN)
         w_plane = keep.tile([P, E * PASSES, N], U8, name="w_plane", align_bytes=ALIGN)
-        gathered, rounded, x_codes, x_plane = {}, {}, {}, {}
-        for g, width in enumerate(WIDTHS):
-            for a in range(PASSES):
-                for c0, c1 in FETCHED[a] if g else [(0, OWN)]:
-                    gathered[(g, a, c0)] = keep.tile([P, PACK, c1 - c0], F32, name="gathered%d%d_%d" % (g, a, c0))
-            x_codes[g] = keep.tile([P, PASSES * width], U32, name="x_codes%d" % g, align_bytes=ALIGN)
-            x_plane[g] = keep.tile([P, PASSES * width], U8, name="x_plane%d" % g, align_bytes=ALIGN)
-        rounded[(0, 0)] = shared.tile([P, PASSES * OWN * PACK], BF16, name="rounded_own", offset=0, align_bytes=ALIGN)
-        rounded[(1, 0)] = shared.tile([P, REST * PACK], BF16, name="rounded0", offset=OWN_BYTES, align_bytes=ALIGN)
-        rounded[(1, REST)] = shared.tile([P, PIECE * PACK], BF16, name="rounded1", offset=0, align_bytes=ALIGN)
-        rounded[(1, REST + PIECE)] = keep.tile([P, (REST - PIECE) * PACK], BF16, name="rounded2", align_bytes=ALIGN)
+        gathered = {
+            (0, 0): staged.tile([P, PACK, OWN], F32, name="own0", offset=0),
+            (1, 0): keep.tile([P, PACK, OWN], F32, name="own1"),
+            (0, OWN): keep.tile([P, PACK, S - OWN], F32, name="rest0"),
+            (1, CUTS[0]): keep.tile([P, PACK, CUTS[1] - CUTS[0]], F32, name="rest1a"),
+            (1, CUTS[1]): shared.tile([P, PACK, PIECE], F32, name="rest1b", offset=early_bytes, align_bytes=ALIGN),
+            (1, CUTS[2]): staged.tile([P, PACK, PIECE], F32, name="rest1c", offset=0),
+        }
+        rounded = {
+            0: shared.tile([P, (S + CUTS[1]) * PACK], BF16, name="rounded_early", offset=0, align_bytes=ALIGN),
+            S + CUTS[1]: keep.tile([P, PIECE * PACK], BF16, name="rounded_mid", align_bytes=ALIGN),
+            S + CUTS[2]: shared.tile([P, PIECE * PACK], BF16, name="rounded_last", offset=0, align_bytes=ALIGN),
+        }
+        x_codes = keep.tile([P, PASSES * S], U32, name="x_codes", align_bytes=ALIGN)
+        x_plane = keep.tile([P, PASSES * S], U8, name="x_plane", align_bytes=ALIGN)
 
-        def rounded_at(g, c0, c1):
-            base = max(start for gg, start in rounded if gg == g and start <= c0)
-            return rounded[(g, base)][:, (c0 - base) * PACK : (c1 - base) * PACK]
+        def rounded_at(a, s0, s1):
+            base = max(start for start in rounded if start <= a * S + s0) - a * S
+            return rounded[base + a * S][:, (s0 - base) * PACK : (s1 - base) * PACK]
+
+        def gathered_at(a, s0, s1):
+            base = max(start for aa, start in gathered if aa == a and start <= s0)
+            return gathered[(a, base)][:, :, s0 - base : s1 - base]
 
         y = [keep.tile([P, S], F32, name="y%d" % h) for h in range(HALVES)]
         first = [keep.tile([P, T], F32, name="first%d" % h) for h in range(HALVES)]
@@ -114,53 +125,45 @@ def tile_moe_pre_lin_silu_kernel(tc, xT, w_words, w_scales, b, gate, offs, pos1,
         def window(a, j, s0, s1):
             return x_sb[(a, j)][:].indirect(offs_sb[:, s0 // LANES : s1 // LANES])
 
-        def by_pairs(g, a, c0, c1):
-            at = a * WIDTHS[g]
-            into = rounded_at(g, at + c0, at + c1).rearrange("p (c m j) -> p c j m", m=PAIR, j=PACK)
-            base = max(start for gg, aa, start in gathered if (gg, aa) == (g, a) and start <= c0)
-            return into, gathered[(g, a, base)][:, :, c0 - base : c1 - base].rearrange("p j (c m) -> p c j m", m=PAIR)
-
-        def interleave(a, c0, c1):
-            into, source = by_pairs(0, a, c0, c1)
-            nc.gpsimd.tensor_scalar(into, source, 1.0, 0.0, MULT, ADD)
+        def interleave(a):
+            into = rounded_at(a, 0, OWN).rearrange("p (c j) -> p c j", j=PACK)
+            nc.gpsimd.tensor_scalar(into, gathered_at(a, 0, OWN).rearrange("p j c -> p c j"), 1.0, 0.0, MULT, ADD)
 
         turned = psum.tile([P, P], F32, name="bank4")
         nc.tensor.transpose(turned[:], gate_blocks[:], identity[:])
         nc.vector.tensor_copy(gate_by_slot[:], turned[:, 0:E])
-        gate_rest = [psum.tile([P, PIECE], F32, name="bank%d" % (5 + i)) for i in range(REST // PIECE)]
-        for c0 in range(0, REST, C):
-            column = gate_by_slot[:, (OWN + c0) // C : (OWN + c0) // C + 1]
-            nc.tensor.transpose(
-                gate_rest[c0 // PIECE][:, c0 % PIECE : c0 % PIECE + C], column.to_broadcast([P, P]), identity[:]
-            )
+        gate_rest = {i: psum.tile([P, PIECE], F32, name="bank%d" % (4 + i)) for i in range(1, S // PIECE)}
+        for e in range(PIECE // C, E):
+            at = e * C % PIECE
+            column = gate_by_slot[:, e : e + 1].to_broadcast([P, P])
+            nc.tensor.transpose(gate_rest[e * C // PIECE][:, at : at + C], column, identity[:])
 
-        def weigh(a, c0, c1):
-            into, source = by_pairs(1, a, c0, c1)
-            at = c0 % PIECE
-            weight = gate_rest[c0 // PIECE][:, at : at + c1 - c0].rearrange("p (c o m) -> p c o m", o=1, m=PAIR)
-            nc.vector.tensor_tensor(into, source, weight.to_broadcast([P, (c1 - c0) // PAIR, PACK, PAIR]), MULT)
+        def weigh(a, s0, s1):
+            into = rounded_at(a, s0, s1).rearrange("p (c m j) -> p c j m", m=PAIR, j=PACK)
+            source = gathered_at(a, s0, s1).rearrange("p j (c m) -> p c j m", m=PAIR)
+            at = s0 % PIECE
+            weight = gate_rest[s0 // PIECE][:, at : at + s1 - s0].rearrange("p (c o m) -> p c o m", o=1, m=PAIR)
+            nc.vector.tensor_tensor(into, source, weight.to_broadcast([P, (s1 - s0) // PAIR, PACK, PAIR]), MULT)
 
-        def quantise(g, c0, c1):
+        def quantise(a, s0, s1):
+            cols = slice(a * S + s0, a * S + s1)
             nc.vector.quantize_mx(
-                out=x_codes[g][:, c0:c1].bitcast(FP8X4),
-                scales=x_plane[g][:, c0:c1],
-                in_=rounded_at(g, c0, c1),
+                out=x_codes[:, cols].bitcast(FP8X4), scales=x_plane[:, cols], in_=rounded_at(a, s0, s1)
             )
 
         def bank(i, sums):
             tile = psum.tile([P, len(sums), C], F32, name="bank%d" % i)
             accs = {unit: tile[:, n, :] for n, unit in enumerate(sums)}
             for (e, h), acc in accs.items():
-                g = 0 if e * C < OWN else 1
                 cols = slice(h * P, (h + 1) * P)
                 for a in range(PASSES):
-                    at = a * WIDTHS[g] + e * C - g * OWN
+                    slots = slice(a * S + e * C, a * S + (e + 1) * C)
                     nc.tensor.matmul_mx(
                         out=acc,
                         lhsT=w_codes[:, e * PASSES + a, cols].bitcast(FP8X4),
                         lhsT_scale=w_plane[:, e * PASSES + a, cols],
-                        rhs=x_codes[g][:, at : at + C].bitcast(FP8X4),
-                        rhs_scale=x_plane[g][:, at : at + C],
+                        rhs=x_codes[:, slots].bitcast(FP8X4),
+                        rhs_scale=x_plane[:, slots],
                         start=(a == 0),
                         stop=(a == PASSES - 1),
                     )
@@ -172,42 +175,41 @@ def tile_moe_pre_lin_silu_kernel(tc, xT, w_words, w_scales, b, gate, offs, pos1,
         def fetch(h, t0, t1):
             nc.scalar.activation(first[h][:, t0:t1], y[h][:].indirect(pos1_sb[:, t0 // LANES : t1 // LANES]), COPY)
 
-        nc.vector.tensor_copy(gathered[(1, 0, 2 * PIECE)][:, 0, :], window(0, 0, OWN + 2 * PIECE, S))
-        for a in range(PASSES):
-            for c0, c1 in FETCHED[a]:
-                for j in range(PACK):
-                    if (a, c0, j) != (0, 2 * PIECE, 0):
-                        nc.scalar.activation(gathered[(1, a, c0)][:, j, :], window(a, j, OWN + c0, OWN + c1), COPY)
+        def fetch_row(a, j, s0, s1):
+            nc.scalar.activation(gathered_at(a, s0, s1)[:, j, :], window(a, j, s0, s1), COPY)
+
+        nc.vector.tensor_copy(gathered_at(0, S - HEAD, S)[:, 0, :], window(0, 0, S - HEAD, S))
+        for j in range(PACK):
+            fetch_row(0, j, OWN, S - HEAD if j == 0 else S)
 
         for a in range(PASSES):
             for j in range(PACK):
-                nc.vector.tensor_tensor(gathered[(0, a, 0)][:, j, :], window(a, j, 0, OWN), gate_own[:], MULT)
+                nc.vector.tensor_tensor(gathered_at(a, 0, OWN)[:, j, :], window(a, j, 0, OWN), gate_own[:], MULT)
         for a in range(PASSES):
-            interleave(a, 0, OWN)
-        for c0 in range(0, REST, PIECE):
-            weigh(0, c0, c0 + PIECE)
+            interleave(a)
+        for s0, s1 in PIECES:
+            for j in range(PACK):
+                fetch_row(1, j, s0, s1)
+        for s0, s1 in PIECES:
+            weigh(0, s0, s1)
+        weigh(1, *PIECES[0])
         quantise(0, 0, 512)
-        quantise(0, 512, 768)
-        weigh(1, 0, PIECE)
-        quantise(1, 0, 1024)
-        weigh(1, PIECE, 2 * PIECE)
-        quantise(1, 1024, REST)
-        quantise(1, REST, REST + PIECE)
-        quantise(1, REST + PIECE, REST + 2 * PIECE)
-        weigh(1, 768, 896)
-        weigh(1, 896, 1024)
-        quantise(1, REST + 768, REST + 896)
-        weigh(1, 1024, REST)
-        quantise(1, REST + 896, REST + 1024)
-        quantise(1, REST + 1024, 2 * REST)
+        quantise(1, 0, 512)
+        weigh(1, *PIECES[1])
+        quantise(0, 512, S)
+        quantise(1, 512, CUTS[1])
+        quantise(1, *PIECES[1])
+        weigh(1, 9 * C, 10 * C)
+        weigh(1, 10 * C, 11 * C)
+        quantise(1, 9 * C, 10 * C)
+        weigh(1, 11 * C, S)
+        quantise(1, 10 * C, 11 * C)
+        quantise(1, 11 * C, S)
 
         for i, sums in enumerate(EARLY_BANKS):
             accs = bank(i, sums)
             for e, h in sums:
                 activate(accs, e, h)
-        accs = bank(4, [(8, 0), (8, 1), (9, 0), (9, 1)])
-        for e, h in accs:
-            activate(accs, e, h)
         accs = bank(0, [(10, 0)])
         accs.update(bank(1, [(11, 0)]))
         accs.update(bank(2, [(10, 1), (11, 1)]))

@@ -29,18 +29,15 @@ PAIR = 2
 ALIGN = 64
 BANKS = 8
 
-OWN = 448
-HEAD = 288
-PIECE = 3 * C
-CUTS = [OWN, 2 * PIECE, 3 * PIECE, S]
-PIECES = list(zip(CUTS[:-1], CUTS[1:]))
-WINDOWS = [S - OWN + LANES, T + LANES]
+QUAD = 4 * C
+OWN = [QUAD, 3 * C]
+HEAD = 3 * C
+CUTS = [OWN[1], 6 * C, 2 * QUAD, S]
+HELPED = [3, 8]
+WINDOWS = [S - OWN[0] + LANES, T + LANES]
 BIAS_COLUMNS = 16
 WEIGHT_LOADS = 2
-
-EARLY_BANKS = [[(e, h) for e in range(4)] for h in range(HALVES)] + [
-    [(e, h) for e in (e0, e0 + 1) for h in range(HALVES)] for e0 in (4, 6, 8)
-]
+EARLY = 5 * QUAD
 
 OWN_FETCHES = [(0, 128), (128, 256)]
 FETCHES = [(0, 256, 512), (0, 512, 768), (1, 0, 384), (1, 384, 640), (1, 640, 768)]
@@ -59,33 +56,42 @@ def tile_moe_pre_lin_silu_kernel(tc, xT, w_words, w_scales, b, gate, offs, pos1,
         offs_sb = keep.tile([P, S // LANES], U16, name="offs_sb")
         pos1_sb = keep.tile([P, T // LANES], U16, name="pos1_sb")
         pos2_sb = keep.tile([P, T // LANES], U16, name="pos2_sb")
-        early_bytes = 2 * PACK * (S + CUTS[1])
-        gate_own = shared.tile([P, OWN], F32, name="gate_own", offset=early_bytes - 2 * OWN, align_bytes=ALIGN)
-        gate_blocks = keep.tile([P, C], F32, name="gate_blocks")
+        early_bytes = 2 * PACK * EARLY
+        gate_own = shared.tile([P, QUAD], F32, name="gate_own", offset=early_bytes - 2 * QUAD, align_bytes=ALIGN)
+        gate_helped = keep.tile([P, len(HELPED), C], F32, name="gate_helped")
+        gate_blocks = staged.tile([P, C], F32, name="gate_blocks", offset=0, align_bytes=ALIGN)
         gate_by_slot = keep.tile([P, E], F32, name="gate_by_slot")
         identity = keep.tile([P, P], F32, name="identity")
         x_sb = {(a, j): keep.tile([P, WINDOWS[a]], F32, name="x%d%d" % (a, j)) for a in range(PASSES) for j in range(PACK)}
         w_codes = keep.tile([P, E * PASSES, N], U32, name="w_codes", align_bytes=ALIGN)
         w_plane = keep.tile([P, E * PASSES, N], U8, name="w_plane", align_bytes=ALIGN)
+        row_bytes = 4 * PACK
         gathered = {
-            (0, 0): staged.tile([P, PACK, OWN], F32, name="own0", offset=0),
-            (1, 0): keep.tile([P, PACK, OWN], F32, name="own1"),
-            (0, OWN): keep.tile([P, PACK, S - OWN], F32, name="rest0"),
+            (0, 0): staged.tile([P, PACK, OWN[0]], F32, name="own0", offset=row_bytes * OWN[1], align_bytes=ALIGN),
+            (1, 0): staged.tile([P, PACK, OWN[1]], F32, name="own1", offset=0, align_bytes=ALIGN),
+            (0, OWN[0]): keep.tile([P, PACK, S - OWN[0]], F32, name="rest0"),
             (1, CUTS[0]): keep.tile([P, PACK, CUTS[1] - CUTS[0]], F32, name="rest1a"),
-            (1, CUTS[1]): shared.tile([P, PACK, PIECE], F32, name="rest1b", offset=early_bytes, align_bytes=ALIGN),
-            (1, CUTS[2]): staged.tile([P, PACK, PIECE], F32, name="rest1c", offset=0),
+            (1, CUTS[1]): shared.tile(
+                [P, PACK, CUTS[2] - CUTS[1]], F32, name="rest1b", offset=early_bytes, align_bytes=ALIGN
+            ),
+            (1, CUTS[2]): staged.tile(
+                [P, PACK, S - CUTS[2]], F32, name="rest1c", offset=row_bytes * OWN[1], align_bytes=ALIGN
+            ),
         }
         rounded = {
-            0: shared.tile([P, (S + CUTS[1]) * PACK], BF16, name="rounded_early", offset=0, align_bytes=ALIGN),
-            S + CUTS[1]: keep.tile([P, PIECE * PACK], BF16, name="rounded_mid", align_bytes=ALIGN),
-            S + CUTS[2]: shared.tile([P, PIECE * PACK], BF16, name="rounded_last", offset=0, align_bytes=ALIGN),
+            0: shared.tile([P, EARLY * PACK], BF16, name="rounded_early", offset=0, align_bytes=ALIGN),
+            EARLY: staged.tile([P, QUAD * PACK], BF16, name="rounded_last", offset=0, align_bytes=ALIGN),
         }
         x_codes = keep.tile([P, PASSES * S], U32, name="x_codes", align_bytes=ALIGN)
         x_plane = keep.tile([P, PASSES * S], U8, name="x_plane", align_bytes=ALIGN)
 
+        def column(a, s):
+            return (PASSES * (s // QUAD) + a) * QUAD + s % QUAD
+
         def rounded_at(a, s0, s1):
-            base = max(start for start in rounded if start <= a * S + s0) - a * S
-            return rounded[base + a * S][:, (s0 - base) * PACK : (s1 - base) * PACK]
+            at = column(a, s0)
+            base = max(start for start in rounded if start <= at)
+            return rounded[base][:, (at - base) * PACK : (at - base + s1 - s0) * PACK]
 
         def gathered_at(a, s0, s1):
             base = max(start for aa, start in gathered if aa == a and start <= s0)
@@ -106,13 +112,15 @@ def tile_moe_pre_lin_silu_kernel(tc, xT, w_words, w_scales, b, gate, offs, pos1,
         x_rows = xT.rearrange("(a p j) t -> a j p t", a=PASSES, j=PACK)
         words = w_words.rearrange("e a p n r -> p (e a) (n r)")
         scale_rows = w_scales.rearrange("e a q n -> q (e a) n")
+        blocks = gate.rearrange("r (m s) -> r m s", s=C)
         for (a, j), tile in x_sb.items():
             nc.sync.dma_start(tile[:, 0:T], x_rows[a, j])
             if (a, j) == (0, 0):
                 nc.sync.dma_start(offs_sb[:], offs)
-                nc.sync.dma_start(gate_own[:], gate[0:P, 0:OWN])
+                nc.sync.dma_start(gate_own[:], gate[0:P, 0:QUAD])
                 nc.sync.dma_start(gate_blocks[:], gate.rearrange("r (m s) -> (r m) s", s=C)[0:P, :])
-        nc.sync.dma_start(bias[:, :, 0:E], b.rearrange("(h p) e -> p h e", p=P))
+        nc.sync.dma_start(gate_helped[:], blocks[0:P, HELPED[0] : E : HELPED[1] - HELPED[0], :])
+        nc.gpsimd.dma_start(bias[:, :, 0:E], b.rearrange("(h p) e -> p h e", p=P))
         for q in range(QUADRANTS):
             nc.sync.dma_start(w_plane[32 * q : 32 * q + 4].bitcast(I32), scale_rows[4 * q : 4 * q + 4].bitcast(I32))
         share = E * PASSES // WEIGHT_LOADS
@@ -126,46 +134,52 @@ def tile_moe_pre_lin_silu_kernel(tc, xT, w_words, w_scales, b, gate, offs, pos1,
             return x_sb[(a, j)][:].indirect(offs_sb[:, s0 // LANES : s1 // LANES])
 
         def interleave(a):
-            into = rounded_at(a, 0, OWN).rearrange("p (c j) -> p c j", j=PACK)
-            nc.gpsimd.tensor_scalar(into, gathered_at(a, 0, OWN).rearrange("p j c -> p c j"), 1.0, 0.0, MULT, ADD)
+            into = rounded_at(a, 0, OWN[a]).rearrange("p (c j) -> p c j", j=PACK)
+            nc.gpsimd.tensor_scalar(into, gathered_at(a, 0, OWN[a]).rearrange("p j c -> p c j"), 1.0, 0.0, MULT, ADD)
 
-        turned = psum.tile([P, P], F32, name="bank4")
+        def help_weigh(e):
+            into = rounded_at(1, e * C, (e + 1) * C).rearrange("p (c j) -> p c j", j=PACK)
+            weight = gate_helped[:, HELPED.index(e), :].rearrange("p (c o) -> p c o", o=1)
+            source = gathered_at(1, e * C, (e + 1) * C).rearrange("p j c -> p c j")
+            nc.gpsimd.tensor_tensor(into, source, weight.to_broadcast([P, C, PACK]), MULT)
+
+        turned = psum.tile([P, P], F32, name="bank5")
         nc.tensor.transpose(turned[:], gate_blocks[:], identity[:])
         nc.vector.tensor_copy(gate_by_slot[:], turned[:, 0:E])
-        gate_rest = {i: psum.tile([P, PIECE], F32, name="bank%d" % (4 + i)) for i in range(1, S // PIECE)}
-        for e in range(PIECE // C, E):
-            at = e * C % PIECE
-            column = gate_by_slot[:, e : e + 1].to_broadcast([P, P])
-            nc.tensor.transpose(gate_rest[e * C // PIECE][:, at : at + C], column, identity[:])
+        gate_rest = {q: psum.tile([P, QUAD], F32, name="bank%d" % (5 + q)) for q in range(1, S // QUAD)}
+        for e in range(QUAD // C, E):
+            at = e * C % QUAD
+            spread = gate_by_slot[:, e : e + 1].to_broadcast([P, P])
+            nc.tensor.transpose(gate_rest[e * C // QUAD][:, at : at + C], spread, identity[:])
 
         def weigh(a, s0, s1):
             into = rounded_at(a, s0, s1).rearrange("p (c m j) -> p c j m", m=PAIR, j=PACK)
             source = gathered_at(a, s0, s1).rearrange("p j (c m) -> p c j m", m=PAIR)
-            at = s0 % PIECE
-            weight = gate_rest[s0 // PIECE][:, at : at + s1 - s0].rearrange("p (c o m) -> p c o m", o=1, m=PAIR)
+            at = s0 % QUAD
+            weight = gate_rest[s0 // QUAD][:, at : at + s1 - s0].rearrange("p (c o m) -> p c o m", o=1, m=PAIR)
             nc.vector.tensor_tensor(into, source, weight.to_broadcast([P, (s1 - s0) // PAIR, PACK, PAIR]), MULT)
 
-        def quantise(a, s0, s1):
-            cols = slice(a * S + s0, a * S + s1)
+        def quantise(a, s0, width):
+            cols = slice(column(a, s0), column(a, s0) + width)
             nc.vector.quantize_mx(
-                out=x_codes[:, cols].bitcast(FP8X4), scales=x_plane[:, cols], in_=rounded_at(a, s0, s1)
+                out=x_codes[:, cols].bitcast(FP8X4), scales=x_plane[:, cols], in_=rounded_at(a, s0, s0 + width)
             )
 
         def bank(i, sums):
             tile = psum.tile([P, len(sums), C], F32, name="bank%d" % i)
             accs = {unit: tile[:, n, :] for n, unit in enumerate(sums)}
-            for (e, h), acc in accs.items():
-                cols = slice(h * P, (h + 1) * P)
-                for a in range(PASSES):
-                    slots = slice(a * S + e * C, a * S + (e + 1) * C)
+            for a in range(PASSES):
+                for n, (e, h) in enumerate(sums):
+                    cols = slice(h * P, (h + 1) * P)
+                    slots = slice(column(a, e * C), column(a, e * C) + C)
                     nc.tensor.matmul_mx(
-                        out=acc,
+                        out=accs[(e, h)],
                         lhsT=w_codes[:, e * PASSES + a, cols].bitcast(FP8X4),
                         lhsT_scale=w_plane[:, e * PASSES + a, cols],
                         rhs=x_codes[:, slots].bitcast(FP8X4),
                         rhs_scale=x_plane[:, slots],
-                        start=(a == 0),
-                        stop=(a == PASSES - 1),
+                        start=(a == 0 and n == 0),
+                        stop=(a == PASSES - 1 and n == len(sums) - 1),
                     )
             return accs
 
@@ -180,39 +194,42 @@ def tile_moe_pre_lin_silu_kernel(tc, xT, w_words, w_scales, b, gate, offs, pos1,
 
         nc.vector.tensor_copy(gathered_at(0, S - HEAD, S)[:, 0, :], window(0, 0, S - HEAD, S))
         for j in range(PACK):
-            fetch_row(0, j, OWN, S - HEAD if j == 0 else S)
+            fetch_row(0, j, OWN[0], S - HEAD if j == 0 else S)
 
         for a in range(PASSES):
             for j in range(PACK):
-                nc.vector.tensor_tensor(gathered_at(a, 0, OWN)[:, j, :], window(a, j, 0, OWN), gate_own[:], MULT)
+                nc.vector.tensor_tensor(
+                    gathered_at(a, 0, OWN[a])[:, j, :], window(a, j, 0, OWN[a]), gate_own[:, 0 : OWN[a]], MULT
+                )
         for a in range(PASSES):
             interleave(a)
-        for s0, s1 in PIECES:
+        for s0, s1 in zip(CUTS[:-1], CUTS[1:]):
             for j in range(PACK):
                 fetch_row(1, j, s0, s1)
-        for s0, s1 in PIECES:
-            weigh(0, s0, s1)
-        weigh(1, *PIECES[0])
-        quantise(0, 0, 512)
-        quantise(1, 0, 512)
-        weigh(1, *PIECES[1])
-        quantise(0, 512, S)
-        quantise(1, 512, CUTS[1])
-        quantise(1, *PIECES[1])
-        weigh(1, 9 * C, 10 * C)
-        weigh(1, 10 * C, 11 * C)
-        quantise(1, 9 * C, 10 * C)
+        help_weigh(HELPED[0])
+        weigh(0, QUAD, 2 * QUAD)
+        weigh(0, 2 * QUAD, S)
+        weigh(1, QUAD, CUTS[1])
+        weigh(1, CUTS[1], 2 * QUAD)
+        quantise(0, 0, QUAD)
+        quantise(1, 0, QUAD)
+        quantise(0, QUAD, 2 * QUAD)
+        quantise(0, 2 * QUAD, QUAD)
+        help_weigh(HELPED[1])
+        weigh(1, 9 * C, 11 * C)
         weigh(1, 11 * C, S)
-        quantise(1, 10 * C, 11 * C)
-        quantise(1, 11 * C, S)
+        quantise(1, 8 * C, 2 * C)
+        quantise(1, 10 * C, C)
+        quantise(1, 11 * C, C)
 
-        for i, sums in enumerate(EARLY_BANKS):
+        for i, sums in enumerate([(e, h) for e in range(e0, e0 + 4)] for e0 in (0, 4) for h in range(HALVES)):
             accs = bank(i, sums)
             for e, h in sums:
                 activate(accs, e, h)
-        accs = bank(0, [(10, 0)])
-        accs.update(bank(1, [(11, 0)]))
-        accs.update(bank(2, [(10, 1), (11, 1)]))
+        accs = bank(4, [(8, 0), (9, 0)])
+        accs.update(bank(5, [(10, 0)]))
+        accs.update(bank(0, [(11, 0)]))
+        accs.update(bank(1, [(e, 1) for e in range(8, E)]))
         for e, h in accs:
             activate(accs, e, h)
         for t0, t1 in OWN_FETCHES:

@@ -31,7 +31,7 @@ BANKS = 8
 
 QUAD = 4 * C
 OWN = [QUAD, 3 * C]
-HEAD = 3 * C
+HEAD = 5 * C
 CUTS = [OWN[1], 6 * C, 2 * QUAD, S]
 HELPED = [3, 8]
 WINDOWS = [S - OWN[0] + LANES, T + LANES]
@@ -117,6 +117,7 @@ def tile_moe_pre_lin_silu_kernel(tc, xT, w_words, w_scales, b, gate, offs, pos1,
             nc.sync.dma_start(tile[:, 0:T], x_rows[a, j])
             if (a, j) == (0, 0):
                 nc.sync.dma_start(offs_sb[:], offs)
+            if (a, j) == (0, 1):
                 nc.sync.dma_start(gate_own[:], gate[0:P, 0:QUAD])
                 nc.sync.dma_start(gate_blocks[:], gate.rearrange("r (m s) -> (r m) s", s=C)[0:P, :])
         nc.sync.dma_start(gate_helped[:], blocks[0:P, HELPED[0] : E : HELPED[1] - HELPED[0], :])

@@ -39,10 +39,10 @@ BIAS_COLUMNS = 16
 WEIGHT_LOADS = 2
 EARLY = 5 * QUAD
 
-OWN_FETCHES = [(0, 128), (128, 256)]
-FETCHES = [(0, 256, 512), (0, 512, 768), (1, 0, 384), (1, 384, 640), (1, 640, 768)]
-SUMS = [(0, 0, 128), (0, 128, 512), (0, 512, 768), (1, 0, 384), (1, 384, 640), (1, 640, 768)]
-STORES = [(0, 0, 768), (1, 0, 384), (1, 384, 640), (1, 640, 768)]
+OWN_FETCHES = [(0, 160), (160, 320)]
+FETCHES = [(0, 320, 544), (0, 544, 768), (1, 0, 256), (1, 256, 512), (1, 512, 768)]
+SUMS = [(0, 0, 160), (0, 160, 544), (0, 544, 768), (1, 0, 256), (1, 256, 512), (1, 512, 640), (1, 640, 768)]
+STORES = [(0, 0, 768), (1, 0, 512), (1, 512, 640), (1, 640, 768)]
 
 
 def tile_moe_pre_lin_silu_kernel(tc, xT, w_words, w_scales, b, gate, offs, pos1, pos2, out):

@@ -24,24 +24,24 @@ PACK = 4
 PASSES = K // (P * PACK)
 HALVES = N // P
 LANES = 16
-QUADRANTS = 4
+QUADRANT = 32
 PAIR = 2
 ALIGN = 64
-BANKS = 8
 
 QUAD = 4 * C
-OWN = [QUAD, 3 * C]
-HEAD = 5 * C
-CUTS = [OWN[1], 6 * C, 2 * QUAD, S]
-HELPED = [3, 8]
-WINDOWS = [S - OWN[0] + LANES, T + LANES]
+FUSED = 3 * C
+POOL_SHARE = 192
+POOL_END = QUAD + POOL_SHARE
+HEAD_END = QUAD + 2 * C
+PITCH = FUSED // 2
+WINDOWS = [2 * QUAD + LANES, T + LANES]
 BIAS_COLUMNS = 16
-WEIGHT_LOADS = 2
-EARLY = 5 * QUAD
+GATHERED_BYTES = 4 * PACK
+ROUNDED_BYTES = 2 * PACK
 
-OWN_FETCHES = [(0, 160), (160, 320)]
-FETCHES = [(0, 320, 544), (0, 544, 768), (1, 0, 256), (1, 256, 512), (1, 512, 768)]
-SUMS = [(0, 0, 160), (0, 160, 544), (0, 544, 768), (1, 0, 256), (1, 256, 512), (1, 512, 640), (1, 640, 768)]
+OWN_FETCHES = [(0, 128), (128, 256)]
+FETCHES = [(0, 256, 512), (0, 512, 768), (1, 0, 256), (1, 256, 512), (1, 512, 768)]
+SUMS = [(0, 0, 128), (0, 128, 512), (0, 512, 768), (1, 0, 256), (1, 256, 512), (1, 512, 640), (1, 640, 768)]
 STORES = [(0, 0, 768), (1, 0, 512), (1, 512, 640), (1, 640, 768)]
 
 
@@ -49,49 +49,52 @@ def tile_moe_pre_lin_silu_kernel(tc, xT, w_words, w_scales, b, gate, offs, pos1,
     nc = tc.nc
     with ExitStack() as ctx:
         keep = ctx.enter_context(tc.tile_pool(name="keep", bufs=1))
-        shared = ctx.enter_context(tc.tile_pool(name="shared", bufs=1))
-        staged = ctx.enter_context(tc.tile_pool(name="staged", bufs=1))
+        chain_a = ctx.enter_context(tc.tile_pool(name="chain_a", bufs=1))
+        chain_c = ctx.enter_context(tc.tile_pool(name="chain_c", bufs=1))
         psum = ctx.enter_context(tc.psum_pool(name="psum", bufs=1))
 
         offs_sb = keep.tile([P, S // LANES], U16, name="offs_sb")
         pos1_sb = keep.tile([P, T // LANES], U16, name="pos1_sb")
         pos2_sb = keep.tile([P, T // LANES], U16, name="pos2_sb")
-        early_bytes = 2 * PACK * EARLY
-        gate_own = shared.tile([P, QUAD], F32, name="gate_own", offset=early_bytes - 2 * QUAD, align_bytes=ALIGN)
-        gate_helped = keep.tile([P, len(HELPED), C], F32, name="gate_helped")
-        gate_blocks = staged.tile([P, C], F32, name="gate_blocks", offset=0, align_bytes=ALIGN)
+        gate_pool = keep.tile([P, POOL_END], F32, name="gate_pool")
+        gate_blocks = keep.tile([P, C], F32, name="gate_blocks")
         gate_by_slot = keep.tile([P, E], F32, name="gate_by_slot")
         identity = keep.tile([P, P], F32, name="identity")
         x_sb = {(a, j): keep.tile([P, WINDOWS[a]], F32, name="x%d%d" % (a, j)) for a in range(PASSES) for j in range(PACK)}
         w_codes = keep.tile([P, E * PASSES, N], U32, name="w_codes", align_bytes=ALIGN)
         w_plane = keep.tile([P, E * PASSES, N], U8, name="w_plane", align_bytes=ALIGN)
-        row_bytes = 4 * PACK
+
+        quad_bytes = GATHERED_BYTES * QUAD
+        expert3 = chain_a.tile(
+            [P, PACK * PITCH], F32, name="expert3", offset=quad_bytes - GATHERED_BYTES * C // 2, align_bytes=ALIGN
+        )
+        gate_fused = expert3[:, C : C + FUSED]
+        late_rows = keep.tile([P, PACK, 3 * QUAD - POOL_SHARE], F32, name="late_rows")
         gathered = {
-            (0, 0): staged.tile([P, PACK, OWN[0]], F32, name="own0", offset=row_bytes * OWN[1], align_bytes=ALIGN),
-            (1, 0): staged.tile([P, PACK, OWN[1]], F32, name="own1", offset=0, align_bytes=ALIGN),
-            (0, OWN[0]): keep.tile([P, PACK, S - OWN[0]], F32, name="rest0"),
-            (1, CUTS[0]): keep.tile([P, PACK, CUTS[1] - CUTS[0]], F32, name="rest1a"),
-            (1, CUTS[1]): shared.tile(
-                [P, PACK, CUTS[2] - CUTS[1]], F32, name="rest1b", offset=early_bytes, align_bytes=ALIGN
-            ),
-            (1, CUTS[2]): staged.tile(
-                [P, PACK, S - CUTS[2]], F32, name="rest1c", offset=row_bytes * OWN[1], align_bytes=ALIGN
-            ),
+            (0, 0): keep.tile([P, PACK, FUSED], F32, name="fused")[:],
+            (0, FUSED): expert3[:].rearrange("p (j c) -> p j c", j=PACK)[:, :, 0:C],
+            (0, QUAD): late_rows[:, :, QUAD - POOL_SHARE :],
+            (1, 0): chain_c.tile([P, PACK, QUAD], F32, name="quad0", offset=0, align_bytes=ALIGN)[:],
+            (1, QUAD): late_rows[:, :, 0:QUAD],
+            (1, 2 * QUAD): chain_c.tile([P, PACK, QUAD], F32, name="quad2", offset=quad_bytes, align_bytes=ALIGN)[:],
         }
+        rounded_quad0 = keep.tile([P, PASSES * QUAD * PACK], BF16, name="rounded_quad0", align_bytes=ALIGN)
         rounded = {
-            0: shared.tile([P, EARLY * PACK], BF16, name="rounded_early", offset=0, align_bytes=ALIGN),
-            EARLY: staged.tile([P, QUAD * PACK], BF16, name="rounded_last", offset=0, align_bytes=ALIGN),
+            (1, 0): rounded_quad0[:],
+            (0, 0): rounded_quad0[:, QUAD * PACK : 2 * QUAD * PACK],
+            (0, QUAD): chain_a.tile([P, 2 * QUAD * PACK], BF16, name="rounded_rest0", offset=0, align_bytes=ALIGN)[:],
+            (1, QUAD): chain_a.tile([P, QUAD * PACK], BF16, name="rounded_quad1", offset=0, align_bytes=ALIGN)[:],
+            (1, 2 * QUAD): keep.tile([P, QUAD * PACK], BF16, name="rounded_quad2", align_bytes=ALIGN)[:],
         }
-        x_codes = keep.tile([P, PASSES * S], U32, name="x_codes", align_bytes=ALIGN)
+        x_codes = chain_c.tile([P, PASSES * S], U32, name="x_codes", offset=quad_bytes // 4, align_bytes=ALIGN)
         x_plane = keep.tile([P, PASSES * S], U8, name="x_plane", align_bytes=ALIGN)
 
         def column(a, s):
-            return (PASSES * (s // QUAD) + a) * QUAD + s % QUAD
+            return (PASSES * (s // QUAD) + 1 - a) * QUAD + s % QUAD
 
         def rounded_at(a, s0, s1):
-            at = column(a, s0)
-            base = max(start for start in rounded if start <= at)
-            return rounded[base][:, (at - base) * PACK : (at - base + s1 - s0) * PACK]
+            base = max(start for aa, start in rounded if aa == a and start <= s0)
+            return rounded[(a, base)][:, (s0 - base) * PACK : (s1 - base) * PACK]
 
         def gathered_at(a, s0, s1):
             base = max(start for aa, start in gathered if aa == a and start <= s0)
@@ -112,21 +115,20 @@ def tile_moe_pre_lin_silu_kernel(tc, xT, w_words, w_scales, b, gate, offs, pos1,
         x_rows = xT.rearrange("(a p j) t -> a j p t", a=PASSES, j=PACK)
         words = w_words.rearrange("e a p n r -> p (e a) (n r)")
         scale_rows = w_scales.rearrange("e a q n -> q (e a) n")
-        blocks = gate.rearrange("r (m s) -> r m s", s=C)
         for (a, j), tile in x_sb.items():
             nc.sync.dma_start(tile[:, 0:T], x_rows[a, j])
             if (a, j) == (0, 0):
                 nc.sync.dma_start(offs_sb[:], offs)
-            if (a, j) == (0, 1):
-                nc.sync.dma_start(gate_own[:], gate[0:P, 0:QUAD])
+                nc.sync.dma_start(gate_fused, gate[0:P, 0:FUSED])
+            if (a, j) == (1, 2):
                 nc.sync.dma_start(gate_blocks[:], gate.rearrange("r (m s) -> (r m) s", s=C)[0:P, :])
-        nc.sync.dma_start(gate_helped[:], blocks[0:P, HELPED[0] : E : HELPED[1] - HELPED[0], :])
+            if (a, j) == (1, 1):
+                nc.sync.dma_start(gate_pool[:], gate[0:P, 0:POOL_END])
         nc.gpsimd.dma_start(bias[:, :, 0:E], b.rearrange("(h p) e -> p h e", p=P))
-        for q in range(QUADRANTS):
-            nc.sync.dma_start(w_plane[32 * q : 32 * q + 4].bitcast(I32), scale_rows[4 * q : 4 * q + 4].bitcast(I32))
-        share = E * PASSES // WEIGHT_LOADS
-        for g0 in range(0, E * PASSES, share):
-            g = slice(g0, g0 + share)
+        for r in range(PACK):
+            nc.sync.dma_start(w_plane[r:P:QUADRANT].bitcast(I32), scale_rows[r : 4 * PACK : PACK].bitcast(I32))
+        for e0, e1 in ((8, E), (0, 8)):
+            g = slice(e0 * PASSES, e1 * PASSES)
             nc.sync.dma_start(w_codes[:, g, :].bitcast(I32), words[:, g, :].bitcast(I32))
         nc.sync.dma_start(pos1_sb[:], pos1)
         nc.sync.dma_start(pos2_sb[:], pos2)
@@ -134,30 +136,23 @@ def tile_moe_pre_lin_silu_kernel(tc, xT, w_words, w_scales, b, gate, offs, pos1,
         def window(a, j, s0, s1):
             return x_sb[(a, j)][:].indirect(offs_sb[:, s0 // LANES : s1 // LANES])
 
-        def interleave(a):
-            into = rounded_at(a, 0, OWN[a]).rearrange("p (c j) -> p c j", j=PACK)
-            nc.gpsimd.tensor_scalar(into, gathered_at(a, 0, OWN[a]).rearrange("p j c -> p c j"), 1.0, 0.0, MULT, ADD)
+        def gather_on_vector(a, j, s0, s1):
+            nc.vector.tensor_copy(gathered_at(a, s0, s1)[:, j, :], window(a, j, s0, s1))
 
-        def help_weigh(e):
-            into = rounded_at(1, e * C, (e + 1) * C).rearrange("p (c j) -> p c j", j=PACK)
-            weight = gate_helped[:, HELPED.index(e), :].rearrange("p (c o) -> p c o", o=1)
-            source = gathered_at(1, e * C, (e + 1) * C).rearrange("p j c -> p c j")
-            nc.gpsimd.tensor_tensor(into, source, weight.to_broadcast([P, C, PACK]), MULT)
+        def gather_on_scalar(a, j, s0, s1):
+            nc.scalar.activation(gathered_at(a, s0, s1)[:, j, :], window(a, j, s0, s1), COPY)
 
-        turned = psum.tile([P, P], F32, name="bank5")
-        nc.tensor.transpose(turned[:], gate_blocks[:], identity[:])
-        nc.vector.tensor_copy(gate_by_slot[:], turned[:, 0:E])
-        gate_rest = {q: psum.tile([P, QUAD], F32, name="bank%d" % (5 + q)) for q in range(1, S // QUAD)}
-        for e in range(QUAD // C, E):
-            at = e * C % QUAD
-            spread = gate_by_slot[:, e : e + 1].to_broadcast([P, P])
-            nc.tensor.transpose(gate_rest[e * C // QUAD][:, at : at + C], spread, identity[:])
+        def weigh_on_gpsimd(a, s0, s1):
+            into = rounded_at(a, s0, s1).rearrange("p (c j) -> p c j", j=PACK)
+            weight = gate_pool[:, s0:s1].rearrange("p (c o) -> p c o", o=1)
+            source = gathered_at(a, s0, s1).rearrange("p j c -> p c j")
+            nc.gpsimd.tensor_tensor(into, source, weight.to_broadcast([P, s1 - s0, PACK]), MULT)
 
-        def weigh(a, s0, s1):
+        def weigh_on_vector(a, s0, s1):
             into = rounded_at(a, s0, s1).rearrange("p (c m j) -> p c j m", m=PAIR, j=PACK)
             source = gathered_at(a, s0, s1).rearrange("p j (c m) -> p c j m", m=PAIR)
             at = s0 % QUAD
-            weight = gate_rest[s0 // QUAD][:, at : at + s1 - s0].rearrange("p (c o m) -> p c o m", o=1, m=PAIR)
+            weight = gate_banks[s0 // QUAD][:, at : at + s1 - s0].rearrange("p (c o m) -> p c o m", o=1, m=PAIR)
             nc.vector.tensor_tensor(into, source, weight.to_broadcast([P, (s1 - s0) // PAIR, PACK, PAIR]), MULT)
 
         def quantise(a, s0, width):
@@ -190,52 +185,72 @@ def tile_moe_pre_lin_silu_kernel(tc, xT, w_words, w_scales, b, gate, offs, pos1,
         def fetch(h, t0, t1):
             nc.scalar.activation(first[h][:, t0:t1], y[h][:].indirect(pos1_sb[:, t0 // LANES : t1 // LANES]), COPY)
 
-        def fetch_row(a, j, s0, s1):
-            nc.scalar.activation(gathered_at(a, s0, s1)[:, j, :], window(a, j, s0, s1), COPY)
-
-        nc.vector.tensor_copy(gathered_at(0, S - HEAD, S)[:, 0, :], window(0, 0, S - HEAD, S))
+        gather_on_vector(0, 0, FUSED, QUAD)
+        gather_on_vector(0, 0, QUAD, HEAD_END)
         for j in range(PACK):
-            fetch_row(0, j, OWN[0], S - HEAD if j == 0 else S)
+            nc.vector.tensor_tensor(gathered_at(0, 0, FUSED)[:, j, :], window(0, j, 0, FUSED), gate_fused, MULT)
+        for j in (3, 1, 2):
+            gather_on_vector(0, j, FUSED, QUAD)
+        for j, s0, s1 in ((0, HEAD_END, S), (1, QUAD, S), (2, QUAD, S), (3, QUAD, POOL_END), (3, POOL_END, S)):
+            gather_on_scalar(0, j, s0, s1)
 
-        for a in range(PASSES):
-            for j in range(PACK):
-                nc.vector.tensor_tensor(
-                    gathered_at(a, 0, OWN[a])[:, j, :], window(a, j, 0, OWN[a]), gate_own[:, 0 : OWN[a]], MULT
-                )
-        for a in range(PASSES):
-            interleave(a)
-        for s0, s1 in zip(CUTS[:-1], CUTS[1:]):
-            for j in range(PACK):
-                fetch_row(1, j, s0, s1)
-        help_weigh(HELPED[0])
-        weigh(0, QUAD, 2 * QUAD)
-        weigh(0, 2 * QUAD, S)
-        weigh(1, QUAD, CUTS[1])
-        weigh(1, CUTS[1], 2 * QUAD)
-        quantise(0, 0, QUAD)
-        quantise(1, 0, QUAD)
-        quantise(0, QUAD, 2 * QUAD)
+        turned = psum.tile([P, P], F32, name="bank5")
+        nc.tensor.transpose(turned[:], gate_blocks[:], identity[:])
+        nc.vector.tensor_copy(gate_by_slot[:], turned[:, 0:E])
+        gate_banks = {q: psum.tile([P, QUAD], F32, name="bank%d" % (5 + q)) for q in range(1, S // QUAD)}
+        for e in range(QUAD // C + 1, E):
+            at = e * C % QUAD
+            spread = gate_by_slot[:, e : e + 1].to_broadcast([P, P])
+            nc.tensor.transpose(gate_banks[e * C // QUAD][:, at : at + C], spread, identity[:])
+
+        for j in range(PACK):
+            gather_on_vector(1, j, 0, QUAD)
+        for j in range(PACK):
+            gather_on_scalar(1, j, 2 * QUAD, S)
+        nc.gpsimd.tensor_scalar(
+            rounded_at(0, 0, FUSED).rearrange("p (c j) -> p c j", j=PACK),
+            gathered_at(0, 0, FUSED).rearrange("p j c -> p c j"),
+            1.0,
+            0.0,
+            MULT,
+            ADD,
+        )
+        weigh_on_gpsimd(0, FUSED, QUAD)
+        weigh_on_gpsimd(0, QUAD, POOL_END)
+        weigh_on_gpsimd(1, 0, QUAD)
+        weigh_on_vector(0, POOL_END, 2 * QUAD)
+        weigh_on_vector(0, 2 * QUAD, S)
+        for j in range(PACK):
+            gather_on_scalar(1, j, QUAD, 2 * QUAD)
+        weigh_on_vector(1, 2 * QUAD, S)
         quantise(0, 2 * QUAD, QUAD)
-        help_weigh(HELPED[1])
-        weigh(1, 9 * C, 11 * C)
-        weigh(1, 11 * C, S)
-        quantise(1, 8 * C, 2 * C)
-        quantise(1, 10 * C, C)
-        quantise(1, 11 * C, C)
+        quantise(1, 2 * QUAD, QUAD)
+        quantise(1, 0, 2 * QUAD)
+        quantise(0, QUAD, QUAD)
+        weigh_on_gpsimd(1, 4 * C, 5 * C)
+        weigh_on_vector(1, 5 * C, 7 * C)
+        weigh_on_vector(1, 7 * C, 8 * C)
+        quantise(1, 4 * C, 2 * C)
+        quantise(1, 6 * C, C)
+        quantise(1, 7 * C, C)
 
-        for i, sums in enumerate([(e, h) for e in range(e0, e0 + 4)] for e0 in (0, 4) for h in range(HALVES)):
+        for i, sums in enumerate([(e, h) for e in range(e0, e0 + 4)] for e0 in (8, 0) for h in range(HALVES)):
             accs = bank(i, sums)
             for e, h in sums:
                 activate(accs, e, h)
-        accs = bank(4, [(8, 0), (9, 0)])
-        accs.update(bank(5, [(10, 0)]))
-        accs.update(bank(0, [(11, 0)]))
-        accs.update(bank(1, [(e, 1) for e in range(8, E)]))
-        for e, h in accs:
-            activate(accs, e, h)
+        accs = bank(4, [(4, 0), (5, 0)])
+        accs.update(bank(5, [(6, 0)]))
+        accs.update(bank(0, [(7, 0)]))
+        accs.update(bank(1, [(e, 1) for e in range(4, 8)]))
+        for e in range(4, 8):
+            activate(accs, e, 0)
+        activate(accs, 4, 1)
         for t0, t1 in OWN_FETCHES:
             nc.vector.tensor_copy(first[0][:, t0:t1], y[0][:].indirect(pos1_sb[:, t0 // LANES : t1 // LANES]))
-        for h, t0, t1 in FETCHES:
+        fetch(*FETCHES[0])
+        for e in range(5, 8):
+            activate(accs, e, 1)
+        for h, t0, t1 in FETCHES[1:]:
             fetch(h, t0, t1)
         for h, t0, t1 in SUMS:
             nc.vector.tensor_tensor(

@@ -29,15 +29,10 @@ PAIR = 2
 ALIGN = 64
 
 QUAD = 4 * C
-FUSED = 3 * C
-POOL_SHARE = 192
-POOL_END = QUAD + POOL_SHARE
+POOL_END = QUAD + C
 HEAD_END = QUAD + 2 * C
-PITCH = FUSED // 2
 WINDOWS = [2 * QUAD + LANES, T + LANES]
 BIAS_COLUMNS = 16
-GATHERED_BYTES = 4 * PACK
-ROUNDED_BYTES = 2 * PACK
 
 OWN_FETCHES = [(0, 128), (128, 256)]
 FETCHES = [(0, 256, 512), (0, 512, 768), (1, 0, 256), (1, 256, 512), (1, 512, 768)]
@@ -50,43 +45,37 @@ def tile_moe_pre_lin_silu_kernel(tc, xT, w_words, w_scales, b, gate, offs, pos1,
     with ExitStack() as ctx:
         keep = ctx.enter_context(tc.tile_pool(name="keep", bufs=1))
         chain_a = ctx.enter_context(tc.tile_pool(name="chain_a", bufs=1))
+        chain_b = ctx.enter_context(tc.tile_pool(name="chain_b", bufs=1))
         chain_c = ctx.enter_context(tc.tile_pool(name="chain_c", bufs=1))
         psum = ctx.enter_context(tc.psum_pool(name="psum", bufs=1))
 
         offs_sb = keep.tile([P, S // LANES], U16, name="offs_sb")
         pos1_sb = keep.tile([P, T // LANES], U16, name="pos1_sb")
         pos2_sb = keep.tile([P, T // LANES], U16, name="pos2_sb")
-        gate_pool = keep.tile([P, POOL_END], F32, name="gate_pool")
+        gate_rows = {0: keep.tile([P, QUAD], F32, name="gate_quad0"), QUAD: keep.tile([P, C], F32, name="gate_expert4")}
         gate_blocks = keep.tile([P, C], F32, name="gate_blocks")
-        gate_by_slot = keep.tile([P, E], F32, name="gate_by_slot")
+        gate_by_slot = chain_b.tile([P, E], F32, name="gate_by_slot", offset=0, align_bytes=ALIGN)
         identity = keep.tile([P, P], F32, name="identity")
         x_sb = {(a, j): keep.tile([P, WINDOWS[a]], F32, name="x%d%d" % (a, j)) for a in range(PASSES) for j in range(PACK)}
         w_codes = keep.tile([P, E * PASSES, N], U32, name="w_codes", align_bytes=ALIGN)
         w_plane = keep.tile([P, E * PASSES, N], U8, name="w_plane", align_bytes=ALIGN)
 
-        quad_bytes = GATHERED_BYTES * QUAD
-        expert3 = chain_a.tile(
-            [P, PACK * PITCH], F32, name="expert3", offset=quad_bytes - GATHERED_BYTES * C // 2, align_bytes=ALIGN
-        )
-        gate_fused = expert3[:, C : C + FUSED]
-        late_rows = keep.tile([P, PACK, 3 * QUAD - POOL_SHARE], F32, name="late_rows")
         gathered = {
-            (0, 0): keep.tile([P, PACK, FUSED], F32, name="fused")[:],
-            (0, FUSED): expert3[:].rearrange("p (j c) -> p j c", j=PACK)[:, :, 0:C],
-            (0, QUAD): late_rows[:, :, QUAD - POOL_SHARE :],
+            (0, 0): keep.tile([P, PACK, QUAD], F32, name="fused")[:],
+            (0, QUAD): keep.tile([P, PACK, 2 * QUAD], F32, name="rest0")[:],
             (1, 0): chain_c.tile([P, PACK, QUAD], F32, name="quad0", offset=0, align_bytes=ALIGN)[:],
-            (1, QUAD): late_rows[:, :, 0:QUAD],
-            (1, 2 * QUAD): chain_c.tile([P, PACK, QUAD], F32, name="quad2", offset=quad_bytes, align_bytes=ALIGN)[:],
+            (1, QUAD): chain_b.tile([P, PACK, QUAD], F32, name="quad1", offset=0, align_bytes=ALIGN)[:],
+            (1, 2 * QUAD): keep.tile([P, PACK, QUAD], F32, name="quad2")[:],
         }
-        rounded_quad0 = keep.tile([P, PASSES * QUAD * PACK], BF16, name="rounded_quad0", align_bytes=ALIGN)
+        rounded_quad0 = chain_a.tile([P, PASSES * QUAD * PACK], BF16, name="rounded_quad0", offset=0, align_bytes=ALIGN)
         rounded = {
             (1, 0): rounded_quad0[:],
             (0, 0): rounded_quad0[:, QUAD * PACK : 2 * QUAD * PACK],
-            (0, QUAD): chain_a.tile([P, 2 * QUAD * PACK], BF16, name="rounded_rest0", offset=0, align_bytes=ALIGN)[:],
+            (0, QUAD): keep.tile([P, 2 * QUAD * PACK], BF16, name="rounded_rest0", align_bytes=ALIGN)[:],
             (1, QUAD): chain_a.tile([P, QUAD * PACK], BF16, name="rounded_quad1", offset=0, align_bytes=ALIGN)[:],
             (1, 2 * QUAD): keep.tile([P, QUAD * PACK], BF16, name="rounded_quad2", align_bytes=ALIGN)[:],
         }
-        x_codes = chain_c.tile([P, PASSES * S], U32, name="x_codes", offset=quad_bytes // 4, align_bytes=ALIGN)
+        x_codes = chain_c.tile([P, PASSES * S], U32, name="x_codes", offset=0, align_bytes=ALIGN)
         x_plane = keep.tile([P, PASSES * S], U8, name="x_plane", align_bytes=ALIGN)
 
         def column(a, s):
@@ -119,11 +108,11 @@ def tile_moe_pre_lin_silu_kernel(tc, xT, w_words, w_scales, b, gate, offs, pos1,
             nc.sync.dma_start(tile[:, 0:T], x_rows[a, j])
             if (a, j) == (0, 0):
                 nc.sync.dma_start(offs_sb[:], offs)
-                nc.sync.dma_start(gate_fused, gate[0:P, 0:FUSED])
+                nc.sync.dma_start(gate_rows[0][:], gate[0:P, 0:QUAD])
             if (a, j) == (1, 2):
                 nc.sync.dma_start(gate_blocks[:], gate.rearrange("r (m s) -> (r m) s", s=C)[0:P, :])
             if (a, j) == (1, 1):
-                nc.sync.dma_start(gate_pool[:], gate[0:P, 0:POOL_END])
+                nc.sync.dma_start(gate_rows[QUAD][:], gate[0:P, QUAD:POOL_END])
         nc.gpsimd.dma_start(bias[:, :, 0:E], b.rearrange("(h p) e -> p h e", p=P))
         for r in range(PACK):
             nc.sync.dma_start(w_plane[r:P:QUADRANT].bitcast(I32), scale_rows[r : 4 * PACK : PACK].bitcast(I32))
@@ -144,7 +133,7 @@ def tile_moe_pre_lin_silu_kernel(tc, xT, w_words, w_scales, b, gate, offs, pos1,
 
         def weigh_on_gpsimd(a, s0, s1):
             into = rounded_at(a, s0, s1).rearrange("p (c j) -> p c j", j=PACK)
-            weight = gate_pool[:, s0:s1].rearrange("p (c o) -> p c o", o=1)
+            weight = gate_rows[s0][:].rearrange("p (c o) -> p c o", o=1)
             source = gathered_at(a, s0, s1).rearrange("p j c -> p c j")
             nc.gpsimd.tensor_tensor(into, source, weight.to_broadcast([P, s1 - s0, PACK]), MULT)
 
@@ -185,12 +174,9 @@ def tile_moe_pre_lin_silu_kernel(tc, xT, w_words, w_scales, b, gate, offs, pos1,
         def fetch(h, t0, t1):
             nc.scalar.activation(first[h][:, t0:t1], y[h][:].indirect(pos1_sb[:, t0 // LANES : t1 // LANES]), COPY)
 
-        gather_on_vector(0, 0, FUSED, QUAD)
         gather_on_vector(0, 0, QUAD, HEAD_END)
         for j in range(PACK):
-            nc.vector.tensor_tensor(gathered_at(0, 0, FUSED)[:, j, :], window(0, j, 0, FUSED), gate_fused, MULT)
-        for j in (3, 1, 2):
-            gather_on_vector(0, j, FUSED, QUAD)
+            nc.vector.tensor_tensor(gathered_at(0, 0, QUAD)[:, j, :], window(0, j, 0, QUAD), gate_rows[0][:], MULT)
         for j, s0, s1 in ((0, HEAD_END, S), (1, QUAD, S), (2, QUAD, S), (3, QUAD, POOL_END), (3, POOL_END, S)):
             gather_on_scalar(0, j, s0, s1)
 
@@ -208,14 +194,13 @@ def tile_moe_pre_lin_silu_kernel(tc, xT, w_words, w_scales, b, gate, offs, pos1,
         for j in range(PACK):
             gather_on_scalar(1, j, 2 * QUAD, S)
         nc.gpsimd.tensor_scalar(
-            rounded_at(0, 0, FUSED).rearrange("p (c j) -> p c j", j=PACK),
-            gathered_at(0, 0, FUSED).rearrange("p j c -> p c j"),
+            rounded_at(0, 0, QUAD).rearrange("p (c j) -> p c j", j=PACK),
+            gathered_at(0, 0, QUAD).rearrange("p j c -> p c j"),
             1.0,
             0.0,
             MULT,
             ADD,
         )
-        weigh_on_gpsimd(0, FUSED, QUAD)
         weigh_on_gpsimd(0, QUAD, POOL_END)
         weigh_on_gpsimd(1, 0, QUAD)
         weigh_on_vector(0, POOL_END, 2 * QUAD)

from contextlib import ExitStack

import concourse.mybir as mybir
from concourse.masks import make_identity

K, T, E, C, N = 1024, 768, 12, 128, 256
S = E * C
FLOPS = 2 * K * N * S

F32 = mybir.dt.float32
BF16 = mybir.dt.bfloat16
I32 = mybir.dt.int32
U32 = mybir.dt.uint32
U16 = mybir.dt.uint16
U8 = mybir.dt.uint8
FP8X4 = mybir.dt.float8_e4m3fn_x4
MULT = mybir.AluOpType.mult
ADD = mybir.AluOpType.add
COPY = mybir.ActivationFunctionType.Copy
SILU = mybir.ActivationFunctionType.Silu

P = 128
PACK = 4
PASSES = K // (P * PACK)
HALVES = N // P
LANES = 16
QUADRANT = 32
PAIR = 2
ALIGN = 64

QUAD = 4 * C
POOL_END = QUAD + C
HEAD_END = QUAD + 2 * C
WINDOWS = [2 * QUAD + LANES, T + LANES]
BIAS_COLUMNS = 16

OWN_FETCHES = [(0, 128), (128, 256)]
FETCHES = [(0, 256, 512), (0, 512, 768), (1, 0, 256), (1, 256, 512), (1, 512, 768)]
SUMS = [(0, 0, 128), (0, 128, 512), (0, 512, 768), (1, 0, 256), (1, 256, 512), (1, 512, 640), (1, 640, 768)]
STORES = [(0, 0, 768), (1, 0, 512), (1, 512, 640), (1, 640, 768)]


def tile_moe_pre_lin_silu_kernel(tc, xT, w_words, w_scales, b, gate, offs, pos1, pos2, out):
    nc = tc.nc
    with ExitStack() as ctx:
        keep = ctx.enter_context(tc.tile_pool(name="keep", bufs=1))
        chain_a = ctx.enter_context(tc.tile_pool(name="chain_a", bufs=1))
        chain_b = ctx.enter_context(tc.tile_pool(name="chain_b", bufs=1))
        chain_c = ctx.enter_context(tc.tile_pool(name="chain_c", bufs=1))
        psum = ctx.enter_context(tc.psum_pool(name="psum", bufs=1))

        offs_sb = keep.tile([P, S // LANES], U16, name="offs_sb")
        pos1_sb = keep.tile([P, T // LANES], U16, name="pos1_sb")
        pos2_sb = keep.tile([P, T // LANES], U16, name="pos2_sb")
        gate_rows = {0: keep.tile([P, QUAD], F32, name="gate_quad0"), QUAD: keep.tile([P, C], F32, name="gate_expert4")}
        gate_blocks = keep.tile([P, C], F32, name="gate_blocks")
        gate_by_slot = chain_b.tile([P, E], F32, name="gate_by_slot", offset=0, align_bytes=ALIGN)
        identity = keep.tile([P, P], F32, name="identity")
        x_sb = {(a, j): keep.tile([P, WINDOWS[a]], F32, name="x%d%d" % (a, j)) for a in range(PASSES) for j in range(PACK)}
        w_codes = keep.tile([P, E * PASSES, N], U32, name="w_codes", align_bytes=ALIGN)
        w_plane = keep.tile([P, E * PASSES, N], U8, name="w_plane", align_bytes=ALIGN)

        gathered = {
            (0, 0): keep.tile([P, PACK, QUAD], F32, name="fused")[:],
            (0, QUAD): keep.tile([P, PACK, 2 * QUAD], F32, name="rest0")[:],
            (1, 0): chain_c.tile([P, PACK, QUAD], F32, name="quad0", offset=0, align_bytes=ALIGN)[:],
            (1, QUAD): chain_b.tile([P, PACK, QUAD], F32, name="quad1", offset=0, align_bytes=ALIGN)[:],
            (1, 2 * QUAD): keep.tile([P, PACK, QUAD], F32, name="quad2")[:],
        }
        rounded_quad0 = chain_a.tile([P, PASSES * QUAD * PACK], BF16, name="rounded_quad0", offset=0, align_bytes=ALIGN)
        rounded = {
            (1, 0): rounded_quad0[:],
            (0, 0): rounded_quad0[:, QUAD * PACK : 2 * QUAD * PACK],
            (0, QUAD): keep.tile([P, 2 * QUAD * PACK], BF16, name="rounded_rest0", align_bytes=ALIGN)[:],
            (1, QUAD): chain_a.tile([P, QUAD * PACK], BF16, name="rounded_quad1", offset=0, align_bytes=ALIGN)[:],
            (1, 2 * QUAD): keep.tile([P, QUAD * PACK], BF16, name="rounded_quad2", align_bytes=ALIGN)[:],
        }
        x_codes = chain_c.tile([P, PASSES * S], U32, name="x_codes", offset=0, align_bytes=ALIGN)
        x_plane = keep.tile([P, PASSES * S], U8, name="x_plane", align_bytes=ALIGN)

        def column(a, s):
            return (PASSES * (s // QUAD) + 1 - a) * QUAD + s % QUAD

        def rounded_at(a, s0, s1):
            base = max(start for aa, start in rounded if aa == a and start <= s0)
            return rounded[(a, base)][:, (s0 - base) * PACK : (s1 - base) * PACK]

        def gathered_at(a, s0, s1):
            base = max(start for aa, start in gathered if aa == a and start <= s0)
            return gathered[(a, base)][:, :, s0 - base : s1 - base]

        y = [keep.tile([P, S], F32, name="y%d" % h) for h in range(HALVES)]
        first = [keep.tile([P, T], F32, name="first%d" % h) for h in range(HALVES)]
        total = [keep.tile([P, T], F32, name="total%d" % h) for h in range(HALVES)]
        bias = keep.tile([P, HALVES, BIAS_COLUMNS], F32, name="bias")

        seed = keep.tile([P, 1], F32, name="seed")
        warm = keep.tile([P, 1], F32, name="warm")
        nc.gpsimd.memset(seed[:], 0.0)
        nc.scalar.activation(warm[:], seed[:], SILU)
        make_identity(nc, identity[:])
        nc.vector.memset(w_plane[:].rearrange("p g n -> p (g n)").bitcast(I32), 0)

        x_rows = xT.rearrange("(a p j) t -> a j p t", a=PASSES, j=PACK)
        words = w_words.rearrange("e a p n r -> p (e a) (n r)")
        scale_rows = w_scales.rearrange("e a q n -> q (e a) n")
        for (a, j), tile in x_sb.items():
            nc.sync.dma_start(tile[:, 0:T], x_rows[a, j])
            if (a, j) == (0, 0):
                nc.sync.dma_start(offs_sb[:], offs)
                nc.sync.dma_start(gate_rows[0][:], gate[0:P, 0:QUAD])
            if (a, j) == (1, 2):
                nc.sync.dma_start(gate_blocks[:], gate.rearrange("r (m s) -> (r m) s", s=C)[0:P, :])
            if (a, j) == (1, 1):
                nc.sync.dma_start(gate_rows[QUAD][:], gate[0:P, QUAD:POOL_END])
        nc.gpsimd.dma_start(bias[:, :, 0:E], b.rearrange("(h p) e -> p h e", p=P))
        for r in range(PACK):
            nc.sync.dma_start(w_plane[r:P:QUADRANT].bitcast(I32), scale_rows[r : 4 * PACK : PACK].bitcast(I32))
        for e0, e1 in ((8, E), (0, 8)):
            g = slice(e0 * PASSES, e1 * PASSES)
            nc.sync.dma_start(w_codes[:, g, :].bitcast(I32), words[:, g, :].bitcast(I32))
        nc.sync.dma_start(pos1_sb[:], pos1)
        nc.sync.dma_start(pos2_sb[:], pos2)

        def window(a, j, s0, s1):
            return x_sb[(a, j)][:].indirect(offs_sb[:, s0 // LANES : s1 // LANES])

        def gather_on_vector(a, j, s0, s1):
            nc.vector.tensor_copy(gathered_at(a, s0, s1)[:, j, :], window(a, j, s0, s1))

        def gather_on_scalar(a, j, s0, s1):
            nc.scalar.activation(gathered_at(a, s0, s1)[:, j, :], window(a, j, s0, s1), COPY)

        def weigh_on_gpsimd(a, s0, s1):
            into = rounded_at(a, s0, s1).rearrange("p (c j) -> p c j", j=PACK)
            weight = gate_rows[s0][:].rearrange("p (c o) -> p c o", o=1)
            source = gathered_at(a, s0, s1).rearrange("p j c -> p c j")
            nc.gpsimd.tensor_tensor(into, source, weight.to_broadcast([P, s1 - s0, PACK]), MULT)

        def weigh_on_vector(a, s0, s1):
            into = rounded_at(a, s0, s1).rearrange("p (c m j) -> p c j m", m=PAIR, j=PACK)
            source = gathered_at(a, s0, s1).rearrange("p j (c m) -> p c j m", m=PAIR)
            at = s0 % QUAD
            weight = gate_banks[s0 // QUAD][:, at : at + s1 - s0].rearrange("p (c o m) -> p c o m", o=1, m=PAIR)
            nc.vector.tensor_tensor(into, source, weight.to_broadcast([P, (s1 - s0) // PAIR, PACK, PAIR]), MULT)

        def quantise(a, s0, width):
            cols = slice(column(a, s0), column(a, s0) + width)
            nc.vector.quantize_mx(
                out=x_codes[:, cols].bitcast(FP8X4), scales=x_plane[:, cols], in_=rounded_at(a, s0, s0 + width)
            )

        def bank(i, sums):
            tile = psum.tile([P, len(sums), C], F32, name="bank%d" % i)
            accs = {unit: tile[:, n, :] for n, unit in enumerate(sums)}
            for a in range(PASSES):
                for n, (e, h) in enumerate(sums):
                    cols = slice(h * P, (h + 1) * P)
                    slots = slice(column(a, e * C), column(a, e * C) + C)
                    nc.tensor.matmul_mx(
                        out=accs[(e, h)],
                        lhsT=w_codes[:, e * PASSES + a, cols].bitcast(FP8X4),
                        lhsT_scale=w_plane[:, e * PASSES + a, cols],
                        rhs=x_codes[:, slots].bitcast(FP8X4),
                        rhs_scale=x_plane[:, slots],
                        start=(a == 0 and n == 0),
                        stop=(a == PASSES - 1 and n == len(sums) - 1),
                    )
            return accs

        def activate(accs, e, h):
            nc.scalar.activation(y[h][:, e * C : (e + 1) * C], accs[(e, h)], SILU, bias=bias[:, h, e : e + 1])

        def fetch(h, t0, t1):
            nc.scalar.activation(first[h][:, t0:t1], y[h][:].indirect(pos1_sb[:, t0 // LANES : t1 // LANES]), COPY)

        gather_on_vector(0, 0, QUAD, HEAD_END)
        for j in range(PACK):
            nc.vector.tensor_tensor(gathered_at(0, 0, QUAD)[:, j, :], window(0, j, 0, QUAD), gate_rows[0][:], MULT)
        for j, s0, s1 in ((0, HEAD_END, S), (1, QUAD, S), (2, QUAD, S), (3, QUAD, POOL_END), (3, POOL_END, S)):
            gather_on_scalar(0, j, s0, s1)

        turned = psum.tile([P, P], F32, name="bank5")
        nc.tensor.transpose(turned[:], gate_blocks[:], identity[:])
        nc.vector.tensor_copy(gate_by_slot[:], turned[:, 0:E])
        gate_banks = {q: psum.tile([P, QUAD], F32, name="bank%d" % (5 + q)) for q in range(1, S // QUAD)}
        for e in range(QUAD // C + 1, E):
            at = e * C % QUAD
            spread = gate_by_slot[:, e : e + 1].to_broadcast([P, P])
            nc.tensor.transpose(gate_banks[e * C // QUAD][:, at : at + C], spread, identity[:])

        for j in range(PACK):
            gather_on_vector(1, j, 0, QUAD)
        for j in range(PACK):
            gather_on_scalar(1, j, 2 * QUAD, S)
        nc.gpsimd.tensor_scalar(
            rounded_at(0, 0, QUAD).rearrange("p (c j) -> p c j", j=PACK),
            gathered_at(0, 0, QUAD).rearrange("p j c -> p c j"),
            1.0,
            0.0,
            MULT,
            ADD,
        )
        weigh_on_gpsimd(0, QUAD, POOL_END)
        weigh_on_gpsimd(1, 0, QUAD)
        weigh_on_vector(0, POOL_END, 2 * QUAD)
        weigh_on_vector(0, 2 * QUAD, S)
        for j in range(PACK):
            gather_on_scalar(1, j, QUAD, 2 * QUAD)
        weigh_on_vector(1, 2 * QUAD, S)
        quantise(0, 2 * QUAD, QUAD)
        quantise(1, 2 * QUAD, QUAD)
        quantise(1, 0, 2 * QUAD)
        quantise(0, QUAD, QUAD)
        weigh_on_gpsimd(1, 4 * C, 5 * C)
        weigh_on_vector(1, 5 * C, 7 * C)
        weigh_on_vector(1, 7 * C, 8 * C)
        quantise(1, 4 * C, 2 * C)
        quantise(1, 6 * C, C)
        quantise(1, 7 * C, C)

        for i, sums in enumerate([(e, h) for e in range(e0, e0 + 4)] for e0 in (8, 0) for h in range(HALVES)):
            accs = bank(i, sums)
            for e, h in sums:
                activate(accs, e, h)
        accs = bank(4, [(4, 0), (5, 0)])
        accs.update(bank(5, [(6, 0)]))
        accs.update(bank(0, [(7, 0)]))
        accs.update(bank(1, [(e, 1) for e in range(4, 8)]))
        for e in range(4, 8):
            activate(accs, e, 0)
        activate(accs, 4, 1)
        for t0, t1 in OWN_FETCHES:
            nc.vector.tensor_copy(first[0][:, t0:t1], y[0][:].indirect(pos1_sb[:, t0 // LANES : t1 // LANES]))
        fetch(*FETCHES[0])
        for e in range(5, 8):
            activate(accs, e, 1)
        for h, t0, t1 in FETCHES[1:]:
            fetch(h, t0, t1)
        for h, t0, t1 in SUMS:
            nc.vector.tensor_tensor(
                total[h][:, t0:t1], y[h][:].indirect(pos2_sb[:, t0 // LANES : t1 // LANES]), first[h][:, t0:t1], ADD
            )
        for h, t0, t1 in STORES:
            nc.sync.dma_start(out[h * P : (h + 1) * P, t0:t1], total[h][:, t0:t1])
